import numpy as np, ml_dtypes
CORES = [16,18,20,22]
N = 4
BF = ml_dtypes.bfloat16
def gentries(a):
    return np.ascontiguousarray(a.reshape(8, 16, -1).transpose(0, 2, 1)).reshape(8, -1)
def gtable(e):
    e = np.asarray(e); return np.ascontiguousarray(e.reshape(8, -1, 16).transpose(0, 2, 1)).reshape(128, -1).astype(np.int32)
GW, GH, M, RO, HP = 64, 64, 1024, 3, 2
W, D = GW * GH, 255
def parts(rng):
    s = np.exp2(rng.permutation(np.arange(16) % 3 - 1)).astype(np.float32).reshape(1, 1, 16, 1)
    x = s * np.exp2(2 * rng.random((N, 8, 16, W), dtype=np.float32) - 1)
    eps = s * (0.17 + 0.34 * rng.random((N, 8, 16, 1)))
    fl = np.where(rng.random((N, 8, 1, W)) < 0.6, rng.integers(-48, 49, (N, 8, 4, W)), rng.integers(-D, D + 1, (N, 8, 4, W)))
    cor = rng.integers(0, W, (N, 8, 4, W))
    ms = np.ascontiguousarray(np.argsort(rng.random((N, 8, W)), axis=-1)[..., :M])
    return x, eps, fl, cor, ms
def pack(x, eps, fl, cor, ms):
    return {"x": np.clip(x, 2.0 ** -20, 4.0).astype(BF).reshape(N, 128, W), "eps": np.ascontiguousarray(eps).astype(np.float32).reshape(N, 128, 1),
            "fl": np.ascontiguousarray(fl.transpose(0, 2, 1, 3)).astype(np.int32).reshape(N, 32, W),
            "cor": np.stack([gtable(a.reshape(8, -1)) for a in cor]), "ms": np.stack([gtable(a) for a in ms])}
def setup_inputs(rng):
    return pack(*parts(rng))
def setup_inputs_calm(rng):
    x, eps, fl, cor, ms = parts(rng)
    v = (np.arange(N).reshape(N, 1, 1, 1) + np.arange(8).reshape(1, 8, 1, 1) + np.arange(4).reshape(1, 1, 4, 1)) % 4
    fl = v * np.where(rng.random((N, 8, 4, W)) < 0.5, 1, -1) * (rng.random((N, 8, 1, W)) < 0.8)
    return pack(x, eps, fl, cor, ms)
def setup_inputs_corners(rng):
    x, eps, fl, cor, ms = parts(rng); sh = int(rng.integers(0, 6)); clear = int(rng.integers(0, 8)); own = np.arange(W)
    for q in range(N):
        o = rng.permutation(8); u = [int(v) for v in rng.permutation(8)]
        j = u.index(2 + q % 3); u[j], u[clear] = u[clear], u[j]
        for g in range(8):
            k = 0 if g == clear else (q + g + sh) % 6
            if k in (1, 4):
                m = ms[q, g]; ms[q, g] = rng.permutation(np.concatenate([np.array([0, W - 1]), m[(m != 0) & (m != W - 1)]])[:M])
            m = ms[q, g]; there = np.ones(W, bool); there[m] = False; kno = np.flatnonzero(there)
            if k == 0: cor[q, g] = rng.choice(kno, (4, W))
            if k == 1:
                c = rng.choice(kno, (4, W)); c[rng.integers(0, 4, W), own] = rng.choice(m, W); cor[q, g] = c
            if k == 2: cor[q, g] = own
            if k == 3: cor[q, g] = rng.choice(np.array([0, W - 1]), (4, W))
            if k == 4: cor[q, g] = rng.choice(m, (4, W))
            if o[g] == 0: fl[q, g] = 0
            if o[g] == 1: fl[q, g] = rng.choice(np.array([-D, D]), (4, W))
            if o[g] == 2: fl[q, g] = rng.choice(np.array([-D, 0, D]), (4, W))
            n = (0, 8, 9, 15, 16, -1, -1, -1)[u[g]]
            if n >= 0: eps[q, g, :, 0] = rng.permutation(np.where(np.arange(16) < n, 4.0, 0.0))
    return pack(x, eps, fl, cor, ms)
def setup_inputs_ends(rng):
    x, eps, fl, cor, ms = parts(rng); h = M // 2; tips = np.array([0, GW - 1, W - GW, W - 1])
    x = np.where(rng.random(x.shape) < 0.5, np.float32(4), np.float32(2.0 ** -20))
    m = rng.random((N, 8, 1, W)) < 0.8; m[..., tips] = True
    fl = np.where(m, np.where(rng.random(fl.shape) < 0.5, D, -D), fl)
    cor = np.where(rng.random((N, 8, 1, W)) < 0.75, np.where(rng.random(cor.shape) < 0.5, 0, W - 1), cor)
    top = np.where(np.arange(16) % 2 == 0, 4.0, 4.0 - 2.0 ** -20)
    for q in range(N):
        o = rng.permutation(8)
        for g in range(8):
            lo, hi = (1, 1, 1, 1, 0, 1, 0, 0)[g], (1, 1, 1, 1, 0, 0, 1, 0)[g]
            s = np.concatenate([np.arange(lo, lo + h), np.arange(W - hi - h, W - hi)])
            ms[q, g] = np.concatenate([s[:1], rng.permutation(s[1:-1]), s[-1:]])
            if g >= 4 and q % 2 == 1: cor[q, g][:, tips[[0, 3]]] = rng.integers(h + 1, W - 1 - h, (4, 2))
            n = (16, 9, 8, 9, 8, 7, 12, 0)[int(o[g])]
            eps[q, g, :, 0] = rng.permutation(np.where(np.arange(16) < n, top, 0.0))
    return pack(x, eps, fl, cor, ms)
def setup_inputs_spread(rng):
    x, eps, fl, cor, ms = parts(rng)
    x = np.exp2(2 * rng.random((N, 8, 16, W), dtype=np.float32) - 1) * np.exp2(rng.integers(-1, 2, (N, 8, 1, W))).astype(np.float32)
    eps = np.exp2(4 * rng.random((N, 8, 16, 1)) - 2.5)
    fl = rng.integers(-D, D + 1, (N, 8, 4, W))
    v = np.minimum(np.exp2(rng.random((N, 4, 4, W)) * np.log2(D)).astype(np.int64), D)
    fl[:, 1::2] = v * np.where(rng.random((N, 4, 4, W)) < 0.5, 1, -1)
    cor[:, ::2] = np.minimum((W * rng.random((N, 4, 4, W)) ** 3).astype(np.int64), W - 1)
    return pack(x, eps, fl, cor, ms)
def setup_inputs_ties(rng):
    x, eps, fl, cor, ms = parts(rng)
    x = rng.integers(1, 9, (N, 8, 16, W)).astype(np.float32) * np.float32(0.5)
    eps = rng.choice(np.array([0.0, 1.0 - 2.0 ** -24, 1.0, 1.5, 2.0]), (N, 8, 16, 1))
    fl = np.where(rng.random((N, 8, 1, W)) < 0.8, np.maximum(fl // 4 * 4, 3 - D), fl)
    own = np.arange(W); pool = np.flatnonzero((own % GW % 2 == 0) & (own // GW % 2 == 0))
    for i, g in enumerate([int(v) for v in rng.permutation(8)[:3]]):
        pix = rng.permutation(pool)[:M]; kno = np.setdiff1d(own, pix); fx, fy = [int(v) for v in rng.integers(1, 4, 2)]
        x[:, g] = (128 + rng.integers(0, 128, (16, W))) * np.exp2(np.where(rng.random((16, W)) < 0.5, rng.integers(-8, -5, (16, W)), rng.integers(-27, -24, (16, W))))
        eps[:, g] = 0; t = rng.choice(kno, (4, W)); v = fl[:, g]
        v[:] = np.array([fx, fy, fx, fy + 4]).reshape(4, 1)
        if i == 0:
            n = M // 3; a, b, c = pix[:n], pix[n:2 * n], pix[2 * n:3 * n]
            t[:, a + GW] = t[:, a]; t[:, b + GW] = t[:, a]; t[:, c + GW] = t[:, a]
            t[:, b] = a; t[:, c] = b
        else:
            v[:, :, pix + (1, GW)[i - 1]] = np.array([fx + 4, fy, fx + 4, fy]).reshape(4, 1)
        cor[:, g] = t
        for q in range(N): ms[q, g] = rng.permutation(pix)
    return pack(x, eps, fl, cor, ms)
def check_ranges(d):
    bad = []
    for k, lo, hi in (("x", 2.0 ** -20, 4), ("eps", 0, 4), ("fl", -D, D), ("cor", 0, W - 1), ("ms", 0, W - 1)):
        v = np.asarray(d[k]).astype(np.float64)
        if not np.all((v >= lo) & (v <= hi)): bad.append("range of " + k)
    s = np.sort(np.stack([gentries(np.asarray(a)) for a in d["ms"]]), axis=-1)
    if np.any(s[..., 1:] == s[..., :-1]): bad.append("a number twice in a group of ms")
    return bad
def chase(a, way, xs, kn, fw, taps, mis, home):
    sg = 1 - 2 * way; lim = np.array([4 * GW - 1, 4 * GH - 1]).reshape(1, 2, 1)
    z = np.zeros((8, 16, M), np.float32); got = np.zeros((8, M), np.int64); end = np.zeros((8, 2, M), np.int64)
    pos = home[a]; step = np.take_along_axis(fw[a][:, 2 * way:2 * way + 2], mis[a][:, None, :], 2)
    for h in range(1, HP + 1):
        q = (a + sg * h) % N; gi = (np.arange(8) + sg * (h - 1)) % 8
        pos = np.minimum(np.maximum(pos + step, 0), lim)
        cell = (pos[:, 1] >> 2) * GW + (pos[:, 0] >> 2); part = (pos & 3).astype(np.float32) * np.float32(0.25)
        t = np.take_along_axis(taps[q][gi], cell[:, None, :], 2).reshape(8, 4 * M)
        ok = np.all(np.take_along_axis(kn[q][gi], t, 1).reshape(8, 4, M), axis=1)
        v = np.take_along_axis(xs[q][gi], t[:, None, :], 2).reshape(8, 16, 4, M)
        u0 = part[:, 0][:, None, :]; u1 = part[:, 1][:, None, :]
        up = v[:, :, 0] + u0 * (v[:, :, 1] - v[:, :, 0]); dn = v[:, :, 2] + u0 * (v[:, :, 3] - v[:, :, 2])
        w = up + u1 * (dn - up)
        new = ok & (got == 0)
        z = np.where(new[:, None, :], w, z); end = np.where(new[:, None, :], pos, end); got = np.where(new, h, got)
        step = np.take_along_axis(fw[q][:, 2 * way:2 * way + 2][gi], cell[:, None, :], 2)
    return z, got, end
def reference(x, eps, fl, cor, ms):
    xs = x.astype(np.float32).reshape(N, 8, 16, W); ep = eps.astype(np.float32).reshape(N, 8, 16, 1)
    fw = np.ascontiguousarray(fl.astype(np.int64).reshape(N, 4, 8, W).transpose(0, 2, 1, 3))
    taps = np.stack([gentries(a) for a in cor]).astype(np.int64).reshape(N, 8, 4, W); mis = np.stack([gentries(a) for a in ms]).astype(np.int64)
    kn = np.ones((N, 8, W), bool); np.put_along_axis(kn, mis, False, 2)
    mx = mis % GW; my = mis // GW; home = np.stack([4 * mx, 4 * my], axis=2)
    done = np.zeros((N, 8, M), bool); val = np.zeros((N, 8, 16, M), np.float32); ex = np.zeros((N, 8, 16, M), np.float64)
    for rnd in range(RO):
        ends = [(chase(a, 0, xs, kn, fw, taps, mis, home), chase(a, 1, xs, kn, fw, taps, mis, home)) for a in range(N)]
        nb = ((my + (0, 1, 0)[rnd]) % GH) * GW + (mx + (1, 0, GW - 1)[rnd]) % GW
        for a in range(N):
            (zf, gf, pf), (zb, gb, pb) = ends[a]
            both = (gf > 0) & (gb > 0); open_ = ~done[a]; dif = zf - zb; gap = np.abs(dif)
            agree = np.add.reduce((gap <= ep[a]).astype(np.int64), axis=1)
            won = both & open_ & (agree >= 9)
            ex[a] = np.where(open_[:, None, :], np.where(both[:, None, :], np.exp(-gap.astype(np.float64)), 0.0), ex[a])
            val[a] = np.where(won[:, None, :], zb + np.float32(0.5) * dif, val[a])
            cur = np.take_along_axis(fw[a], mis[a][:, None, :], 2); near = np.take_along_axis(fw[a], nb[a][:, None, :], 2)
            own = np.concatenate([(pf - home[a]) >> np.maximum(gf - 1, 0)[:, None, :], (pb - home[a]) >> np.maximum(gb - 1, 0)[:, None, :]], axis=1)
            new = np.where(won[:, None, :], own, np.where(open_[:, None, :], near, cur))
            done[a] = done[a] | won
            np.put_along_axis(fw[a], np.broadcast_to(mis[a][:, None, :], (8, 4, M)), new, 2)
            np.put_along_axis(kn[a], mis[a], done[a], 1)
            np.put_along_axis(xs[a], np.broadcast_to(mis[a][:, None, :], (8, 16, M)), val[a], 2)
    last = np.stack([np.take_along_axis(fw[a], mis[a][:, None, :], 2) for a in range(N)])
    yf = np.concatenate([last.transpose(0, 2, 1, 3).reshape(N, 32, M), done.astype(np.int64)], axis=1)
    return {"y": val.reshape(N, 128, M), "ye": ex.reshape(N, 128, M).astype(np.float32), "yf": yf.astype(np.float32)}

def check_inputs(d):
    bad = list(check_ranges(d))
    if not bad:
        for name, y in reference(**d).items():
            for q in range(N):
                v = np.abs(np.asarray(y[q], np.float64)); s = np.sqrt(np.mean(v * v))
                if v.max() > 8 * s or s < 2.0 ** -3: bad.append('%s of rank %d is uneven or too small' % (name, q))
    return bad

@@ -1,0 +1,778 @@
+from concourse.bass import DstId, RemoteDMATransfer
+from concourse.mybir import AluOpType as ALU, ActivationFunctionType as AF
+
+F32, BF, I32, U16 = "float32", "bfloat16", "int32", "uint16"
+SCRATCH = {
+    "WF": ("sbuf", [128, 10240], F32), "WB": ("sbuf", [128, 10240], F32),
+    "XF": ("sbuf", [128, 8224], BF), "XB": ("sbuf", [128, 8224], BF),
+    "PTf": ("sbuf", [128, 4096], BF), "PTb": ("sbuf", [128, 4096], BF), "PT2": ("sbuf", [128, 4096], BF),
+    "AR": ("sbuf", [128, 8192], BF), "INV": ("sbuf", [128, 4128], BF),
+    "IB": ("sbuf", [128, 1024], I32), "IS": ("sbuf", [128, 640], I32),
+    "CU": ("sbuf", [128, 1024], U16), "OF": ("sbuf", [128, 1024], U16),
+    "WK": ("sbuf", [128, 3584], F32), "GAP": ("sbuf", [128, 3072], F32), "VAL": ("sbuf", [128, 3080], F32),
+    "LL": ("sbuf", [128, 2048], BF), "BA": ("sbuf", [128, 1440], BF), "BC": ("sbuf", [128, 144], BF),
+    "RM": ("sbuf", [128, 288], BF), "PM": ("sbuf", [128, 768], BF), "IDN": ("sbuf", [128, 64], F32),
+    "Q": ("sbuf", [128, 896], F32), "COL": ("sbuf", [128, 52], F32), "EPS": ("sbuf", [128, 4], F32),
+    "ST": ("sbuf", [128, 3520], F32), "SB": ("sbuf", [128, 512], BF),
+    "MSG": ("sbuf", [128, 640], BF), "MF": ("sbuf", [128, 384], BF), "MB": ("sbuf", [128, 384], BF),
+    "xd": ("dram", [128, 4096], BF), "xe": ("dram", [160, 4096], BF),
+    "xf": ("dram", [128, 4096], F32), "xg": ("dram", [160, 4096], F32),
+    "vs": ("dram", [4, 128, 1024], F32),
+}
+for _b in range(8):
+    SCRATCH["PS%d" % _b] = ("psum", [128, 512], F32)
+ARRIVALS = (["aXh", "aXF0", "aXF1", "aXB0", "aXB1", "aWh", "aWF0", "aWF1", "aWB0", "aWB1"]
+            + ["aPT%s%d" % (t, h) for t in "fb" for h in range(4)] + ["aPT20", "aPT21"]
+            + ["aM%s%d" % (t, r) for t in "FB" for r in range(2)] + ["aV%s%d" % (t, r) for t in "fbpn" for r in range(2)])
+SEMAPHORES = ["cP", "cV", "cA", "cG", "h00", "h10", "h20", "h01", "h11", "h21"] + ARRIVALS + ["d%d" % i for i in range(60)]
+
+TINY = 2.0 ** -48
+ROOT = 2.0 ** 52
+BIG = 16384.0
+
+
+def S(name, lo, hi, step=1, p0=0, p1=128, ps=1):
+    return (name, lo, hi, step, p0, p1, ps)
+
+
+def D3(name, t, p0=0, p1=128, ps=1):
+    return (name, t, t + 1, 0, p0, p1, ps)
+
+
+def width(s):
+    return (s[2] - s[1] + s[3] - 1) // s[3]
+
+
+def sub(s, a, w):
+    return (s[0], s[1] + a, s[1] + a + w) + s[3:]
+
+
+def helper_of(T, topo, rank):
+    free = [c for c in topo.cores_of(T.cores[0]) if T.rank_of(c) is None]
+    out = []
+    for c in T.cores:
+        far = [h for h in free if h not in out and topo.die(h) != topo.die(c)] or [h for h in free if h not in out]
+        out.append(far[0])
+    return out[rank]
+
+
+def pair_masks(topo, src, a, b):
+    ea, eb = topo.engines(src, a), topo.engines(src, b)
+    return sum(1 << e for e in ea[0::2]), sum(1 << e for e in eb[1::2]), len(ea[0::2]), len(eb[1::2])
+
+
+def dst_id(topo, c):
+    rid, pid, _ = topo.addr(c)
+    return DstId(rid=rid, pnc=pid)
+
+
+def helper_program(g, core, T, topo, rank):
+    n = len(T.cores)
+    lo, hi, far = T.cores[(rank - 1) % n], T.cores[(rank + 1) % n], T.cores[(rank + 2) % n]
+    full = len(topo.engines(T.cores[rank], core))
+    ma, mb, na, nb = pair_masks(topo, core, lo, hi)
+    mc, md, nc, nd = pair_masks(topo, core, far, far)
+    for k, (t, x, a, b) in enumerate((("X", T.xe, 16, 4128), ("W", T.xg, 1024, 6144))):
+        one = lambda c, m, w, v, row, at: RemoteDMATransfer(dst_ids=[dst_id(topo, c)], dma_engine_mask=m, remote_sem=T.sem["a%s%s%d" % (t, w, v)],
+                                                            src=x[row:row + 128, :], dst=T[t + w][:, at:at + 4096])
+        g.sync.wait_ge(T.sem["a%sh" % t], full)
+        g.sync.dma_start(x[0:16, :], x[128:144, :]).then_inc(T.sem["h0%d" % k], 16)
+        g.sync.dma_start(x[144:160, :], x[16:32, :]).then_inc(T.sem["h0%d" % k], 16)
+        g.wait_ge(T.sem["a%sh" % t], full)
+        g.remote_dma_fused([one(lo, ma, "F", 0, 16, a), one(hi, mb, "B", 0, 16, a)], local_sem=T.sem["h1%d" % k])
+        g.wait_ge(T.sem["h0%d" % k], 32)
+        g.remote_dma_fused([one(far, mc, "F", 1, 32, b), one(far, md, "B", 1, 0, b)], local_sem=T.sem["h2%d" % k])
+    for k in range(2):
+        g.wait_ge(T.sem["h1%d" % k], na + nb)
+        g.wait_ge(T.sem["h2%d" % k], nc + nd)
+
+
+def build(g, core, T, topo, rank):
+    n = len(T.cores)
+    lo, hi, far = T.cores[(rank - 1) % n], T.cores[(rank + 1) % n], T.cores[(rank + 2) % n]
+    ops = []
+    acc = {}
+    nsem = [0]
+    q = {"P": g.tensor, "V": g.vector, "A": g.scalar, "S": g.sync, "G": g}
+
+    def ap(s):
+        if s[3] == 0:
+            return T[s[0]][s[1], s[4]:s[5]:s[6], :] if (s[4], s[5], s[6]) != (0, 128, 1) else T[s[0]][s[1]]
+        return T[s[0]][s[4]:s[5]:s[6], s[1]:s[2]:s[3]]
+
+    def ind(win, off):
+        return ap(win).indirect(ap(off))
+
+    def add(eng, dur, emit, reads, writes, kind="c", sem=None, cnt=0, after=(), hold=None):
+        i = len(ops)
+        deps = {}
+        for s, mode in [(s, "r") for s in reads] + [(s, "w") for s in writes]:
+            for (l, h, m, j, k) in acc.get(s[0], []):
+                if l < s[2] and s[1] < h and (m == "w" or mode == "w") and j != i and not (k == s[3] > 1 and (l - s[1]) % k):
+                    deps[j] = True
+        for s in list(reads) + list(writes):
+            if s[0].startswith("PS"):
+                j = acc.get("lock" + s[0])
+                if j is not None and j != i:
+                    deps[j] = deps.get(j, False)
+                acc["lock" + s[0]] = i
+        for s in writes:
+            full = s[3] <= 1 and (s[4], s[5], s[6]) == (0, 128, 1)
+            if full:
+                acc[s[0]] = [e for e in acc.get(s[0], []) if not (s[1] <= e[0] and e[1] <= s[2])]
+            acc.setdefault(s[0], []).append((s[1], s[2], "w", i, s[3]))
+        for s in reads:
+            acc.setdefault(s[0], []).append((s[1], s[2], "r", i, s[3]))
+        for j in after:
+            deps[j] = True
+        ops.append({"eng": eng, "dur": dur, "emit": emit, "deps": deps, "kind": kind, "sem": sem, "cnt": cnt,
+                    "hold": dur if hold is None else hold, "soft": []})
+        return i
+
+    def new_sem():
+        nsem[0] += 1
+        return "d%d" % (nsem[0] - 1)
+
+    def is2(s):
+        return SCRATCH[s[0]][2] in (BF, U16)
+
+    def cost(c, k):
+        return 0.06 + max(64, c * k) * 0.001
+
+    def cols(x):
+        return [x] if isinstance(x, tuple) else []
+
+    def val(x):
+        return ap(x) if isinstance(x, tuple) else x
+
+    def ts(out, in0, s1, op0, s2=None, op1=None, off=None):
+        def emit():
+            a = ind(in0, off) if off else ap(in0)
+            if op1 is None:
+                return g.vector.tensor_scalar(ap(out), a, val(s1), None, op0)
+            return g.vector.tensor_scalar(ap(out), a, val(s1), val(s2), op0, op1)
+        c = 1.55 if off else (0.5 if is2(out) and is2(in0) else 1)
+        return add("V", cost(c, width(out)), emit, [in0] + cols(s1) + cols(s2) + cols(off), [out])
+
+    def tt(out, in0, in1, op, off=None):
+        def emit():
+            return g.vector.tensor_tensor(ap(out), ind(in0, off) if off else ap(in0), ap(in1), op)
+        c = 2 if not (in0[0].startswith("PS") or in1[0].startswith("PS")) else 1
+        return add("V", cost(1.8 if off else c, width(out)), emit, [in0, in1] + cols(off), [out])
+
+    def cp(eng, out, in_, off=None, func=None, scale=1.0, bias=0.0, after=()):
+        def emit():
+            a = ind(in_, off) if off else ap(in_)
+            if eng == "V":
+                return g.vector.tensor_copy(ap(out), a)
+            if bias != 0.0:
+                return g.scalar.activation(ap(out), a, func or AF.Identity, bias=val(bias), scale=scale)
+            if scale != 1.0:
+                return g.scalar.activation(ap(out), a, func or AF.Copy, scale=scale)
+            return g.scalar.activation(ap(out), a, func or AF.Copy)
+        c = 1.55 if off else (0.5 if eng == "V" and is2(out) and is2(in_) else 1)
+        return add(eng, cost(c, width(out)), emit, [in_] + cols(off) + cols(bias), [out], after=after)
+
+    def axb(eng, out, in_, a, b):
+        return cp("A", out, in_, None, None, a, b) if eng == "A" else ts(out, in_, a, ALU.mult, b, ALU.add)
+
+    def mset(out, v):
+        return add("V", cost(0.5 if is2(out) else 1, width(out)), lambda: g.vector.memset(ap(out), v), [], [out])
+
+    def iota(out, pat, base, cm):
+        return add("G", 0.15 + width(out) * 0.002, lambda: g.iota(ap(out), pat, base, cm), [], [out])
+
+    def asel(out, pat, base, cm):
+        return add("G", 0.2 + width(out) * 0.002,
+                   lambda: g.affine_select(ap(out), ap(out), pat, ALU.is_equal, 0.0, base, cm), [out], [out])
+
+    def mm(items, each=0.04):
+        def emit():
+            r = None
+            for (o, l, x, a, b) in items:
+                r = g.tensor.matmul(ap(o), ap(l), ap(x), a, b)
+            return r
+        rd = sorted({s for it in items for s in it[1:3]})
+        wr = sorted({it[0] for it in items})
+        return add("P", 0.05 + each * len(items), emit, rd, wr)
+
+    def tr(items):
+        def emit():
+            r = None
+            for (o, x) in items:
+                r = g.tensor.transpose(ap(o), ap(x), T.IDN[0:64, 0:64])
+            return r
+        return add("P", 0.05 + sum(0.002 * width(it[0]) for it in items), emit,
+                   [it[1] for it in items] + [S("IDN", 0, 64)], [it[0] for it in items])
+
+    def dma(eng, items, kb, reads, writes, after=()):
+        sem = new_sem()
+
+        def emit():
+            for (o, x) in items:
+                q[eng].dma_start(o(), x()).then_inc(T.sem[sem], 16)
+        return add(eng, 2.0 + kb / 330.0, emit, reads, writes, "d", sem, 16 * len(items), after,
+                   hold=(1.0 if eng == "G" else 0.1) * len(items))
+
+    def sdma(eng, pairs, kb, after=()):
+        return dma(eng, [((lambda o=o: ap(o)), (lambda x=x: ap(x))) for (o, x) in pairs], kb,
+                   [x for (_, x) in pairs], [o for (o, _) in pairs], after)
+
+    def send(items, kb, after=()):
+        sem = new_sem()
+        if len(items) == 2:
+            ma, mb, na, nb = pair_masks(topo, core, items[0][0], items[1][0])
+            masks, cnt = [ma, mb], na + nb
+        else:
+            masks, cnt = [topo.mask(core, items[0][0])], len(topo.engines(core, items[0][0]))
+
+        def emit():
+            if len(items) == 1:
+                c, s, d, rs = items[0]
+                rid, pid, _ = topo.addr(c)
+                g.remote_dma(ap(d), ap(s), T.sem[rs], T.sem[sem], pid, rid, masks[0])
+            else:
+                g.remote_dma_fused([RemoteDMATransfer(dst_ids=[dst_id(topo, c)], dma_engine_mask=m, remote_sem=T.sem[rs],
+                                                      src=ap(s), dst=ap(d)) for (c, s, d, rs), m in zip(items, masks)],
+                                   local_sem=T.sem[sem])
+        return add("G", 2.0 + kb / 270.0, emit, [it[1] for it in items], [], "d", sem, cnt, after, hold=0.3)
+
+    half = len(topo.engines(core, lo)[0::2])
+    whole = len(topo.engines(core, far))
+
+    def arrive(sem, cnt, piece, like, lag=0.5):
+        i = add(None, lag, None, [], [piece], "a", sem, cnt)
+        ops[i]["soft"].append(like)
+        return i
+
+    PS = lambda b, l=0, h=512, step=1, p1=128: S("PS%d" % b, l, h, step, 0, p1)
+    X0, X1, TA, U0, U1, VF0, VF1, VB = 0, 1, 2, 3, 4, 5, 6, 7
+    col = lambda j: S("COL", j, j + 1)
+    H, P1, B2, T1A = 0, 128, 384, 896
+    NB = [None, 1408, 1664]
+    FL, FLO, AA, TM, MM, GG, CNT, NOTL = 1920, 2176, 2432, 2688, 2944, 3072, 3200, 3328
+    JJ, THR, WON, MISS, BASE, JC, GI = 640, 704, 768, 832, 3392, 3456, CNT
+    st = lambda a, w: S("ST", a, a + w)
+    IA, IC = S("IB", 0, 256), S("IB", 256, 512)
+    OFS, OFT = S("CU", 0, 512), S("CU", 512, 1024)
+    OC1, OC2, OSP, ONB, OMS, OJS, OVP, OVN, OGI, ONS = [S("OF", a, b) for a, b in (
+        (0, 128), (128, 256), (256, 384), (384, 576), (576, 640), (640, 704), (704, 768), (768, 832), (832, 896), (896, 1024))]
+    UV, QB = S("SB", 0, 256), S("SB", 256, 512)
+    MSI = S("IS", 0, 64)
+    FB = S("BA", 0, 1024)
+
+    dma("S", [(lambda: ap(MSI), lambda: T.ms[:])], 32, [], [MSI])
+    lc = dma("S", [(lambda: T.IB[:], lambda: T.fl[:])], 512, [], [S("IB", 0, 1024)])
+    cp("V", FB, S("IB", 0, 1024))
+    dma("A", [(lambda: T.IB[:], lambda: T.cor[:])], 512, [], [S("IB", 0, 1024)])
+    ops[lc]["soft"].append(lc - 1)
+    ops[dma("S", [(lambda: T.xd[:], lambda: T.x[:])], 1024, [], [S("xd", 0, 4096)])]["soft"].append(lc)
+    dma("S", [(lambda: T.EPS[:, 0:1], lambda: T.eps[:])], 1, [], [S("EPS", 0, 1)])
+    sx = send([(helper_of(T, topo, rank), S("xd", 0, 4096), S("xe", 0, 4096, 1, 16, 144), "aXh")], 1024)
+    arrive("aXF0", half, S("XF", 16, 4112), sx, 9)
+    arrive("aXB0", half, S("XB", 16, 4112), sx, 9)
+    arrive("aXF1", half, S("XF", 4128, 8224), sx, 15)
+    arrive("aXB1", half, S("XB", 4128, 8224), sx, 15)
+
+    pc = S("IS", 64, 65)
+    iota(pc, [[0, 1]], 0, 1)
+    iota(S("IS", 384, 640), [[1, 16], [0, 16]], 0, 0)
+    iota(S("IS", 128, 144), [[1, 16]], 0, 0)
+    iota(S("IS", 80, 97), [[16, 17]], -64, 0)
+    ts(S("IS", 66, 67), pc, 8, ALU.bitwise_and)
+    ts(col(0), S("IS", 66, 67), 0, ALU.is_equal)
+    ts(col(1), S("IS", 66, 67), 8, ALU.is_equal)
+    ts(S("COL", 32, 49), S("IS", 80, 97), col(0), ALU.mult)
+    step = lambda v: col(32 + (v + 64) // 16)
+    ts(S("INV", 256, 272), S("IS", 128, 144), col(1), ALU.mult)
+    for j in range(4):
+        cp("V", S("INV", 256 + (16 << j), 256 + (32 << j)), S("INV", 256, 256 + (16 << j)))
+    ts(PS(0, 0, 256), S("IS", 384, 640), col(0), ALU.mult)
+    tt(S("INV", 0, 256), PS(0, 0, 256), S("INV", 256, 512), ALU.add)
+    LC = S("AR", 7168, 8192)
+    for j in range(1, 4):
+        ts(S("INV", 256 * j, 256 * j + 256), S("INV", 0, 256), step(16 * j), ALU.add)
+    cp("A", S("INV", 3072, 4096), S("INV", 0, 1024), None, None, 1.0, step(192))
+    ts(S("INV", 1024, 2048), S("INV", 0, 1024), step(64), ALU.add)
+    ts(S("INV", 2048, 3072), S("INV", 0, 1024), step(128), ALU.add)
+    ts(LC, S("INV", 0, 1024), step(-64), ALU.add)
+    cp("V", OMS, MSI)
+    add("V", cost(3.5, 1024), lambda: g.vector.tensor_copy(ind(S("INV", 0, 4096), OMS), ap(LC)), [LC, OMS], [S("INV", 0, 4096)])
+    for i in range(2):
+        cp("V", S("CU", 512 * i, 512 * i + 512), S("IB", 512 * i, 512 * i + 512))
+    first = [cp("VA"[k % 2], S("AR", 1024 * k, 1024 * k + 1024), S("INV", 0, 4096), S("CU", 64 * k, 64 * k + 64)) for k in range(4)]
+    rowq = (5, 6, 13, 14)
+    rest = [dma("S", [(lambda: T.AR[4:128:8, 0:4096], lambda: T.INV[4:128:8, 0:4096])], 128, [S("INV", 0, 4096)], [], first),
+            dma("S", [((lambda k=k: T.AR[rowq[k]:128:16, 0:4096]), (lambda k=k: T.BA[32 * k:32 * k + 32, 0:1024])) for k in range(4)],
+                256, [FB], [], first)]
+    aPT, rows, last = [], [], {"V": first[2], "A": first[3]}
+    for k in range(2):
+        ops[first[k + 2]]["soft"].append(first[k])
+    for k in range(4):
+        for i in range(1, 4):
+            c = 4096 + 1024 * ((3 * k + i - 1) % 4)
+            e = "AVAAVAVAVAVA"[3 * k + i - 1]
+            j = cp(e, S("AR", c, c + 1024), S("INV", 0, 4096), S("CU", 256 * i + 64 * k, 256 * i + 64 * k + 64))
+            ops[j]["soft"].append(last[e])
+            last[e] = j
+            rows.append(dma("S", [((lambda i=i, k=k: T.AR[i:128:8, 1024 * k:1024 * k + 1024]), (lambda i=i, c=c: T.AR[i:128:8, c:c + 1024]))],
+                            32, [S("AR", c, c + 1024)], [], [first[k]]))
+        land = lambda t: S(t, 1024 * k, 1024 * k + 1024)
+        s1 = send([(lo, land("AR"), land("PTf"), "aPTf%d" % k), (hi, land("AR"), land("PTb"), "aPTb%d" % k)], 512, rest + rows[-3:])
+        aPT += [arrive("aPTf%d" % k, half, land("PTf"), s1), arrive("aPTb%d" % k, half, land("PTb"), s1)]
+        if k % 2:
+            land = lambda t: S(t, 1024 * k - 1024, 1024 * k + 1024)
+            s2 = send([(far, land("AR"), land("PT2"), "aPT2%d" % (k // 2))], 700, rest + rows[-6:])
+            aPT.append(arrive("aPT2%d" % (k // 2), whole, land("PT2"), s2, 1.0))
+
+    mset(S("IDN", 0, 64), 1.0)
+    asel(S("IDN", 0, 64), [[-1, 64]], 0, 1)
+    ei = S("IS", 128, 296)
+    iota(ei, [[-16, 3], [-1, 7], [-16, 8]], 144, 1)
+    ts(ei, ei, 127, ALU.bitwise_and)
+    E0, E8, RT, RS = S("BA", 1024, 1192), S("BA", 1192, 1360), S("RM", 0, 168), S("RM", 168, 208)
+    RC, RO = [S("RM", 208, 232), S("RM", 232, 256)], S("RM", 256, 288)
+    ts(E0, ei, 0, ALU.is_equal)
+    ts(E8, ei, 8, ALU.is_equal)
+    ts(RT, E0, 16.0, ALU.mult)
+    tt(RT, RT, E8, ALU.add)
+    ts(RS, sub(E0, 56, 40), 32.0, ALU.mult)
+    tt(RS, RS, sub(E8, 56, 40), ALU.add)
+    for w, e in ((0, E0), (1, E8)):
+        cp("A", sub(RC[w], 0, 8), sub(RS, 32, 8))
+        cp("A", sub(RC[w], 8, 16), sub(e, 96, 16))
+        cp("A", sub(RO, 16 * w, 16), sub(e, 96, 16))
+    pi = S("IS", 256, 640)
+    iota(pi, [[16, 3], [1, 128]], 112, -1)
+    ts(pi, pi, 127, ALU.bitwise_and)
+    ts(S("PM", 0, 384), pi, 0, ALU.is_equal)
+    cp("A", S("PM", 384, 768), S("PM", 0, 384), None, None, 64.0)
+    ts(S("IS", 68, 69), pc, 15, ALU.bitwise_and)
+    ts(S("IS", 70, 71), pc, 31, ALU.bitwise_and)
+    ts(S("IS", 72, 73), pc, 16, ALU.bitwise_and)
+    ts(S("IS", 74, 75), pc, 4, ALU.arith_shift_right)
+    cp("V", col(8), S("IS", 68, 69))
+    cp("V", col(9), S("IS", 70, 71))
+    ts(col(10), S("IS", 72, 73), 2048.0, ALU.add)
+    cp("V", col(11), S("IS", 74, 75))
+    ki = S("IS", 128, 192)
+    iota(ki, [[1, 64]], 0, 0)
+    ts(st(JJ, 64), ki, 16.0, ALU.mult, col(8), ALU.add)
+    ts(OJS, ki, 32.0, ALU.mult, col(9), ALU.add)
+    mset(S("BC", 0, 144), 0.0)
+    ts(S("BC", 16, 144, 16), sub(ki, 0, 8), col(11), ALU.is_equal)
+    mset(S("LL", 0, 128), 1.0)
+    for j in range(4):
+        cp("A", S("LL", 128 << j, 256 << j), S("LL", 0, 128 << j))
+    ops[sx]["soft"].append(asel(S("LL", 0, 2048), [[-1, 16], [-16, 8], [0, 16]], 0, 1))
+    cp("A", S("BA", 0, 1440), S("LL", 0, 1440), None, None, 0.0, 1.0)
+    ops[asel(S("BA", 0, 1440), [[-1, 10], [-16, 9], [1000, 16]], 16, 1)]["soft"].append(s2)
+    for row in (0, 3):
+        cp("A", S("BA", 144 * row, 144 * row + 144), S("BA", 144 * row, 144 * row + 144), None, None, BIG)
+    mset(S("VAL", 2048, 2056), 0.0)
+    mset(S("COL", 16, 32), ROOT)
+    cp("A", S("VAL", 2048, 2049), col(16), None, None, ROOT)
+    cp("A", S("VAL", 2049, 2050), col(16), None, None, -ROOT)
+    for a in (0, 4112):
+        cp("A", S("XF", a, a + 16), S("COL", 16, 32), None, None, ROOT)
+        cp("A", S("XB", a, a + 16), S("COL", 16, 32), None, None, -ROOT)
+    m1, m2, m3 = S("IS", 192, 256), S("IS", 256, 320), S("IS", 320, 384)
+    ts(m1, MSI, 63, ALU.bitwise_and)
+    ts(m2, MSI, 6, ALU.arith_shift_right)
+    ts(st(H, 64), m1, 4.0, ALU.mult)
+    ts(st(H + 64, 64), m2, 4.0, ALU.mult)
+    ts(m2, m2, 64.0, ALU.mult)
+    for r, d in ((0, 1.0), (2, 63.0)):
+        ts(m3, m1, d, ALU.add)
+        ts(m3, m3, 63, ALU.bitwise_and)
+        tt(m3, m3, m2, ALU.add)
+        cp("V", sub(ONB, 64 * r, 64), m3)
+    ts(m3, MSI, 64.0, ALU.add)
+    ts(m3, m3, 4095, ALU.bitwise_and)
+    cp("V", sub(ONB, 64, 64), m3)
+    mset(st(MISS, 64), 1.0)
+    mset(st(THR, 64), 9.0)
+
+    def turn(ba, src, rhs, qoff, ev, out, ok=None):
+        nq = width(rhs) // 8
+        mm([(PS(ba, s, nq * 128, 16, 64), (src[0], src[1] + s, src[2], 16) + src[4:], rhs, True, True) for s in range(16)])
+        cp(ev, S("Q", qoff, qoff + nq * 128, 1, 0, 64), PS(ba, 0, nq * 128, 1, 64))
+        back = [(sub(out, 64 * j, 64), S("Q", qoff + 128 * j, qoff + 128 * j + 128, 1, 0, 64)) for j in range(nq)]
+        if ok:
+            mm([it for (o, x) in back for it in ((o, x, S("IDN", 0, 64, 1, 0, 64), True, False), (o, S("PM", 128, 256), ok, False, True))], 0.09)
+        else:
+            tr(back)
+
+    def pick(out, row, src, first=True, last=True):
+        mm([(out, S("BA", row * 144 + 16 - s, row * 144 + 144 - s), (src[0], src[1] + s, src[2], 16) + src[4:],
+             first and s == 0, last and s == 15) for s in range(16)])
+
+    def place_of(eng, pos, w, var, bank, out):
+        qb = sub(QB, 128 * w, 128)
+        axb(eng, qb, pos, 0.25, 191.625)
+        mm([(bank, S("PM", 384 * k + 128 * var, 384 * k + 128 * var + 128), sub(qb, 64 * k, 64), k == 0, k == 1) for k in range(2)])
+        ts(out, bank, -12480.0, ALU.add)
+
+    def own(off, gcol, out, sp, ba, bb):
+        cp("A", gcol, S("AR", 0, 4096), off, after=rest + rows)
+        turn(ba, gcol, RO, 0, "A", PS(bb, 0, 256))
+        if sp:
+            turn(ba, gcol, sub(RS, 32, 8), 512, "A", PS(bb, 256, 320))
+            ts(sp, PS(bb, 256, 320), col(10), ALU.add, 2048.0, ALU.min)
+            ts(st(NOTL, 64), PS(bb, 256, 320), 0.0, ALU.is_ge)
+            for j in range(4):
+                tt(st(out + 64 * j, 64), PS(bb, 64 * j, 64 * j + 64), st(NOTL, 64), ALU.mult)
+        else:
+            cp("A", st(out, 256), PS(bb, 0, 256))
+
+    def fetch1(ch, w, bb, eng):
+        p1 = st(P1 + 128 * w, 128)
+        tt(p1, st(H, 128), st(ch + 128 * w, 128), ALU.add)
+        ts(p1, p1, 0.0, ALU.max, 255.0, ALU.min)
+        place_of(eng, p1, w, 1, PS(bb, 0, 64), sub(OC1, 64 * w, 64))
+        cp(eng, S("AR", 5120 + 1024 * w, 6144 + 1024 * w), S(("PTf", "PTb")[w], 0, 4096), sub(OC1, 64 * w, 64))
+
+    def visit1(r, w, ba, bb, eng):
+        p1, gc, t1 = st(P1 + 128 * w, 128), S("AR", 5120 + 1024 * w, 6144 + 1024 * w), st(T1A + 256 * w, 256)
+        turn(ba, gc, RC[w], 512, eng, PS(bb, 0, 192))
+        if r:
+            ts(sub(OSP, 64 * w, 64), PS(bb, 0, 64), col(10), ALU.add, 2048.0, ALU.min)
+            ts(st(NOTL, 64), PS(bb, 0, 64), 0.0, ALU.is_ge)
+            for k in (1, 2):
+                tt(PS(bb, 64 * k, 64 * k + 64), PS(bb, 64 * k, 64 * k + 64), st(NOTL, 64), ALU.mult)
+        tt(st(B2 + 128 * w, 128), PS(bb, 64, 192), p1, ALU.add)
+        turn(ba, gc, sub(RT, 56, 32), 0, "A", PS(bb, 256, 512))
+        if r:
+            axb("A", t1, PS(bb, 256, 512), 1.0, -5120.0)
+            turn(ba, gc, sub(RS, 0, 32), 0, "A", PS(bb, 0, 256))
+            ts(sub(OFS, 256 * w, 256), PS(bb, 0, 256), col(10), ALU.add, 2048.0, ALU.min)
+        else:
+            cp("A", t1, PS(bb, 256, 512), None, AF.Relu, 1.0, 16.0)
+            tt(st(TM, 128), sub(t1, 0, 128), sub(t1, 128, 128), ALU.min)
+            tt(st(TM, 64), st(TM, 64), st(TM + 64, 64), ALU.min)
+            ts(st(CNT + 64 * w, 64), st(TM, 64), 16.0, ALU.is_lt, BIG, ALU.mult)
+            axb("A", t1, t1, 1.0, -4112.0)
+
+    LT, LI = S("INV", 0, 2080), 2080
+
+    def slot(eng, row, src):
+        for d in (0, 16):
+            cp(eng, S("INV", LI + row + d, LI + 2048, 32), src)
+
+    def lanes_table():
+        add("V", cost(0.5, 2048), lambda: g.vector.transpose(T.INV[:, 0:2048], T.INV[:, LI:LI + 2048]),
+            [S("INV", LI, LI + 2048)], [S("INV", 0, 2048)])
+
+    def visit2(r, w):
+        eng = "VA"[w]
+        bd, bc, ba, bt, cnt = ((PS(U1, 0, 128), PS(U1, 128, 192), U0, PS(TA, 0, 256), PS(VF1, 0, 64)),
+                               (PS(X0, 0, 128), PS(X0, 128, 192), X1, PS(X0, 256, 512), PS(VB, 0, 64)))[w]
+        p1, p2 = st(P1 + 128 * w, 128), st(B2 + 128 * w, 128)
+        if r:
+            o = S("AR", 1024 * w, 1024 * w + 1024)
+            cp(eng, o, LT, sub(OSP, 64 * w, 64))
+            for k in range(2):
+                pick(sub(bd, 64 * k, 64), 1 + 3 * w + k, o)
+            tt(bd, bd, p2, ALU.add)
+        ts(bd, bd if r else p2, 0.0, ALU.max, 255.0, ALU.min)
+        place_of(eng, bd, w, 2 * w, bc, sub(OC2, 64 * w, 64))
+        g2 = S("AR", 2048 + 1024 * w, 3072 + 1024 * w) if r else S("INV", 1024 * w, 1024 * w + 1024)
+        cp(eng, g2, S("PT2", 0, 4096), sub(OC2, 64 * w, 64))
+        tt(bd, bd, p1, ALU.subtract)
+        mm_, gg, ic, ia = st(MM + 64 * w, 64), st(GG + 64 * w, 64), sub(IC, 128 * w, 128), sub(IA, 128 * w, 128)
+        if r == 0:
+            turn(ba, g2, sub(RT, 112 - 112 * w, 32), 0, "A", bt)
+            cp("A", bt, bt, None, AF.Relu, 1.0, 16.0)
+            cnt = st(CNT + 64 * w, 64)
+            for i in range(4):
+                tt(st(TM + 64 * i, 64), cnt, st(T1A + 256 * w + 64 * i, 64), ALU.add)
+        else:
+            for i in range(4):
+                o = S(("XF", "XB")[w], 1024 * i, 1024 * i + 1024)
+                cp("A", o, LT, sub(OFS, 256 * w + 64 * i, 64))
+                pick(cnt, 3 * w, o, i == 0, i == 3)
+            ok = sub(QB, 128 * w, 64)
+            ts(ok, cnt, 0.0, ALU.is_equal, -BIG, ALU.mult)
+            turn(ba, g2, sub(RT, 112 - 112 * w, 32), 0, eng, bt, ok)
+        ts(mm_, cnt, 0.0, ALU.is_gt)
+        ts(gg, cnt, 0.0, ALU.is_equal, 1.0, ALU.add)
+        for k in range(2):
+            tt(sub(bd, 64 * k, 64), sub(bd, 64 * k, 64), mm_, ALU.mult)
+        tt(ic, bd, p1, ALU.add)
+        ts(ia, ic, 3, ALU.bitwise_and)
+        ts(sub(UV, 128 * w, 128), ia, 0.25, ALU.mult, TINY, ALU.max)
+        if r:
+            tt(bt, bt, st(T1A + 256 * w, 256), ALU.max)
+        else:
+            tt(bt, bt, st(TM, 256), ALU.min)
+        ts(sub(OFT, 256 * w, 256), bt, 6144.0 if r else 4112.0, ALU.add)
+        tt(bd, ic, st(H, 128), ALU.subtract)
+        for k in range(2):
+            tt(sub(ia, 64 * k, 64), sub(bd, 64 * k, 64), gg, ALU.mult)
+        ts(ia, ia, 1, ALU.arith_shift_right)
+
+    own(OMS, S("AR", 4096, 5120), FL, None, U0, U1)
+    fetch1(FL, 0, U1, "V")
+    fetch1(FL, 1, X0, "A")
+    visit1(0, 0, U0, U1, "V")
+    visit1(0, 1, X1, X0, "A")
+    nch = 0
+    for r in range(3):
+        if r:
+            lanes_table()
+        visit2(r, 0)
+        if r == 0:
+            dma("G", [(lambda: T.xf[:], lambda: T.x[:])], 2048, [], [S("xf", 0, 4096)], aPT)
+            sw = send([(helper_of(T, topo, rank), S("xf", 0, 4096), S("xg", 0, 4096, 1, 16, 144), "aWh")], 2048)
+            for t in "FB":
+                for k in range(2):
+                    arrive("aW%s%d" % (t, k), half, S("W" + t, 5120 * k + 1024, 5120 * k + 5120), sw, 22 + 20 * k)
+            own(sub(ONB, 0, 64), S("AR", 4096, 5120), FLO, None, VB, VF1)
+        else:
+            o = S("AR", 4096, 5120)
+            cp("A", o, LT, sub(ONS, 64 * (r - 1), 64))
+            for j in range(4):
+                pick(PS(X1, 64 * j, 64 * j + 64), 6 + j, o)
+            nbp = PS(X1, 0, 256)
+            tt(nbp, nbp, st(NB[r], 256), ALU.add)
+            tt(nbp, nbp, st(FL, 256), ALU.subtract)
+            for j in range(4):
+                tt(sub(nbp, 64 * j, 64), sub(nbp, 64 * j, 64), st(MISS, 64), ALU.mult)
+            tt(st(FLO, 256), nbp, st(FL, 256), ALU.add)
+        if r < 2:
+            fetch1(FLO, 0, VB, "A")
+        visit2(r, 1)
+        if r < 2:
+            fetch1(FLO, 1, X1, "A")
+        for w in range(2):
+            tt(st(AA + 128 * w, 128), sub(IA, 128 * w, 128), st(FLO + 128 * w, 128), ALU.subtract)
+        cnone = (1024.0, 2048.0, 1026.0)[r]
+        axb("A", st(JC, 64), st(JJ, 64), 1.0, (0.0, 1024.0, 0.0)[r] - cnone)
+        if r == 0:
+            mset(st(BASE, 64), cnone)
+        else:
+            axb("A", st(BASE, 64), st(JJ, 64), -1.0, cnone - (0.0, 0.0, 1032.0)[r])
+            tt(st(BASE, 64), st(BASE, 64), st(MISS, 64), ALU.mult)
+            tt(st(BASE, 64), st(BASE, 64), st(JJ, 64), ALU.add)
+        if r == 2:
+            axb("A", st(BASE, 64), st(BASE, 64), 1.0, 1032.0)
+        if r < 2:
+            visit1(r + 1, 0, X1, X0, "A")
+            visit1(r + 1, 1, X1, X0, "A")
+        if r == 0:
+            own(sub(ONB, 64, 64), S("INV", 0, 1024), NB[1], sub(ONS, 0, 64), X1, X0)
+            own(sub(ONB, 128, 64), S("INV", 1024, 2048), NB[2], sub(ONS, 64, 64), X1, X0)
+            mset(S("INV", 2048, 4128), 0.0)
+        for w in range(2):
+            for hf in range(2):
+                win = S(("XF", "XB")[w], 0, 8224) if r == 0 else S(("WF", "WB")[w], 0, 10240)
+                off = lambda i: sub(OFT, 256 * w + 64 * i + 32 * hf, 32)
+                ub, vb = (U0, U1)[hf], ((VF0, VF1)[hf], VB)[w]
+                a0, a2 = [S("WK", 1024 * hf + 512 * j, 1024 * hf + 512 * j + 512) for j in range(2)]
+                d1, d2 = [S("WK", 2048 + 512 * ((2 * nch + j) % 3), 2560 + 512 * ((2 * nch + j) % 3)) for j in range(2)]
+                nch += 1
+                for b, k in ((ub, 0), (vb, 1)):
+                    mm([(PS(b, s, 512, 16), S("LL", 128 * s, 128 * s + 128), sub(UV, 128 * w + 64 * k + 32 * hf, 32), True, True)
+                        for s in range(16)])
+                cp("A", a0, win, off(0))
+                cp("A", a2, win, off(2))
+                tt(d1, win, a0, ALU.subtract, off(1))
+                tt(d2, win, a2, ALU.subtract, off(3))
+                tt(PS(TA), PS(ub), d1, ALU.mult)
+                tt(PS(ub), PS(ub), d2, ALU.mult)
+                tt(a0, PS(TA), a0, ALU.add)
+                tt(PS(ub), PS(ub), a2, ALU.add)
+                tt(d2, PS(ub), a0, ALU.subtract)
+                tt(PS(vb), PS(vb), d2, ALU.mult)
+                zb = S("VAL", 1024 + 512 * hf, 1536 + 512 * hf)
+                tt(zb if w else PS(vb), PS(vb), a0, ALU.add)
+                if w:
+                    vf = PS((VF0, VF1)[hf])
+                    gp = S("GAP", 1024 * r + 512 * hf, 1024 * r + 512 * hf + 512)
+                    le = S("AR", 7168 + 512 * hf, 7680 + 512 * hf)
+                    tt(vf, vf, zb, ALU.subtract)
+                    cp("A", gp, vf, None, AF.Abs)
+                    cp("A", vf, vf, None, AF.Copy, 0.5)
+                    ts(le, gp, S("EPS", 0, 1), ALU.is_le)
+                    tt(zb, vf, zb, ALU.add)
+                    mm([(PS(ub, 0, 32), S("BC", 16 - s, 144 - s), (le[0], le[1] + s, le[2], 16) + le[4:], s == 0, s == 15) for s in range(16)])
+                    tt(st(WON + 32 * hf, 32), PS(ub, 0, 32), st(THR + 32 * hf, 32), ALU.is_ge)
+        won = st(WON, 64)
+        ms_ = S("MSG", 320 * (r % 2), 320 * (r % 2) + 320)
+        place = (0, 64, 192, 256)
+        for j in range(4):
+            tt(st(AA + 64 * j, 64), st(AA + 64 * j, 64), won, ALU.mult)
+        for w in range(2):
+            tt(sub(ms_, 192 * w, 128), st(AA + 128 * w, 128), st(FLO + 128 * w, 128), ALU.add)
+        tt(sub(ms_, 128, 64), st(MISS, 64), won, ALU.subtract)
+        if r < 2:
+            lf, lb = S("MF", 192 * r, 192 * r + 192), S("MB", 192 * r, 192 * r + 192)
+            sm = send([(lo, sub(ms_, 0, 192), lf, "aMF%d" % r), (hi, sub(ms_, 128, 192), lb, "aMB%d" % r)], 100)
+            am = [arrive("aMF%d" % r, half, lf, sm), arrive("aMB%d" % r, half, lb, sm)]
+        tt(st(JC, 64), st(JC, 64), won, ALU.mult)
+        tt(st(BASE, 64), st(BASE, 64), st(JC, 64), ALU.add)
+        cp("V", OVP, st(BASE, 64))
+        for j in range(4):
+            slot("A" if j % 2 else "V", 6 + j, sub(ms_, place[j], 64))
+        if r < 2:
+            tt(st(BASE, 64), st(BASE, 64), sub(ms_, 128, 64), ALU.add)
+            cp("V", OVN, st(BASE, 64))
+            win = S("VAL", 1024, 2056) if r == 0 else S("VAL", 0, 2056)
+            vp = S("VAL", 0, 1024) if r == 0 else S("VAL", 2056, 3080)
+            vn = S("WK", 2048, 3072)
+            cp("A", vp, win, OVP)
+            cp("V", vn, win, OVN)
+            s1 = send([(far, vp, D3("vs", 2 * r), "aVp%d" % r), (far, vn, D3("vs", 2 * r + 1), "aVn%d" % r)], 1024)
+            s2 = send([(lo, vp, S("WF", 0, 1024), "aVf%d" % r), (hi, vn, S("WB", 0, 1024), "aVb%d" % r)], 1500, am)
+            arrive("aVf%d" % r, half, S("WF", 0, 1024), s2)
+            arrive("aVb%d" % r, half, S("WB", 0, 1024), s2)
+            arrive("aVp%d" % r, half, D3("vs", 2 * r), s1)
+            arrive("aVn%d" % r, half, D3("vs", 2 * r + 1), s1)
+            sdma("S", [(S("WF", 5120, 6144, 1, 0, 112), D3("vs", 2 * r, 16, 128)), (S("WF", 5120, 6144, 1, 112, 128), D3("vs", 2 * r, 0, 16))], 512)
+            sdma("S", [(S("WB", 5120, 6144, 1, 16, 128), D3("vs", 2 * r + 1, 0, 112)), (S("WB", 5120, 6144, 1, 0, 16), D3("vs", 2 * r + 1, 112, 128))], 512)
+            for row, k in ((1, 0), (2, 1), (0, 2)):
+                slot("V", row, sub(lf, 64 * k, 64))
+            for row, k in ((4, 1), (5, 2), (3, 0)):
+                slot("A", row, sub(lb, 64 * k, 64))
+            for w in range(2):
+                cp("A", st(FL + 128 * w, 128), sub(ms_, 192 * w, 128))
+            cp("A", st(MISS, 64), sub(ms_, 128, 64))
+            axb("A", st(THR, 64), st(MISS, 64), -100.0, 109.0)
+            cp("A", st(GI + 64 * r, 64), st(MISS, 64), None, None, 1024.0)
+            tt(st(GI, 64), st(GI, 64), st((JJ, GI + 64)[r], 64), ALU.add)
+            if r:
+                cp("V", OGI, st(GI, 64))
+    ts(S("WK", 2048, 3072), S("GAP", 0, 3072), 128.0, ALU.min, None, None, OGI)
+    cp("A", S("WK", 2048, 3072), S("WK", 2048, 3072), None, AF.Exp, -1.0)
+    dma("S", [(lambda: T.ye[:], lambda: T.WK[:, 2048:3072])], 512, [S("WK", 2048, 3072)], [])
+    cp("A", S("VAL", 0, 1024), S("VAL", 1024, 3080), OVP)
+    dma("A", [(lambda: T.y[:], lambda: T.VAL[:, 0:1024])], 512, [S("VAL", 0, 1024)], [])
+    axb("V", sub(QB, 0, 64), S("MSG", 128, 192), -1.0, 1.0)
+    slot("V", 0, sub(QB, 0, 64))
+    lanes_table()
+    cp("V", S("WK", 0, 1024), LT, OJS)
+    dma("S", [((lambda k=k: T.yf[8 * k:8 * k + 8, :]), (lambda row=row: T.WK[row:128:16, 0:1024])) for k, row in enumerate((6, 7, 8, 9, 0))],
+        160, [S("WK", 0, 1024)], [])
+    return ops, q
+
+
+ORDER = []
+
+
+def schedule(ops):
+    if ORDER:
+        return ORDER[0]
+    n = len(ops)
+    succ = [[] for _ in range(n)]
+    pred = [sorted(set(o["deps"]) | set(o["soft"])) for o in ops]
+    for i in range(n):
+        for j in pred[i]:
+            succ[j].append(i)
+    prio = [0.0] * n
+    for i in range(n - 1, -1, -1):
+        prio[i] = ops[i]["dur"] + 0.1 + max([prio[j] for j in succ[i]] or [0.0])
+    best, seed = None, 1
+    for it in range(ROUNDS):
+        got = one_pass(ops, succ, pred, prio, (0.25, 0.6, 1.0, 1.6)[it % 4])
+        if best is None or max(got[2]) < max(best[2]):
+            best = got
+        base = got if it % 8 < 6 else best
+        back = one_pass(ops, pred, succ, base[2], 0.25)
+        prio = []
+        for i in range(n):
+            seed = (seed * 1103515245 + 12345) % 2147483648
+            prio.append(back[2][i] + (seed / 2147483648.0) * (0.0, 0.5, 1.5)[it % 3])
+    for it in range(TRIES):
+        prio = [-t for t in best[1]]
+        seed = (seed * 1103515245 + 12345) % 2147483648
+        mid = (seed / 2147483648.0) * max(best[2])
+        for i in range(n):
+            if abs(best[1][i] - mid) < 12.0:
+                seed = (seed * 1103515245 + 12345) % 2147483648
+                if seed % 1000 < (60, 150, 300)[it % 3]:
+                    prio[i] += (seed / 1073741824.0 - 1.0) * (1.0, 3.0, 8.0)[(it // 3) % 3]
+        got = one_pass(ops, succ, pred, prio, (0.3, 1.0, 1.7)[(it // 9) % 3])
+        if max(got[2]) <= max(best[2]):
+            best = got
+    ORDER.append(best)
+    return best
+
+
+ROUNDS, TRIES = 60, 1800
+
+
+def one_pass(ops, succ, pred, prio, slack):
+    n = len(ops)
+    left = [len(p) for p in pred]
+    free = {}
+    done = [0.0] * n
+    start = [0.0] * n
+    can = [0.0] * n
+    ready = [i for i in range(n) if left[i] == 0]
+    order = []
+    while ready:
+        est = [(max(can[i], free.get(ops[i]["eng"], 0.0)) if ops[i]["eng"] else can[i]) for i in ready]
+        first = min(est)
+        e0 = ops[ready[est.index(first)]]["eng"]
+        k = max((k for k in range(len(ready)) if ops[ready[k]]["eng"] == e0 and est[k] <= first + slack), key=lambda k: prio[ready[k]])
+        i = ready.pop(k)
+        o = ops[i]
+        start[i] = est[k]
+        done[i] = est[k] + o["dur"]
+        if o["kind"] == "d":
+            done[i] = free["D"] = max(done[i], free.get("D", 0.0) + o["dur"] - 2.0)
+        if o["eng"]:
+            free[o["eng"]] = est[k] + o["hold"]
+        order.append(i)
+        for j in succ[i]:
+            same = ops[j]["eng"] == o["eng"] and o["kind"] == "c" and not (ops[j]["deps"].get(i) or o["deps"].get(j))
+            same = same or (ops[j]["eng"] == o["eng"] and (i in ops[j]["soft"] or j in o["soft"]))
+            can[j] = max(can[j], start[i] if same else done[i] + 0.1)
+            left[j] -= 1
+            if left[j] == 0:
+                ready.append(j)
+    return order, start, done
+
+
+def rank_program(g, core, T, topo):
+    rank = T.rank_of(core)
+    if rank is None:
+        for r in range(len(T.cores)):
+            if helper_of(T, topo, r) == core:
+                helper_program(g, core, T, topo, r)
+        return
+    ops, q = build(g, core, T, topo, rank)
+    order, _, _ = schedule(ops)
+    count = {}
+    mark = {}
+    for i in order:
+        o = ops[i]
+        if o["kind"] == "c":
+            count[o["eng"]] = count.get(o["eng"], 0) + 1
+            mark[i] = ("c" + o["eng"], count[o["eng"]])
+        else:
+            mark[i] = (o["sem"], o["cnt"])
+    seen = {}
+    for i in order:
+        o = ops[i]
+        if o["kind"] == "a":
+            continue
+        want = {}
+        for j, raw in o["deps"].items():
+            if ops[j]["kind"] == "c" and o["kind"] == "c" and ops[j]["eng"] == o["eng"] and not raw:
+                continue
+            sem, v = mark[j]
+            want[sem] = max(want.get(sem, 0), v)
+        for sem, v in sorted(want.items()):
+            if seen.get((o["eng"], sem), 0) < v:
+                q[o["eng"]].wait_ge(T.sem[sem], v)
+                seen[(o["eng"], sem)] = v
+        r = o["emit"]()
+        if o["kind"] == "c":
+            r.then_inc(T.sem["c" + o["eng"]], 1)
+    total = {}
+    for sem, v in mark.values():
+        total[sem] = max(total.get(sem, 0), v)
+    for sem, v in sorted(total.items()):
+        if seen.get(("G", sem), 0) < v:
+            g.wait_ge(T.sem[sem], v)

@@ -6,29 +6,28 @@ SCRATCH = {
     "WF": ("sbuf", [128, 10240], F32), "WB": ("sbuf", [128, 10240], F32),
     "XF": ("sbuf", [128, 8224], BF), "XB": ("sbuf", [128, 8224], BF),
     "PTf": ("sbuf", [128, 4096], BF), "PTb": ("sbuf", [128, 4096], BF), "PT2": ("sbuf", [128, 4096], BF),
-    "AR": ("sbuf", [128, 8192], BF), "INV": ("sbuf", [128, 4128], BF),
-    "IB": ("sbuf", [128, 1024], I32), "IS": ("sbuf", [128, 640], I32),
-    "CU": ("sbuf", [128, 1024], U16), "OF": ("sbuf", [128, 1024], U16),
-    "WK": ("sbuf", [128, 3584], F32), "GAP": ("sbuf", [128, 3072], F32), "VAL": ("sbuf", [128, 3080], F32),
-    "LL": ("sbuf", [128, 2048], BF), "BA": ("sbuf", [128, 1440], BF), "BC": ("sbuf", [128, 144], BF),
-    "RM": ("sbuf", [128, 288], BF), "PM": ("sbuf", [128, 768], BF), "IDN": ("sbuf", [128, 64], F32),
-    "Q": ("sbuf", [128, 896], F32), "COL": ("sbuf", [128, 52], F32), "EPS": ("sbuf", [128, 4], F32),
-    "ST": ("sbuf", [128, 3520], F32), "SB": ("sbuf", [128, 512], BF),
-    "MSG": ("sbuf", [128, 640], BF), "MF": ("sbuf", [128, 384], BF), "MB": ("sbuf", [128, 384], BF),
+    "AR": ("sbuf", [128, 4096], BF), "INV": ("sbuf", [128, 4096], BF), "GB": ("sbuf", [128, 8224], BF),
+    "IB": ("sbuf", [128, 1024], I32), "IS": ("sbuf", [128, 512], I32),
+    "CU": ("sbuf", [128, 1024], U16), "OF": ("sbuf", [128, 768], U16),
+    "WK": ("sbuf", [128, 3072], F32), "GAP": ("sbuf", [128, 3072], F32), "VAL": ("sbuf", [128, 3072], F32),
+    "LL": ("sbuf", [128, 2048], BF), "BA": ("sbuf", [128, 720], BF), "BC": ("sbuf", [128, 144], BF),
+    "RM": ("sbuf", [128, 240], BF), "PM": ("sbuf", [128, 1920], BF), "ID": ("sbuf", [128, 384], F32),
+    "Q": ("sbuf", [128, 1024], F32), "COL": ("sbuf", [128, 48], F32), "EPS": ("sbuf", [128, 4], F32),
+    "ST": ("sbuf", [128, 576], F32), "SB": ("sbuf", [128, 3712], BF),
     "xd": ("dram", [128, 4096], BF), "xe": ("dram", [160, 4096], BF),
-    "xf": ("dram", [128, 4096], F32), "xg": ("dram", [160, 4096], F32),
-    "vs": ("dram", [4, 128, 1024], F32),
+    "vn": ("dram", [4, 128, 512], F32), "vp": ("dram", [288, 1024], F32),
 }
 for _b in range(8):
     SCRATCH["PS%d" % _b] = ("psum", [128, 512], F32)
-ARRIVALS = (["aXh", "aXF0", "aXF1", "aXB0", "aXB1", "aWh", "aWF0", "aWF1", "aWB0", "aWB1"]
-            + ["aPT%s%d" % (t, h) for t in "fb" for h in range(4)] + ["aPT20", "aPT21"]
-            + ["aM%s%d" % (t, r) for t in "FB" for r in range(2)] + ["aV%s%d" % (t, r) for t in "fbpn" for r in range(2)])
-SEMAPHORES = ["cP", "cV", "cA", "cG", "h00", "h10", "h20", "h01", "h11", "h21"] + ARRIVALS + ["d%d" % i for i in range(60)]
+ARRIVALS = (["aXh", "aXF0", "aXF1", "aXB0", "aXB1", "sB", "sL"]
+            + ["aPT%s%d" % (t, h) for t in "fb" for h in range(4)] + ["aPT2"]
+            + ["a%s%d%d" % (t, r, h) for t in ("Lf", "Lb", "Vb", "Vn") for r in range(2) for h in range(2)]
+            + ["aV%s%d" % (t, r) for t in "fp" for r in range(2)])
+HANDED = ["h0", "h1", "hF", "hv0", "hv1", "hw0", "hw1"]
+SEMAPHORES = ["cP", "cV", "cA", "cG"] + ARRIVALS + HANDED + ["d%d" % i for i in range(60)]
 
 TINY = 2.0 ** -48
 ROOT = 2.0 ** 52
-BIG = 16384.0
 
 
 def S(name, lo, hi, step=1, p0=0, p1=128, ps=1):
@@ -43,8 +42,12 @@ def width(s):
     return (s[2] - s[1] + s[3] - 1) // s[3]
 
 
-def sub(s, a, w):
-    return (s[0], s[1] + a, s[1] + a + w) + s[3:]
+def sub(s, a, w, step=1):
+    return (s[0], s[1] + a, s[1] + a + (w - 1) * step + 1, step) + s[4:]
+
+
+def part(s, p0, p1):
+    return s[:4] + (p0, p1, 1)
 
 
 def helper_of(T, topo, rank):
@@ -70,21 +73,40 @@ def helper_program(g, core, T, topo, rank):
     n = len(T.cores)
     lo, hi, far = T.cores[(rank - 1) % n], T.cores[(rank + 1) % n], T.cores[(rank + 2) % n]
     full = len(topo.engines(T.cores[rank], core))
-    ma, mb, na, nb = pair_masks(topo, core, lo, hi)
-    mc, md, nc, nd = pair_masks(topo, core, far, far)
-    for k, (t, x, a, b) in enumerate((("X", T.xe, 16, 4128), ("W", T.xg, 1024, 6144))):
-        one = lambda c, m, w, v, row, at: RemoteDMATransfer(dst_ids=[dst_id(topo, c)], dma_engine_mask=m, remote_sem=T.sem["a%s%s%d" % (t, w, v)],
-                                                            src=x[row:row + 128, :], dst=T[t + w][:, at:at + 4096])
-        g.sync.wait_ge(T.sem["a%sh" % t], full)
-        g.sync.dma_start(x[0:16, :], x[128:144, :]).then_inc(T.sem["h0%d" % k], 16)
-        g.sync.dma_start(x[144:160, :], x[16:32, :]).then_inc(T.sem["h0%d" % k], 16)
-        g.wait_ge(T.sem["a%sh" % t], full)
-        g.remote_dma_fused([one(lo, ma, "F", 0, 16, a), one(hi, mb, "B", 0, 16, a)], local_sem=T.sem["h1%d" % k])
-        g.wait_ge(T.sem["h0%d" % k], 32)
-        g.remote_dma_fused([one(far, mc, "F", 1, 32, b), one(far, md, "B", 1, 0, b)], local_sem=T.sem["h2%d" % k])
-    for k in range(2):
-        g.wait_ge(T.sem["h1%d" % k], na + nb)
-        g.wait_ge(T.sem["h2%d" % k], nc + nd)
+    x = T.xe
+    g.sync.wait_ge(T.sem.aXh, full)
+    g.sync.dma_start(x[0:16, :], x[128:144, :]).then_inc(T.sem.h0, 16)
+    g.sync.dma_start(x[144:160, :], x[16:32, :]).then_inc(T.sem.h0, 16)
+    g.wait_ge(T.sem.aXh, full)
+    sent = 0
+    for k, (c, w, v, row) in enumerate(((hi, "B", 0, 16), (far, "B", 1, 0), (lo, "F", 0, 16), (far, "F", 1, 32))):
+        if k == 1:
+            g.wait_ge(T.sem.h0, 32)
+        rid, pid, _ = topo.addr(c)
+        g.remote_dma(T["X" + w][:, 16 + 4112 * v:4112 + 4112 * v], x[row:row + 128, :], T.sem["aX%s%d" % (w, v)], T.sem.h1, pid, rid, topo.mask(core, c))
+        sent += len(topo.engines(core, c))
+    for r in range(2):
+        x, top = T.vp, 144 * r
+        g.sync.wait_ge(T.sem["hv%d" % r], full)
+        g.sync.dma_start(x[top + 128:top + 144, :], x[top:top + 16, :]).then_inc(T.sem["hw%d" % r], 16)
+        g.wait_ge(T.sem["hw%d" % r], 16)
+        if r:
+            g.wait_ge(T.sem.hF, 2)
+        ma, mb, na, nb = pair_masks(topo, core, lo, far)
+        g.remote_dma_fused([RemoteDMATransfer(dst_ids=[dst_id(topo, c)], dma_engine_mask=m, remote_sem=T.sem[s % r], src=x[top + row:top + row + 128, :],
+                                              dst=T.WF[:, o:o + 1024])
+                            for c, m, s, row, o in ((lo, ma, "aVf%d", 0, 0), (far, mb, "aVp%d", 16, 5120))], local_sem=T.sem.h1)
+        sent += na + nb
+    g.wait_ge(T.sem.h1, sent)
+
+
+WAKE = 0.22
+CY, PE, GATHER, SCATTER = 0.00086, 0.00045, 1.45, 3.5
+HALVED = [(r, h) for r in range(3) for h in range(2)]
+ADDED = [(r, w, h) for r in range(3) for w in range(2) for h in range(2)]
+BY_DMA = {"B": (4, 4), "F": (4, 2)}
+RATE = (280.0, 210.0)
+START = (32.0, 68.0, 106.0)
 
 
 def build(g, core, T, topo, rank):
@@ -92,7 +114,7 @@ def build(g, core, T, topo, rank):
     lo, hi, far = T.cores[(rank - 1) % n], T.cores[(rank + 1) % n], T.cores[(rank + 2) % n]
     ops = []
     acc = {}
-    nsem = [0]
+    nsem, now = [0], [0.0]
     q = {"P": g.tensor, "V": g.vector, "A": g.scalar, "S": g.sync, "G": g}
 
     def ap(s):
@@ -126,8 +148,12 @@ def build(g, core, T, topo, rank):
         for j in after:
             deps[j] = True
         ops.append({"eng": eng, "dur": dur, "emit": emit, "deps": deps, "kind": kind, "sem": sem, "cnt": cnt,
-                    "hold": dur if hold is None else hold, "soft": []})
+                    "hold": hold, "soft": [], "when": now[0]})
+        now[0] += 0.001
         return i
+
+    def at(t):
+        now[0] = t
 
     def new_sem():
         nsem[0] += 1
@@ -136,8 +162,8 @@ def build(g, core, T, topo, rank):
     def is2(s):
         return SCRATCH[s[0]][2] in (BF, U16)
 
-    def cost(c, k):
-        return 0.06 + max(64, c * k) * 0.001
+    def cost(c, k, e="V"):
+        return (0.055 if e == "V" else 0.07) + max(64, c * k) * CY
 
     def cols(x):
         return [x] if isinstance(x, tuple) else []
@@ -146,242 +172,262 @@ def build(g, core, T, topo, rank):
         return ap(x) if isinstance(x, tuple) else x
 
     def ts(out, in0, s1, op0, s2=None, op1=None, off=None):
-        def emit():
+        def emit(e):
             a = ind(in0, off) if off else ap(in0)
             if op1 is None:
                 return g.vector.tensor_scalar(ap(out), a, val(s1), None, op0)
             return g.vector.tensor_scalar(ap(out), a, val(s1), val(s2), op0, op1)
-        c = 1.55 if off else (0.5 if is2(out) and is2(in0) else 1)
-        return add("V", cost(c, width(out)), emit, [in0] + cols(s1) + cols(s2) + cols(off), [out])
+        c = GATHER if off else (0.5 if is2(out) and is2(in0) else 1)
+        return add("V", {"V": cost(c, width(out))}, emit, [in0] + cols(s1) + cols(s2) + cols(off), [out])
 
     def tt(out, in0, in1, op, off=None):
-        def emit():
+        def emit(e):
             return g.vector.tensor_tensor(ap(out), ind(in0, off) if off else ap(in0), ap(in1), op)
         c = 2 if not (in0[0].startswith("PS") or in1[0].startswith("PS")) else 1
-        return add("V", cost(1.8 if off else c, width(out)), emit, [in0, in1] + cols(off), [out])
+        return add("V", {"V": cost(GATHER if off else c, width(out))}, emit, [in0, in1] + cols(off), [out])
 
-    def cp(eng, out, in_, off=None, func=None, scale=1.0, bias=0.0, after=()):
-        def emit():
-            a = ind(in_, off) if off else ap(in_)
-            if eng == "V":
-                return g.vector.tensor_copy(ap(out), a)
-            if bias != 0.0:
-                return g.scalar.activation(ap(out), a, func or AF.Identity, bias=val(bias), scale=scale)
-            if scale != 1.0:
-                return g.scalar.activation(ap(out), a, func or AF.Copy, scale=scale)
-            return g.scalar.activation(ap(out), a, func or AF.Copy)
-        c = 1.55 if off else (0.5 if eng == "V" and is2(out) and is2(in_) else 1)
-        return add(eng, cost(c, width(out)), emit, [in_] + cols(off) + cols(bias), [out], after=after)
-
-    def axb(eng, out, in_, a, b):
-        return cp("A", out, in_, None, None, a, b) if eng == "A" else ts(out, in_, a, ALU.mult, b, ALU.add)
+    def cp(eng, out, in_, off=None, a=1.0, b=0.0, func=None, after=()):
+        def emit(e):
+            x = ind(in_, off) if off else ap(in_)
+            if e == "V":
+                if func == AF.Relu:
+                    return g.vector.tensor_scalar(ap(out), x, val(b), 0.0, ALU.add, ALU.max)
+                if a == 1.0 and b == 0.0:
+                    return g.vector.tensor_copy(ap(out), x)
+                return g.vector.tensor_scalar(ap(out), x, val(a), val(b), ALU.mult, ALU.add)
+            if b != 0.0:
+                return g.scalar.activation(ap(out), x, func or AF.Identity, bias=val(b), scale=val(a))
+            if a != 1.0:
+                return g.scalar.activation(ap(out), x, func or AF.Copy, scale=val(a))
+            return g.scalar.activation(ap(out), x, func or AF.Copy)
+        dur = {e: cost(GATHER if off else (0.5 if e == "V" and is2(out) and is2(in_) else 1), width(out), e) for e in eng}
+        return add(eng, dur, emit, [in_] + cols(off) + cols(a) + cols(b), [out], after=after)
 
     def mset(out, v):
-        return add("V", cost(0.5 if is2(out) else 1, width(out)), lambda: g.vector.memset(ap(out), v), [], [out])
+        return add("V", {"V": cost(0.5 if is2(out) else 1, width(out))}, lambda e: g.vector.memset(ap(out), v), [], [out])
 
     def iota(out, pat, base, cm):
-        return add("G", 0.15 + width(out) * 0.002, lambda: g.iota(ap(out), pat, base, cm), [], [out])
+        return add("G", {"G": 0.15 + width(out) * 2 * CY}, lambda e: g.iota(ap(out), pat, base, cm), [], [out])
 
-    def asel(out, pat, base, cm):
-        return add("G", 0.2 + width(out) * 0.002,
-                   lambda: g.affine_select(ap(out), ap(out), pat, ALU.is_equal, 0.0, base, cm), [out], [out])
+    def asel(out, pat, base, cm, in_=None):
+        return add("G", {"G": 0.2 + width(out) * 2 * CY},
+                   lambda e: g.affine_select(ap(out), ap(in_ or out), pat, ALU.is_equal, 0.0, base, cm), [in_ or out], [out])
 
-    def mm(items, each=0.04):
-        def emit():
+    def mm(items, first=True, last=True):
+        def emit(e):
             r = None
-            for (o, l, x, a, b) in items:
-                r = g.tensor.matmul(ap(o), ap(l), ap(x), a, b)
+            for k, (o, l, x) in enumerate(items):
+                r = g.tensor.matmul(ap(o), ap(l), ap(x), first and k == 0, last and k == len(items) - 1)
             return r
         rd = sorted({s for it in items for s in it[1:3]})
         wr = sorted({it[0] for it in items})
-        return add("P", 0.05 + each * len(items), emit, rd, wr)
+        i = add("P", {"P": 0.03 + sum(max(64, width(x)) * (1 if is2(x) else 4) * PE for (_, _, x) in items)}, emit, rd, wr)
+        for j in ops[i]["deps"]:
+            ops[i]["deps"][j] = ops[i]["deps"][j] and (first or ops[j]["eng"] != "P")
+        return i
 
-    def tr(items):
-        def emit():
-            r = None
-            for (o, x) in items:
-                r = g.tensor.transpose(ap(o), ap(x), T.IDN[0:64, 0:64])
-            return r
-        return add("P", 0.05 + sum(0.002 * width(it[0]) for it in items), emit,
-                   [it[1] for it in items] + [S("IDN", 0, 64)], [it[0] for it in items])
+    def flip(out, in_):
+        return add("V", {"V": cost(0.5 if is2(out) else 1, width(out))}, lambda e: g.vector.transpose(ap(out), ap(in_)), [in_], [out])
 
     def dma(eng, items, kb, reads, writes, after=()):
         sem = new_sem()
 
-        def emit():
+        def emit(e):
             for (o, x) in items:
                 q[eng].dma_start(o(), x()).then_inc(T.sem[sem], 16)
-        return add(eng, 2.0 + kb / 330.0, emit, reads, writes, "d", sem, 16 * len(items), after,
-                   hold=(1.0 if eng == "G" else 0.1) * len(items))
+        return add(eng, {eng: 1.8 + kb / RATE[0]}, emit, reads, writes, "d", sem, 16 * len(items), after,
+                   hold=(1.0 if eng == "G" else 0.07) * len(items))
 
     def sdma(eng, pairs, kb, after=()):
         return dma(eng, [((lambda o=o: ap(o)), (lambda x=x: ap(x))) for (o, x) in pairs], kb,
                    [x for (_, x) in pairs], [o for (o, _) in pairs], after)
 
-    def send(items, kb, after=()):
+    def send(items, kb, after=(), hold=0.35):
         sem = new_sem()
-        if len(items) == 2:
+        if items[0][1] is None:
+            masks, cnt = [1 << topo.engines(core, it[0])[k] for k, it in enumerate(items)], len(items)
+        elif len(items) == 2:
             ma, mb, na, nb = pair_masks(topo, core, items[0][0], items[1][0])
             masks, cnt = [ma, mb], na + nb
         else:
             masks, cnt = [topo.mask(core, items[0][0])], len(topo.engines(core, items[0][0]))
 
-        def emit():
-            if len(items) == 1:
-                c, s, d, rs = items[0]
-                rid, pid, _ = topo.addr(c)
-                g.remote_dma(ap(d), ap(s), T.sem[rs], T.sem[sem], pid, rid, masks[0])
-            else:
-                g.remote_dma_fused([RemoteDMATransfer(dst_ids=[dst_id(topo, c)], dma_engine_mask=m, remote_sem=T.sem[rs],
-                                                      src=ap(s), dst=ap(d)) for (c, s, d, rs), m in zip(items, masks)],
-                                   local_sem=T.sem[sem])
-        return add("G", 2.0 + kb / 270.0, emit, [it[1] for it in items], [], "d", sem, cnt, after, hold=0.3)
+        def emit(e):
+            g.remote_dma_fused([RemoteDMATransfer(dst_ids=[dst_id(topo, c)], dma_engine_mask=m, remote_sem=T.sem[rs], src=ap(s), dst=ap(d))
+                                if s else RemoteDMATransfer(dst_ids=[dst_id(topo, c)], dma_engine_mask=m, remote_sem=T.sem[rs])
+                                for (c, s, d, rs), m in zip(items, masks)], local_sem=T.sem[sem])
+        return add("G", {"G": 1.8 + hold + kb / RATE[1]}, emit, [it[1] for it in items if it[1]], [], "d", sem, cnt, after, hold=hold)
 
+    helper = lambda d: helper_of(T, topo, (rank + d) % n)
     half = len(topo.engines(core, lo)[0::2])
     whole = len(topo.engines(core, far))
 
-    def arrive(sem, cnt, piece, like, lag=0.5):
-        i = add(None, lag, None, [], [piece], "a", sem, cnt)
+    def arrive(sem, cnt, piece, like, lag=0.3):
+        i = add(None, {None: lag}, None, [], [piece] if piece else [], "a", sem, cnt)
         ops[i]["soft"].append(like)
         return i
 
-    PS = lambda b, l=0, h=512, step=1, p1=128: S("PS%d" % b, l, h, step, 0, p1)
-    X0, X1, TA, U0, U1, VF0, VF1, VB = 0, 1, 2, 3, 4, 5, 6, 7
+    PS = lambda b, l=0, h=512, step=1: S("PS%d" % b, l, h, step)
+    X0, X1, X2, U0, U1, T0, T1, VB = range(8)
     col = lambda j: S("COL", j, j + 1)
-    H, P1, B2, T1A = 0, 128, 384, 896
-    NB = [None, 1408, 1664]
-    FL, FLO, AA, TM, MM, GG, CNT, NOTL = 1920, 2176, 2432, 2688, 2944, 3072, 3200, 3328
-    JJ, THR, WON, MISS, BASE, JC, GI = 640, 704, 768, 832, 3392, 3456, CNT
+    sb = lambda a, w: S("SB", a, a + w)
     st = lambda a, w: S("ST", a, a + w)
-    IA, IC = S("IB", 0, 256), S("IB", 256, 512)
+    gb = lambda a, w=1024: S("GB", a, a + w)
+    H, P1, P2, QB, RR, UV = sb(0, 128), [sb(128, 256), sb(384, 256)], sb(640, 256), sb(896, 640), sb(1536, 768), sb(2304, 256)
+    FL, FLO, MSG, MISS = sb(2560, 256), sb(2816, 256), sb(3072, 256), [sb(3328, 64), sb(3392, 64)]
+    OK, WON, PEN, ONE = sb(3456, 64), sb(3520, 64), sb(3584, 64), sb(3648, 64)
+    T1A, JJ = st(0, 512), st(512, 64)
+    AA, JC, DN, TM = S("IB", 0, 256), S("IB", 256, 384), S("IB", 384, 512), S("IB", 512, 576)
     OFS, OFT = S("CU", 0, 512), S("CU", 512, 1024)
-    OC1, OC2, OSP, ONB, OMS, OJS, OVP, OVN, OGI, ONS = [S("OF", a, b) for a, b in (
-        (0, 128), (128, 256), (256, 384), (384, 576), (576, 640), (640, 704), (704, 768), (768, 832), (832, 896), (896, 1024))]
-    UV, QB = S("SB", 0, 256), S("SB", 256, 512)
+    OC1, OC2, OSP, ONB, OMS, ONS, OGI = [S("OF", a, b) for a, b in (
+        (0, 128), (128, 256), (256, 384), (384, 576), (576, 640), (640, 704), (704, 768))]
+    LTB, LTF, GC, LTO, GNB, LE = 0, 1040, 2080, 4128, 5152, 7200
     MSI = S("IS", 0, 64)
-    FB = S("BA", 0, 1024)
+    FB = S("SB", 1536, 2560)
+    ID, HALF, LESS = S("ID", 0, 128), S("ID", 128, 256), S("ID", 256, 384)
+    pm = lambda k: S("PM", 128 * k, 128 * k + 128)
+    moved = lambda k, var: S("PM", 256 * k + (112, 0, 16)[var], 256 * k + (112, 0, 16)[var] + 128)
+    UP, EYE, DOWN = [moved(0, var) for var in range(3)]
 
-    dma("S", [(lambda: ap(MSI), lambda: T.ms[:])], 32, [], [MSI])
-    lc = dma("S", [(lambda: T.IB[:], lambda: T.fl[:])], 512, [], [S("IB", 0, 1024)])
+    l0 = dma("S", [(lambda: ap(MSI), lambda: T.ms[:])], 32, [], [MSI])
+    lc = dma("S", [(lambda: T.IB[:], lambda: T.cor[:])], 512, [], [S("IB", 0, 1024)])
+    lx = dma("S", [(lambda: T.xd[:], lambda: T.x[:])], 1024, [], [S("xd", 0, 4096)])
+    ops[lc]["soft"].append(l0)
+    ops[lx]["soft"].append(lc)
+    early = [cp("V", S("CU", 512 * i, 512 * i + 512), S("IB", 512 * i, 512 * i + 512)) for i in range(2)]
+    dma("S", [(lambda: T.IB[:], lambda: T.fl[:])], 512, [], [S("IB", 0, 1024)])
+    at(9)
     cp("V", FB, S("IB", 0, 1024))
-    dma("A", [(lambda: T.IB[:], lambda: T.cor[:])], 512, [], [S("IB", 0, 1024)])
-    ops[lc]["soft"].append(lc - 1)
-    ops[dma("S", [(lambda: T.xd[:], lambda: T.x[:])], 1024, [], [S("xd", 0, 4096)])]["soft"].append(lc)
+    at(0)
     dma("S", [(lambda: T.EPS[:, 0:1], lambda: T.eps[:])], 1, [], [S("EPS", 0, 1)])
-    sx = send([(helper_of(T, topo, rank), S("xd", 0, 4096), S("xe", 0, 4096, 1, 16, 144), "aXh")], 1024)
-    arrive("aXF0", half, S("XF", 16, 4112), sx, 9)
-    arrive("aXB0", half, S("XB", 16, 4112), sx, 9)
-    arrive("aXF1", half, S("XF", 4128, 8224), sx, 15)
-    arrive("aXB1", half, S("XB", 4128, 8224), sx, 15)
+    sx = send([(helper(0), S("xd", 0, 4096), S("xe", 0, 4096, 1, 16, 144), "aXh")], 1024, hold=5.0)
+    for k, (t, v) in enumerate((("B", 0), ("B", 1), ("F", 0), ("F", 1))):
+        arrive("aX%s%d" % (t, v), whole, S("X" + t, 16 + 4112 * v, 4112 + 4112 * v), sx, 11 + 4.5 * k)
 
     pc = S("IS", 64, 65)
     iota(pc, [[0, 1]], 0, 1)
-    iota(S("IS", 384, 640), [[1, 16], [0, 16]], 0, 0)
-    iota(S("IS", 128, 144), [[1, 16]], 0, 0)
+    iota(S("IS", 256, 512), [[1, 16], [0, 16]], 0, 0)
+    iota(S("IS", 128, 192), [[0, 4], [1, 16]], 0, 0)
     iota(S("IS", 80, 97), [[16, 17]], -64, 0)
-    ts(S("IS", 66, 67), pc, 8, ALU.bitwise_and)
-    ts(col(0), S("IS", 66, 67), 0, ALU.is_equal)
-    ts(col(1), S("IS", 66, 67), 8, ALU.is_equal)
-    ts(S("COL", 32, 49), S("IS", 80, 97), col(0), ALU.mult)
-    step = lambda v: col(32 + (v + 64) // 16)
-    ts(S("INV", 256, 272), S("IS", 128, 144), col(1), ALU.mult)
-    for j in range(4):
-        cp("V", S("INV", 256 + (16 << j), 256 + (32 << j)), S("INV", 256, 256 + (16 << j)))
-    ts(PS(0, 0, 256), S("IS", 384, 640), col(0), ALU.mult)
+    ts(S("IS", 66, 67), pc, 15, ALU.bitwise_and)
+    cp("V", col(8), S("IS", 66, 67))
+    ts(col(0), col(8), 5.0, ALU.is_lt)
+    ts(col(1), col(8), 5.0, ALU.is_ge)
+    ts(S("COL", 24, 41), S("IS", 80, 97), col(0), ALU.mult)
+    step = lambda v: col(24 + (v + 64) // 16)
+    ts(col(3), col(8), 6.0, ALU.not_equal, col(1), ALU.mult)
+    ts(col(2), col(8), 6.0, ALU.is_equal, step(-64), ALU.add)
+    ts(S("INV", 256, 320), S("IS", 128, 192), col(3), ALU.mult)
+    for j in range(2):
+        cp("V", S("INV", 256 + (64 << j), 256 + (128 << j)), S("INV", 256, 256 + (64 << j)))
+    ts(PS(0, 0, 256), S("IS", 256, 512), col(0), ALU.mult)
     tt(S("INV", 0, 256), PS(0, 0, 256), S("INV", 256, 512), ALU.add)
-    LC = S("AR", 7168, 8192)
+    LC = gb(LE)
+    cp("V", S("INV", 256, 512), S("INV", 0, 256), None, 1.0, step(16))
+    cp("V", S("INV", 512, 1024), S("INV", 0, 512), None, 1.0, step(32))
     for j in range(1, 4):
-        ts(S("INV", 256 * j, 256 * j + 256), S("INV", 0, 256), step(16 * j), ALU.add)
-    cp("A", S("INV", 3072, 4096), S("INV", 0, 1024), None, None, 1.0, step(192))
-    ts(S("INV", 1024, 2048), S("INV", 0, 1024), step(64), ALU.add)
-    ts(S("INV", 2048, 3072), S("INV", 0, 1024), step(128), ALU.add)
-    ts(LC, S("INV", 0, 1024), step(-64), ALU.add)
+        cp("VA", S("INV", 1024 * j, 1024 * j + 1024), S("INV", 0, 1024), None, 1.0, step(64 * j))
+    cp("VA", LC, S("INV", 0, 1024), None, 1.0, col(2))
     cp("V", OMS, MSI)
-    add("V", cost(3.5, 1024), lambda: g.vector.tensor_copy(ind(S("INV", 0, 4096), OMS), ap(LC)), [LC, OMS], [S("INV", 0, 4096)])
-    for i in range(2):
-        cp("V", S("CU", 512 * i, 512 * i + 512), S("IB", 512 * i, 512 * i + 512))
-    first = [cp("VA"[k % 2], S("AR", 1024 * k, 1024 * k + 1024), S("INV", 0, 4096), S("CU", 64 * k, 64 * k + 64)) for k in range(4)]
-    rowq = (5, 6, 13, 14)
-    rest = [dma("S", [(lambda: T.AR[4:128:8, 0:4096], lambda: T.INV[4:128:8, 0:4096])], 128, [S("INV", 0, 4096)], [], first),
-            dma("S", [((lambda k=k: T.AR[rowq[k]:128:16, 0:4096]), (lambda k=k: T.BA[32 * k:32 * k + 32, 0:1024])) for k in range(4)],
-                256, [FB], [], first)]
-    aPT, rows, last = [], [], {"V": first[2], "A": first[3]}
-    for k in range(2):
-        ops[first[k + 2]]["soft"].append(first[k])
+    sc = add("V", {"V": cost(SCATTER, 1024)}, lambda e: g.vector.tensor_copy(ind(S("INV", 0, 4096), OMS), ap(LC)), [LC, OMS], [S("INV", 0, 4096)])
+    ops[sc]["soft"] += early
+    ones = lambda w: S("BA", 0, w)
+    mset(ones(720), 1.0)
+    keep = lambda i: sb(2560 + 128 * i, 128)
+    asel(S("PM", 0, 256), [[0, 2], [-1, 128]], 0, 1, ones(256))
+    asel(sb(2560, 512), [[-1000, 4], [-8, 16], [999, 8]], 0, 1, ones(512))
+    asel(sb(3200, 512), [[-1, 4], [-4, 8], [-32, 16]], 384, 1, ones(512))
+    ts(col(4), col(8), 4.0, ALU.is_ge)
+    ts(col(4), col(8), 7.0, ALU.is_lt, col(4), ALU.mult)
+    cp("VA", keep(4), EYE, None, col(4))
+    stage = (LTB, LTF, GC, GC + 1024, LTO, GNB, GNB + 1024, LE)
+    last, laid = [], []
     for k in range(4):
-        for i in range(1, 4):
-            c = 4096 + 1024 * ((3 * k + i - 1) % 4)
-            e = "AVAAVAVAVAVA"[3 * k + i - 1]
-            j = cp(e, S("AR", c, c + 1024), S("INV", 0, 4096), S("CU", 256 * i + 64 * k, 256 * i + 64 * k + 64))
-            ops[j]["soft"].append(last[e])
-            last[e] = j
-            rows.append(dma("S", [((lambda i=i, k=k: T.AR[i:128:8, 1024 * k:1024 * k + 1024]), (lambda i=i, c=c: T.AR[i:128:8, c:c + 1024]))],
-                            32, [S("AR", c, c + 1024)], [], [first[k]]))
-        land = lambda t: S(t, 1024 * k, 1024 * k + 1024)
-        s1 = send([(lo, land("AR"), land("PTf"), "aPTf%d" % k), (hi, land("AR"), land("PTb"), "aPTb%d" % k)], 512, rest + rows[-3:])
-        aPT += [arrive("aPTf%d" % k, half, land("PTf"), s1), arrive("aPTb%d" % k, half, land("PTb"), s1)]
-        if k % 2:
-            land = lambda t: S(t, 1024 * k - 1024, 1024 * k + 1024)
-            s2 = send([(far, land("AR"), land("PT2"), "aPT2%d" % (k // 2))], 700, rest + rows[-6:])
-            aPT.append(arrive("aPT2%d" % (k // 2), whole, land("PT2"), s2, 1.0))
+        a, b = 1024 * k, 1024 * k + 1024
+        made = []
+        at(7 + k)
+        for h in range(2):
+            mm([(PS(2 * k + h), keep(4), S("INV", a + 512 * h, a + 512 * h + 512))], True, False)
+        at(8 + 3 * k)
+        for i in range(4):
+            c = stage[(4 * k + i) % 8]
+            made.append(cp("VA"[i % 2], gb(c), S("INV", 0, 4096), S("CU", 256 * i + 64 * k, 256 * i + 64 * k + 64)))
+            ops[made[i]]["soft"] += last + (laid[-2:][i % 2:i % 2 + 1] if i > 1 else [])
+            for h in range(2):
+                if i == 2:
+                    mm([(PS(2 * k + h), keep(5 + k), sub(FB, 512 * h, 512))], False, False)
+                mm([(PS(2 * k + h), keep(i), gb(c + 512 * h, 512))], False, i == 3)
+        for h in range(2):
+            laid.append(cp("VA"[h], S("AR", a + 512 * h, a + 512 * h + 512), PS(2 * k + h)))
+        last = made[2:]
+        land = lambda t: S(t, a, b)
+        s1 = send([(hi, land("AR"), land("PTb"), "aPTb%d" % k), (lo, land("AR"), land("PTf"), "aPTf%d" % k)], 512)
+        arrive("aPTf%d" % k, half, land("PTf"), s1)
+        arrive("aPTb%d" % k, half, land("PTb"), s1)
+    s2 = send([(far, S("AR", 0, 4096), S("PT2", 0, 4096), "aPT2")], 1024)
+    ops[s2]["soft"].append(s1)
+    arrive("aPT2", whole, S("PT2", 0, 4096), s2)
 
-    mset(S("IDN", 0, 64), 1.0)
-    asel(S("IDN", 0, 64), [[-1, 64]], 0, 1)
-    ei = S("IS", 128, 296)
-    iota(ei, [[-16, 3], [-1, 7], [-16, 8]], 144, 1)
-    ts(ei, ei, 127, ALU.bitwise_and)
-    E0, E8, RT, RS = S("BA", 1024, 1192), S("BA", 1192, 1360), S("RM", 0, 168), S("RM", 168, 208)
-    RC, RO = [S("RM", 208, 232), S("RM", 232, 256)], S("RM", 256, 288)
-    ts(E0, ei, 0, ALU.is_equal)
-    ts(E8, ei, 8, ALU.is_equal)
-    ts(RT, E0, 16.0, ALU.mult)
-    tt(RT, RT, E8, ALU.add)
-    ts(RS, sub(E0, 56, 40), 32.0, ALU.mult)
-    tt(RS, RS, sub(E8, 56, 40), ALU.add)
-    for w, e in ((0, E0), (1, E8)):
-        cp("A", sub(RC[w], 0, 8), sub(RS, 32, 8))
-        cp("A", sub(RC[w], 8, 16), sub(e, 96, 16))
-        cp("A", sub(RO, 16 * w, 16), sub(e, 96, 16))
-    pi = S("IS", 256, 640)
-    iota(pi, [[16, 3], [1, 128]], 112, -1)
-    ts(pi, pi, 127, ALU.bitwise_and)
-    ts(S("PM", 0, 384), pi, 0, ALU.is_equal)
-    cp("A", S("PM", 384, 768), S("PM", 0, 384), None, None, 64.0)
-    ts(S("IS", 68, 69), pc, 15, ALU.bitwise_and)
-    ts(S("IS", 70, 71), pc, 31, ALU.bitwise_and)
-    ts(S("IS", 72, 73), pc, 16, ALU.bitwise_and)
+    at(20)
+    mset(ID, 1.0)
+    asel(ID, [[-1, 128]], 0, 1)
+    cp("VA", HALF, ID, None, 0.5)
+    cp("VA", LESS, ID, None, -0.5)
+    EM, RT = sb(896, 128), [S("RM", 32 * v, 32 * v + 32) for v in range(3)]
+    RH, RO, RC = S("RM", 96, 128), S("RM", 128, 160), S("RM", 160, 168)
+    asel(EM, [[-1, 16], [-16, 8]], 0, 1, ones(128))
+    cp("VA", RT[1], sub(EM, 0, 32), None, 16.0)
+    tt(RT[1], RT[1], sub(EM, 64, 32), ALU.add)
+    mm([(PS(X2, 0, 32), DOWN, RT[1]), (PS(X2, 64, 96), UP, RT[1])])
+    for v in (0, 2):
+        cp("VA", RT[v], PS(X2, 32 * v, 32 * v + 32))
+    ts(RC, sub(EM, 48, 8), -512.0, ALU.mult)
+    tt(RC, RC, sub(EM, 32, 8), ALU.add)
+    ts(RC, RC, 16.0, ALU.mult)
+    tt(RC, RC, sub(EM, 40, 8), ALU.add)
+    cp("VA", RH, sub(EM, 0, 32), None, -1.0)
+    cp("VA", RO, sub(EM, 96, 32))
+    RF, TWO = S("RM", 168, 176), S("RM", 176, 240)
+    cp("VA", RF, sub(EM, 0, 8))
+    tt(TWO, sub(EYE, 0, 64), sub(EYE, 64, 64), ALU.add)
+    cp("VA", S("PM", 256, 512), S("PM", 0, 256), None, 64.0)
+    scaled = {64.0: pm(2), 1.0: EYE}
+    for k, v in enumerate((-1.0, -16.0, 0.5, -0.5, 0.25, 0.1875, 512.0)):
+        scaled[v] = pm(4 + k)
+        cp("VA", scaled[v], EYE, None, v)
+    ts(S("IS", 68, 69), pc, 16, ALU.bitwise_and)
     ts(S("IS", 74, 75), pc, 4, ALU.arith_shift_right)
-    cp("V", col(8), S("IS", 68, 69))
-    cp("V", col(9), S("IS", 70, 71))
-    ts(col(10), S("IS", 72, 73), 2048.0, ALU.add)
+    ts(col(9), S("IS", 68, 69), 0, ALU.is_equal)
+    ts(col(10), S("IS", 68, 69), 16, ALU.is_equal)
     cp("V", col(11), S("IS", 74, 75))
-    ki = S("IS", 128, 192)
+    SWAP = [pm(11 + k) for k in range(4)]
+    for k, (m, c) in enumerate(((EYE, 9), (UP, 9), (DOWN, 10), (EYE, 10))):
+        cp("VA", SWAP[k], m, None, col(c))
+    ki = S("IS", 192, 256)
     iota(ki, [[1, 64]], 0, 0)
-    ts(st(JJ, 64), ki, 16.0, ALU.mult, col(8), ALU.add)
-    ts(OJS, ki, 32.0, ALU.mult, col(9), ALU.add)
+    ts(JJ, ki, 16.0, ALU.mult, col(8), ALU.add)
+    ts(sub(JC, 0, 64), JJ, GC - LTF - 8192.0, ALU.add)
+    ts(sub(JC, 64, 64), JJ, GC + 1024 - LTB - 8192.0, ALU.add)
     mset(S("BC", 0, 144), 0.0)
     ts(S("BC", 16, 144, 16), sub(ki, 0, 8), col(11), ALU.is_equal)
-    mset(S("LL", 0, 128), 1.0)
     for j in range(4):
-        cp("A", S("LL", 128 << j, 256 << j), S("LL", 0, 128 << j))
-    ops[sx]["soft"].append(asel(S("LL", 0, 2048), [[-1, 16], [-16, 8], [0, 16]], 0, 1))
-    cp("A", S("BA", 0, 1440), S("LL", 0, 1440), None, None, 0.0, 1.0)
-    ops[asel(S("BA", 0, 1440), [[-1, 10], [-16, 9], [1000, 16]], 16, 1)]["soft"].append(s2)
-    for row in (0, 3):
-        cp("A", S("BA", 144 * row, 144 * row + 144), S("BA", 144 * row, 144 * row + 144), None, None, BIG)
-    mset(S("VAL", 2048, 2056), 0.0)
-    mset(S("COL", 16, 32), ROOT)
-    cp("A", S("VAL", 2048, 2049), col(16), None, None, ROOT)
-    cp("A", S("VAL", 2049, 2050), col(16), None, None, -ROOT)
-    for a in (0, 4112):
-        cp("A", S("XF", a, a + 16), S("COL", 16, 32), None, None, ROOT)
-        cp("A", S("XB", a, a + 16), S("COL", 16, 32), None, None, -ROOT)
-    m1, m2, m3 = S("IS", 192, 256), S("IS", 256, 320), S("IS", 320, 384)
+        asel(S("LL", 512 * j, 512 * j + 512), [[-1, 4], [-16, 8], [0, 16]], -4 * j, 1, ones(512))
+    asel(S("BA", 0, 144), [[-16, 9], [1000, 16]], 16, 1)
+    asel(S("BA", 144, 720), [[-1, 4], [-16, 9], [1000, 16]], 4, 1)
+    mset(ONE, 1024.0)
+    mset(S("COL", 16, 24), ROOT)
+    for j, v in enumerate((-8.0, -64.0, 16.0)):
+        cp("VA", col(12 + j), col(16), None, v * ROOT)
+    for a in (0, 8, 4112, 4120):
+        cp("VA", S("XF", a, a + 8), S("COL", 16, 24), None, ROOT)
+        cp("VA", S("XB", a, a + 8), S("COL", 16, 24), None, -ROOT)
+    for a in (LTB, LTF):
+        mset(gb(a + 1024, 16), 0.0)
+    m1, m2, m3 = S("IS", 256, 320), S("IS", 320, 384), S("IS", 384, 448)
     ts(m1, MSI, 63, ALU.bitwise_and)
     ts(m2, MSI, 6, ALU.arith_shift_right)
-    ts(st(H, 64), m1, 4.0, ALU.mult)
-    ts(st(H + 64, 64), m2, 4.0, ALU.mult)
-    ts(m2, m2, 64.0, ALU.mult)
+    ts(sub(H, 0, 128), S("IS", 256, 384), 4.0, ALU.mult)
+    ts(m2, MSI, 4032, ALU.bitwise_and)
     for r, d in ((0, 1.0), (2, 63.0)):
         ts(m3, m1, d, ALU.add)
         ts(m3, m3, 63, ALU.bitwise_and)
@@ -390,269 +436,294 @@ def build(g, core, T, topo, rank):
     ts(m3, MSI, 64.0, ALU.add)
     ts(m3, m3, 4095, ALU.bitwise_and)
     cp("V", sub(ONB, 64, 64), m3)
-    mset(st(MISS, 64), 1.0)
-    mset(st(THR, 64), 9.0)
 
-    def turn(ba, src, rhs, qoff, ev, out, ok=None):
-        nq = width(rhs) // 8
-        mm([(PS(ba, s, nq * 128, 16, 64), (src[0], src[1] + s, src[2], 16) + src[4:], rhs, True, True) for s in range(16)])
-        cp(ev, S("Q", qoff, qoff + nq * 128, 1, 0, 64), PS(ba, 0, nq * 128, 1, 64))
-        back = [(sub(out, 64 * j, 64), S("Q", qoff + 128 * j, qoff + 128 * j + 128, 1, 0, 64)) for j in range(nq)]
-        if ok:
-            mm([it for (o, x) in back for it in ((o, x, S("IDN", 0, 64, 1, 0, 64), True, False), (o, S("PM", 128, 256), ok, False, True))], 0.09)
-        else:
-            tr(back)
+    def turn(bank, src, rhs, qoff, b=0.0, func=None):
+        nq, m = width(rhs) // 8, width(src) // 16
+        mm([(part(PS(bank, s, nq * 128, 16), 0, m), sub(src, s, m, 16), rhs) for s in range(16)])
+        cp("VA", S("Q", qoff, qoff + nq * 128, 1, 0, m), part(PS(bank, 0, nq * 128), 0, m), None, 1.0, b, func)
 
-    def pick(out, row, src, first=True, last=True):
-        mm([(out, S("BA", row * 144 + 16 - s, row * 144 + 144 - s), (src[0], src[1] + s, src[2], 16) + src[4:],
-             first and s == 0, last and s == 15) for s in range(16)])
+    QS = S("INV", 3072, 3584)
 
-    def place_of(eng, pos, w, var, bank, out):
-        qb = sub(QB, 128 * w, 128)
-        axb(eng, qb, pos, 0.25, 191.625)
-        mm([(bank, S("PM", 384 * k + 128 * var, 384 * k + 128 * var + 128), sub(qb, 64 * k, 64), k == 0, k == 1) for k in range(2)])
+    def small(bank, src, rhs):
+        nq, m = width(rhs) // 8, width(src) // 16
+        mm([(part(PS(bank, s, nq * 128, 16), 0, m), sub(src, s, m, 16), rhs) for s in range(16)])
+        cp("VA", part(sub(QS, 0, nq * 128), 0, m), part(PS(bank, 0, nq * 128), 0, m))
+
+    def back(out, qoff, j, w, m=128):
+        return (out, S("Q", qoff + 128 * j, qoff + 128 * j + 128, 1, 0, m), part(sub(ID, 64 * w, 64), 0, m))
+
+    def pick(out, k, src):
+        return [(out, S("BA", k * 144 + 16 - s, k * 144 + 144 - s), sub(src, s, 64, 16)) for s in range(16)]
+
+    def spread(bank, lst):
+        return [(PS(bank, s, 512, 16), S("LL", 128 * s, 128 * s + 128), lst) for s in range(16)]
+
+    def opened(bank):
+        mm([(PS(bank), S("LL", 0, 128), S("LL", 0, 512))], True, False)
+
+    def place_of(pos, qb, var, bank, out):
+        cp("VA", qb, pos, None, 0.25, 191.625)
+        mm([(sub(bank, 64 * w, 64), moved(k, var), sub(qb, 128 * w + 64 * k, 64)) for w in range(width(out) // 64) for k in range(2)])
         ts(out, bank, -12480.0, ALU.add)
 
-    def own(off, gcol, out, sp, ba, bb):
-        cp("A", gcol, S("AR", 0, 4096), off, after=rest + rows)
-        turn(ba, gcol, RO, 0, "A", PS(bb, 0, 256))
-        if sp:
-            turn(ba, gcol, sub(RS, 32, 8), 512, "A", PS(bb, 256, 320))
-            ts(sp, PS(bb, 256, 320), col(10), ALU.add, 2048.0, ALU.min)
-            ts(st(NOTL, 64), PS(bb, 256, 320), 0.0, ALU.is_ge)
-            for j in range(4):
-                tt(st(out + 64 * j, 64), PS(bb, 64 * j, 64 * j + 64), st(NOTL, 64), ALU.mult)
+    def visit1(r, flows):
+        p1 = P1[r % 2]
+        mm([(PS(X2, 128 * w, 128 * w + 128), EYE, H) for w in range(2)] + [(PS(X2, 64 * j, 64 * j + 64), EYE, sub(flows, j, 64, 4)) for j in range(4)])
+        ts(p1, PS(X2, 0, 256), 0.0, ALU.max, 255.0, ALU.min)
+        place_of(p1, sub(QB, 0, 256), 1, PS(X2, 256, 384), OC1)
+        for w in (1, 0):
+            cp("A" if r else "AV"[w], gb(GC + 1024 * w), S(("PTf", "PTb")[w], 0, 4096), sub(OC1, 64 * w, 64))
+        both = gb(GC, 2048)
+        if r:
+            turn(X0, both, RT[1], 0, 1024.0)
+            turn(X1, both, RC, 512, 1024.0)
+            mm([back(PS(X1, 128 + 64 * w, 192 + 64 * w), 512, 0, w) for w in range(2)])
+            tt(PS(X1, 128, 256), PS(X1, 128, 256), JC, ALU.min)
+            ts(OSP, PS(X1, 128, 256), 8192.0, ALU.add)
         else:
-            cp("A", st(out, 256), PS(bb, 0, 256))
-
-    def fetch1(ch, w, bb, eng):
-        p1 = st(P1 + 128 * w, 128)
-        tt(p1, st(H, 128), st(ch + 128 * w, 128), ALU.add)
-        ts(p1, p1, 0.0, ALU.max, 255.0, ALU.min)
-        place_of(eng, p1, w, 1, PS(bb, 0, 64), sub(OC1, 64 * w, 64))
-        cp(eng, S("AR", 5120 + 1024 * w, 6144 + 1024 * w), S(("PTf", "PTb")[w], 0, 4096), sub(OC1, 64 * w, 64))
-
-    def visit1(r, w, ba, bb, eng):
-        p1, gc, t1 = st(P1 + 128 * w, 128), S("AR", 5120 + 1024 * w, 6144 + 1024 * w), st(T1A + 256 * w, 256)
-        turn(ba, gc, RC[w], 512, eng, PS(bb, 0, 192))
+            turn(X0, both, RT[1], 0, 16.0, AF.Relu)
+            turn(X1, both, RH, 512, 0.0, AF.Relu)
+        mm([back(PS(X0, 256 * w + 64 * i, 256 * w + 64 * i + 64), 0, i, w) for w in range(2) for i in range(4)])
+        cp("VA", T1A, PS(X0), None, 1.0, 0.0 if r else -4112.0)
         if r:
-            ts(sub(OSP, 64 * w, 64), PS(bb, 0, 64), col(10), ALU.add, 2048.0, ALU.min)
-            ts(st(NOTL, 64), PS(bb, 0, 64), 0.0, ALU.is_ge)
-            for k in (1, 2):
-                tt(PS(bb, 64 * k, 64 * k + 64), PS(bb, 64 * k, 64 * k + 64), st(NOTL, 64), ALU.mult)
-        tt(st(B2 + 128 * w, 128), PS(bb, 64, 192), p1, ALU.add)
-        turn(ba, gc, sub(RT, 56, 32), 0, "A", PS(bb, 256, 512))
+            ts(OFS, PS(X0), 1024.0, ALU.min)
+
+    def visit2(r, w, t0):
+        bp, ba, bt, cnt, br, by = ((PS(X0, 0, 192), X1, PS(X0, 256, 512), PS(X2, 0, 64), PS(X1, 0, 384), PS(X2, 128, 384)),
+                                   (PS(U0, 0, 192), U1, PS(T0, 0, 256), PS(T1, 0, 64), PS(U0, 0, 384), PS(T0, 256, 512)))[w]
+        p1, p2, rr = sub(P1[r % 2], 128 * w, 128), sub(P2, 128 * w, 128), sub(RR, 384 * w, 384)
+        lt = (LTF, LTB)[w]
+        o = gb(GC + 1024 * w)
+        reads = []
         if r:
-            axb("A", t1, PS(bb, 256, 512), 1.0, -5120.0)
-            turn(ba, gc, sub(RS, 0, 32), 0, "A", PS(bb, 0, 256))
-            ts(sub(OFS, 256 * w, 256), PS(bb, 0, 256), col(10), ALU.add, 2048.0, ALU.min)
+            o = S("INV", 1024 * w, 1024 * w + 1024)
+            at(t0 + 1.5 * (1 - w))
+            reads.append(cp("V", o, S("GB", lt, GC + 1024 * w + 1024), sub(OSP, 64 * w, 64)))
+        at(t0 + (8, 1)[w])
+        if w or not r:
+            mm([(sub(bp, 0, 128), EYE, p1)] + pick(sub(bp, 0, 64), 1 + 2 * w, o) + pick(sub(bp, 64, 64), 2 + 2 * w, o))
         else:
-            cp("A", t1, PS(bb, 256, 512), None, AF.Relu, 1.0, 16.0)
-            tt(st(TM, 128), sub(t1, 0, 128), sub(t1, 128, 128), ALU.min)
-            tt(st(TM, 64), st(TM, 64), st(TM + 64, 64), ALU.min)
-            ts(st(CNT + 64 * w, 64), st(TM, 64), 16.0, ALU.is_lt, BIG, ALU.mult)
-            axb("A", t1, t1, 1.0, -4112.0)
-
-    LT, LI = S("INV", 0, 2080), 2080
-
-    def slot(eng, row, src):
-        for d in (0, 16):
-            cp(eng, S("INV", LI + row + d, LI + 2048, 32), src)
-
-    def lanes_table():
-        add("V", cost(0.5, 2048), lambda: g.vector.transpose(T.INV[:, 0:2048], T.INV[:, LI:LI + 2048]),
-            [S("INV", LI, LI + 2048)], [S("INV", 0, 2048)])
-
-    def visit2(r, w):
-        eng = "VA"[w]
-        bd, bc, ba, bt, cnt = ((PS(U1, 0, 128), PS(U1, 128, 192), U0, PS(TA, 0, 256), PS(VF1, 0, 64)),
-                               (PS(X0, 0, 128), PS(X0, 128, 192), X1, PS(X0, 256, 512), PS(VB, 0, 64)))[w]
-        p1, p2 = st(P1 + 128 * w, 128), st(B2 + 128 * w, 128)
+            small(X0, o, sub(RO, 0, 16))
+            mm([(sub(bp, 0, 128), EYE, p1)] + [(sub(bp, 64 * j, 64), part(sub(QS, 128 * j, 128), 0, 64), part(sub(EYE, 0, 64), 0, 64)) for j in range(2)])
+        ts(p2, sub(bp, 0, 128), 0.0, ALU.max, 255.0, ALU.min)
+        place_of(p2, sub(QB, 256 + 128 * w, 128), 2 * w, sub(bp, 128, 64), sub(OC2, 64 * w, 64))
+        g2 = S("XB", 1024 * w, 1024 * w + 1024) if r else gb((LE, LTO)[w])
+        cp("AV"[w], g2, S("PT2", 0, 4096), sub(OC2, 64 * w, 64))
         if r:
-            o = S("AR", 1024 * w, 1024 * w + 1024)
-            cp(eng, o, LT, sub(OSP, 64 * w, 64))
-            for k in range(2):
-                pick(sub(bd, 64 * k, 64), 1 + 3 * w + k, o)
-            tt(bd, bd, p2, ALU.add)
-        ts(bd, bd if r else p2, 0.0, ALU.max, 255.0, ALU.min)
-        place_of(eng, bd, w, 2 * w, bc, sub(OC2, 64 * w, 64))
-        g2 = S("AR", 2048 + 1024 * w, 3072 + 1024 * w) if r else S("INV", 1024 * w, 1024 * w + 1024)
-        cp(eng, g2, S("PT2", 0, 4096), sub(OC2, 64 * w, 64))
-        tt(bd, bd, p1, ALU.subtract)
-        mm_, gg, ic, ia = st(MM + 64 * w, 64), st(GG + 64 * w, 64), sub(IC, 128 * w, 128), sub(IA, 128 * w, 128)
-        if r == 0:
-            turn(ba, g2, sub(RT, 112 - 112 * w, 32), 0, "A", bt)
-            cp("A", bt, bt, None, AF.Relu, 1.0, 16.0)
-            cnt = st(CNT + 64 * w, 64)
             for i in range(4):
-                tt(st(TM + 64 * i, 64), cnt, st(T1A + 256 * w + 64 * i, 64), ALU.add)
+                o = S("XF", 4096 * w + 1024 * i, 4096 * w + 1024 * i + 1024)
+                at(t0 + ((5, 9, 11, 13), (0, 1.5, 3, 4.5))[w][i])
+                reads.append(cp("A" if w or i else "V", o, gb(lt, 1040), sub(OFS, 256 * w + 64 * i, 64)))
+                if w:
+                    mm(pick(cnt, 0, o), i == 0, i == 3)
+                elif i % 2:
+                    mm([(PS(X2, s, 128, 16), S("XF", 1024 * i - 1024 + s, 1024 * i + 1024, 16), RF) for s in range(16)], i == 1, i == 3)
+            if w == 0:
+                cp("VA", S("INV", 3584, 3712), PS(X2, 0, 128))
+                mm([(cnt, S("INV", 3584, 3712), TWO)])
+            at(t0 + (12, 4)[w])
+            turn(ba, g2, RT[2 - 2 * w], 512, 6144.0)
         else:
-            for i in range(4):
-                o = S(("XF", "XB")[w], 1024 * i, 1024 * i + 1024)
-                cp("A", o, LT, sub(OFS, 256 * w + 64 * i, 64))
-                pick(cnt, 3 * w, o, i == 0, i == 3)
-            ok = sub(QB, 128 * w, 64)
-            ts(ok, cnt, 0.0, ALU.is_equal, -BIG, ALU.mult)
-            turn(ba, g2, sub(RT, 112 - 112 * w, 32), 0, eng, bt, ok)
-        ts(mm_, cnt, 0.0, ALU.is_gt)
-        ts(gg, cnt, 0.0, ALU.is_equal, 1.0, ALU.add)
-        for k in range(2):
-            tt(sub(bd, 64 * k, 64), sub(bd, 64 * k, 64), mm_, ALU.mult)
-        tt(ic, bd, p1, ALU.add)
-        ts(ia, ic, 3, ALU.bitwise_and)
-        ts(sub(UV, 128 * w, 128), ia, 0.25, ALU.mult, TINY, ALU.max)
-        if r:
-            tt(bt, bt, st(T1A + 256 * w, 256), ALU.max)
-        else:
-            tt(bt, bt, st(TM, 256), ALU.min)
-        ts(sub(OFT, 256 * w, 256), bt, 6144.0 if r else 4112.0, ALU.add)
-        tt(bd, ic, st(H, 128), ALU.subtract)
-        for k in range(2):
-            tt(sub(ia, 64 * k, 64), sub(bd, 64 * k, 64), gg, ALU.mult)
-        ts(ia, ia, 1, ALU.arith_shift_right)
+            mm([back(cnt, 512, i, w) for i in range(4)])
+            turn(ba, g2, RT[2 - 2 * w], (512, 0)[w], 16.0, AF.Relu)
+        cp("A", OK, cnt, None, -1024.0, 1024.0, AF.Relu)
+        mm([it for i in range(4) for it in (back(sub(bt, 64 * i, 64), 512 if r or not w else 0, i, 0, 64), (sub(bt, 64 * i, 64), scaled[-16.0], OK))])
+        tt(bt, bt, sub(T1A, 256 * w, 256), ALU.max)
+        ts(sub(OFT, 256 * w, 256), bt, 0.0 if r else 4112.0, ALU.add)
+        mm([(sub(br, 128 * j, 128), EYE, x) for j, x in enumerate((p1, p2, H))]
+           + [(sub(br, 64 * j, 64), scaled[-1.0 if j // 2 == 1 else 1.0], OK) for j in range(6)]
+           + [(sub(br, 128 + 64 * j, 64), EYE, ONE) for j in range(2)])
+        cp("VA", rr, br, None, 1.0, -1024.0, AF.Relu)
+        qe = sub(QB, 512, 128)
+        mm([(sub(by, 0, 128), EYE, sub(rr, 128 * j, 128)) for j in range(2)])
+        cp("VA", qe, sub(by, 0, 128), None, 0.25, 191.625)
+        mm([(sub(by, 128, 128), scaled[0.25], sub(rr, 128 * j, 128)) for j in range(2)] + [(sub(by, 128, 128), scaled[-1.0], qe)]
+           + [(sub(by, 128 + 64 * j, 64), scaled[0.1875], ONE) for j in range(2)])
+        cp("VA", sub(UV, 128 * w, 128), sub(by, 128, 128), None, 1.0, TINY)
+        if w == 0 and (r, 0) in HALVED:
+            v = sub(UV, 64, 64 if (r, 1) in HALVED else 32)
+            cp("VA", v, v, None, 0.5)
+        return reads
 
-    own(OMS, S("AR", 4096, 5120), FL, None, U0, U1)
-    fetch1(FL, 0, U1, "V")
-    fetch1(FL, 1, X0, "A")
-    visit1(0, 0, U0, U1, "V")
-    visit1(0, 1, X1, X0, "A")
-    nch = 0
+    def lanes_table(bank, hf, flag):
+        items = []
+        for row, x in [(0, sub(flag, 32 * hf, 32))] + [(12 + j, sub(MSG, 128 * hf + j, 32, 4)) for j in range(4)]:
+            for k in range(4):
+                items.append((PS(bank, row + 16 * (k // 2), 512, 32), SWAP[k], sub(x, (k % 2) * x[3], 16, 2 * x[3])))
+        mm(items)
+
+    own = S("INV", 2048, 4096)
+    at(23)
+    cp("V", sub(own, 0, 1024), S("AR", 0, 4096), OMS)
+    cp("A", sub(own, 1024, 1024), S("AR", 0, 4096), sub(ONB, 0, 64))
+    turn(X1, own, RO, 0)
+    mm([back(PS(X1, 256 * w + j, 256 * w + 256, 4), 0, j, w) for w in range(2) for j in range(4)])
+    cp("VA", sb(2560, 512), PS(X1))
+    visit1(0, FL)
+    nch, casts = 0, []
+    VN, VP = S("VAL", 1024, 2048), S("VAL", 2048, 3072)
     for r in range(3):
-        if r:
-            lanes_table()
-        visit2(r, 0)
+        t0 = START[r]
+        visit2(r, 1, t0)
         if r == 0:
-            dma("G", [(lambda: T.xf[:], lambda: T.x[:])], 2048, [], [S("xf", 0, 4096)], aPT)
-            sw = send([(helper_of(T, topo, rank), S("xf", 0, 4096), S("xg", 0, 4096, 1, 16, 144), "aWh")], 2048)
-            for t in "FB":
+            for t in "BF":
                 for k in range(2):
-                    arrive("aW%s%d" % (t, k), half, S("W" + t, 5120 * k + 1024, 5120 * k + 5120), sw, 22 + 20 * k)
-            own(sub(ONB, 0, 64), S("AR", 4096, 5120), FLO, None, VB, VF1)
+                    wide = lambda a, b: (S("W" + t, 5120 * k + 1024 + 1024 * a, 5120 * k + 1024 + 1024 * b), S("X" + t, 4112 * k + 16 + 1024 * a, 4112 * k + 16 + 1024 * b))
+                    if BY_DMA[t][k]:
+                        sw = sdma("G", [wide(0, BY_DMA[t][k])], 512 * BY_DMA[t][k])
+                        ops[sw]["soft"].append(s2)
+                        s2 = sw
+                    for j in range(BY_DMA[t][k], 4):
+                        at(t0 + 26 + j + 4 * k)
+                        casts.append(cp("VA", *wide(j, j + 1)))
         else:
-            o = S("AR", 4096, 5120)
-            cp("A", o, LT, sub(ONS, 64 * (r - 1), 64))
-            for j in range(4):
-                pick(PS(X1, 64 * j, 64 * j + 64), 6 + j, o)
-            nbp = PS(X1, 0, 256)
-            tt(nbp, nbp, st(NB[r], 256), ALU.add)
-            tt(nbp, nbp, st(FL, 256), ALU.subtract)
-            for j in range(4):
-                tt(sub(nbp, 64 * j, 64), sub(nbp, 64 * j, 64), st(MISS, 64), ALU.mult)
-            tt(st(FLO, 256), nbp, st(FL, 256), ALU.add)
+            at(t0 - 2)
+            tt(TM, sub(DN, 64 * (r - 1), 64), MISS[r - 1], ALU.mult)
+            tt(TM, TM, JJ, ALU.add)
+            cp("V", ONS, TM)
+            o = S("INV", 2048, 3072)
+            cp("A", o, gb(LTO, 3072), ONS)
+            small(X1, o, RO)
+            mm([(PS(X1, j, 256, 4), part(sub(QS, 128 * j, 128), 0, 64), part(sub(EYE, 0, 64), 0, 64)) for j in range(4)])
+            cp("VA", FLO, PS(X1, 0, 256))
+        flags = visit2(r, 0, t0 - (0 if r else 5))
+        at(t0 + 20)
+        mm([(PS(X1, j, 256, 4), scaled[v], sub(RR, 384 * (j // 2) + 128 * k + 64 * (j % 2), 64)) for j in range(4) for k, v in enumerate((1.0, 0.5, -0.5))]
+           + [(PS(X1, j, 256, 4), scaled[-0.5], sub(H, 64 * (j % 2), 64)) for j in range(4)] + [(PS(X1, 0, 256), scaled[-1.0], FLO)])
+        ts(AA, PS(X1, 0, 256), -0.25, ALU.add)
+        at(t0 + (21 if r else 14))
         if r < 2:
-            fetch1(FLO, 0, VB, "A")
-        visit2(r, 1)
-        if r < 2:
-            fetch1(FLO, 1, X1, "A")
-        for w in range(2):
-            tt(st(AA + 128 * w, 128), sub(IA, 128 * w, 128), st(FLO + 128 * w, 128), ALU.subtract)
-        cnone = (1024.0, 2048.0, 1026.0)[r]
-        axb("A", st(JC, 64), st(JJ, 64), 1.0, (0.0, 1024.0, 0.0)[r] - cnone)
+            visit1(r + 1, FLO)
         if r == 0:
-            mset(st(BASE, 64), cnone)
-        else:
-            axb("A", st(BASE, 64), st(JJ, 64), -1.0, cnone - (0.0, 0.0, 1032.0)[r])
-            tt(st(BASE, 64), st(BASE, 64), st(MISS, 64), ALU.mult)
-            tt(st(BASE, 64), st(BASE, 64), st(JJ, 64), ALU.add)
+            for k in range(2):
+                cp("A", gb(GNB + 1024 * k), S("AR", 0, 4096), sub(ONB, 64 + 64 * k, 64))
+            turn(X1, gb(GNB, 2048), RC, 512, 1024.0)
+            mm([it for k in range(2) for it in (back(PS(X1, 128 + 64 * k, 192 + 64 * k), 512, 0, k), (PS(X1, 128 + 64 * k, 192 + 64 * k), LESS, JJ),
+                                                 (PS(X1, 128 + 64 * k, 192 + 64 * k), LESS, JJ))])
+            for k in range(2):
+                ts(sub(DN, 64 * k, 64), PS(X1, 128 + 64 * k, 192 + 64 * k), 1024.0 * k - 7168.0, ALU.min, 8192.0, ALU.add)
         if r == 2:
-            axb("A", st(BASE, 64), st(BASE, 64), 1.0, 1032.0)
-        if r < 2:
-            visit1(r + 1, 0, X1, X0, "A")
-            visit1(r + 1, 1, X1, X0, "A")
-        if r == 0:
-            own(sub(ONB, 64, 64), S("INV", 0, 1024), NB[1], sub(ONS, 0, 64), X1, X0)
-            own(sub(ONB, 128, 64), S("INV", 1024, 2048), NB[2], sub(ONS, 64, 64), X1, X0)
-            mset(S("INV", 2048, 4128), 0.0)
-        for w in range(2):
+            mm([(PS(X1, 0, 64), ID, JJ)] + [(PS(X1, 0, 64), scaled[512.0], MISS[k]) for k in range(2)])
+            for hf in range(2):
+                ts(sub(OGI, 32 * hf, 32), PS(X1, 32 * hf, 32 * hf + 32), -512.0 * hf, ALU.add)
+            cp("VA", VP, VN, None, 1.0, 0.0, AF.Relu)
+        taps = {}
+        for w in (1, 0):
             for hf in range(2):
                 win = S(("XF", "XB")[w], 0, 8224) if r == 0 else S(("WF", "WB")[w], 0, 10240)
                 off = lambda i: sub(OFT, 256 * w + 64 * i + 32 * hf, 32)
-                ub, vb = (U0, U1)[hf], ((VF0, VF1)[hf], VB)[w]
+                ub, tb = (U0, U1)[hf], (T0, T1)[hf]
                 a0, a2 = [S("WK", 1024 * hf + 512 * j, 1024 * hf + 512 * j + 512) for j in range(2)]
-                d1, d2 = [S("WK", 2048 + 512 * ((2 * nch + j) % 3), 2560 + 512 * ((2 * nch + j) % 3)) for j in range(2)]
+                s_, e_ = a0, a2
+                if r == 0:
+                    a0, a2 = [S("INV", 1024 * hf + 512 * j, 1024 * hf + 512 * j + 512) for j in range(2)]
+                d1, d2 = [S("WK", 2048 + 512 * ((nch + j) % 2), 2560 + 512 * ((nch + j) % 2)) for j in range(2)]
                 nch += 1
-                for b, k in ((ub, 0), (vb, 1)):
-                    mm([(PS(b, s, 512, 16), S("LL", 128 * s, 128 * s + 128), sub(UV, 128 * w + 64 * k + 32 * hf, 32), True, True)
-                        for s in range(16)])
-                cp("A", a0, win, off(0))
+                at(t0 + (7 if r else 5) + 5 * (2 * (1 - w) + hf))
+                mm(spread(ub, sub(UV, 128 * w + 32 * hf, 32)))
+                if (r, w, hf) in ADDED:
+                    opened(tb)
                 cp("A", a2, win, off(2))
-                tt(d1, win, a0, ALU.subtract, off(1))
-                tt(d2, win, a2, ALU.subtract, off(3))
-                tt(PS(TA), PS(ub), d1, ALU.mult)
-                tt(PS(ub), PS(ub), d2, ALU.mult)
-                tt(a0, PS(TA), a0, ALU.add)
-                tt(PS(ub), PS(ub), a2, ALU.add)
-                tt(d2, PS(ub), a0, ALU.subtract)
-                tt(PS(vb), PS(vb), d2, ALU.mult)
-                zb = S("VAL", 1024 + 512 * hf, 1536 + 512 * hf)
-                tt(zb if w else PS(vb), PS(vb), a0, ALU.add)
+                cp("A", a0, win, off(0))
+                taps[w, hf] = [tt(d2, win, a2, ALU.subtract, off(3)), tt(d1, win, a0, ALU.subtract, off(1))]
+                if (r, w, hf) == (0, 0, 0):
+                    for j in casts:
+                        ops[j]["soft"].append(taps[w, hf][0])
+                if r == 1 and hf == 1:
+                    if w:
+                        sg = send([(lo, None, None, "sB"), (hi, None, None, "sL")], 0, taps[1, 0] + taps[1, 1] + flags)
+                        free = {t: arrive("s" + t, 1, None, sg) for t in "BL"}
+                    else:
+                        free["F"] = send([(helper(1), None, None, "hF"), (helper(2), None, None, "hF")], 0, taps[0, 0] + taps[0, 1])
+                tt(PS(tb), PS(ub), d2, ALU.mult)
+                if (r, w, hf) in ADDED:
+                    mm([(PS(tb), ID if r else EYE, a2)], False, True)
+                else:
+                    tt(PS(tb), PS(tb), a2, ALU.add)
+                tt(PS(ub), PS(ub), d1, ALU.mult)
+                tt(s_, PS(ub), a0, ALU.add)
+                mm(spread(ub, sub(UV, 128 * w + 64 + 32 * hf, 32)))
+                tt(e_, PS(tb), s_, ALU.subtract)
+                zb = S("VAL", 512 * hf, 512 * hf + 512)
                 if w:
-                    vf = PS((VF0, VF1)[hf])
-                    gp = S("GAP", 1024 * r + 512 * hf, 1024 * r + 512 * hf + 512)
-                    le = S("AR", 7168 + 512 * hf, 7680 + 512 * hf)
-                    tt(vf, vf, zb, ALU.subtract)
-                    cp("A", gp, vf, None, AF.Abs)
-                    cp("A", vf, vf, None, AF.Copy, 0.5)
-                    ts(le, gp, S("EPS", 0, 1), ALU.is_le)
-                    tt(zb, vf, zb, ALU.add)
-                    mm([(PS(ub, 0, 32), S("BC", 16 - s, 144 - s), (le[0], le[1] + s, le[2], 16) + le[4:], s == 0, s == 15) for s in range(16)])
-                    tt(st(WON + 32 * hf, 32), PS(ub, 0, 32), st(THR + 32 * hf, 32), ALU.is_ge)
-        won = st(WON, 64)
-        ms_ = S("MSG", 320 * (r % 2), 320 * (r % 2) + 320)
-        place = (0, 64, 192, 256)
-        for j in range(4):
-            tt(st(AA + 64 * j, 64), st(AA + 64 * j, 64), won, ALU.mult)
-        for w in range(2):
-            tt(sub(ms_, 192 * w, 128), st(AA + 128 * w, 128), st(FLO + 128 * w, 128), ALU.add)
-        tt(sub(ms_, 128, 64), st(MISS, 64), won, ALU.subtract)
+                    tt(PS(ub), PS(ub), e_, ALU.mult)
+                    tt(zb, PS(ub), s_, ALU.add)
+                    continue
+                gp = S("GAP", 1536 * hf + 512 * r, 1536 * hf + 512 * r + 512)
+                le = gb(LE + 512 * hf, 512)
+                if (r, hf) not in HALVED:
+                    tt(PS(ub), PS(ub), e_, ALU.mult)
+                    tt(PS(ub), PS(ub), s_, ALU.add)
+                    tt(PS(ub), PS(ub), zb, ALU.subtract)
+                    opened(tb)
+                    cp("A", gp, PS(ub), None, 1.0, 0.0, AF.Abs)
+                    cp("A", PS(tb), PS(ub), None, 0.5)
+                    mm([(PS(tb), ID, zb)], False, False)
+                else:
+                    opened(VB)
+                    tt(PS(VB), PS(ub), e_, ALU.mult)
+                    mm([(PS(VB), HALF, s_), (PS(VB), LESS, zb)], False, True)
+                    opened(tb)
+                    cp("A", gp, PS(VB), None, 2.0, 0.0, AF.Abs)
+                    tt(PS(tb), PS(VB), zb, ALU.add)
+                at(t0 + (7 if r else 5) + 5 * (2 + hf) + 4)
+                ts(le, gp, S("EPS", 0, 1), ALU.is_le)
+                won, pen = sub(WON, 32 * hf, 32), sub(PEN, 32 * hf, 32)
+                thr = 73.0 if r else 9.0
+                mm([(PS(ub, 0, 32), S("BC", 16 - s, 144 - s), sub(le, s, 32, 16)) for s in range(16)]
+                   + ([(PS(ub, 0, 32), scaled[64.0], sub(MISS[r - 1], 32 * hf, 32))] if r else []))
+                ts(won, PS(ub, 0, 32), thr, ALU.is_ge)
+                ts(pen, PS(ub, 0, 32), thr, ALU.is_lt, col(13 if r else 12), ALU.mult)
+                mm([(PS(ub, 128 + j, 256, 4), EYE, won) for j in range(4)])
+                mm(spread(tb, pen), False, True)
+                tt(PS(ub, 128, 256), PS(ub, 128, 256), sub(AA, 128 * hf, 128), ALU.mult)
+                tt(sub(MSG, 128 * hf, 128), PS(ub, 128, 256), sub(FLO, 128 * hf, 128), ALU.add)
+                flag = MISS[r] if r < 2 else PEN
+                if r == 0:
+                    cp("VA", sub(flag, 32 * hf, 32), won, None, -1.0, 1.0)
+                elif r == 1:
+                    tt(sub(flag, 32 * hf, 32), sub(MISS[0], 32 * hf, 32), won, ALU.subtract)
+                else:
+                    tt(won, won, sub(MISS[1], 32 * hf, 32), ALU.subtract)
+                    cp("VA", sub(flag, 32 * hf, 32), won, None, 1.0, 1.0)
+                lanes_table(ub, hf, flag)
+                vn = sub(VN, 512 * hf, 512)
+                if r < 2:
+                    cp("VA", le, PS(ub))
+                    flip(gb(LTO + 512 * hf, 512), le)
+                    src = gb(LTO + 512 * hf, 512)
+                    s0 = send([(hi, src, gb(LTB + 512 * hf, 512), "aLb%d%d" % (r, hf)), (lo, src, gb(LTF + 512 * hf, 512), "aLf%d%d" % (r, hf))],
+                              256, [free["B"], free["L"]] if r else [])
+                    arrive("aLb%d%d" % (r, hf), half, gb(LTB + 512 * hf, 512), s0)
+                    arrive("aLf%d%d" % (r, hf), half, gb(LTF + 512 * hf, 512), s0)
+                    at(t0 + 30 + hf)
+                    if r:
+                        tt(vn, PS(tb), vn, ALU.max)
+                    else:
+                        cp("VA", vn, PS(tb))
+                    c0, slot = 512 * hf, D3("vn", 2 * r + hf)
+                    s1 = send([(far, vn, slot, "aVn%d%d" % (r, hf)), (hi, vn, S("WB", c0, c0 + 512), "aVb%d%d" % (r, hf))], 512, [free["B"]] if r else [])
+                    ops[s1]["soft"].append(s0)
+                    arrive("aVb%d%d" % (r, hf), half, S("WB", c0, c0 + 512), s1)
+                    arrive("aVn%d%d" % (r, hf), half, slot, s1)
+                    s1 = sdma("S", [(S("WB", 5120 + c0, 5632 + c0, 1, 16, 128), part(slot, 0, 112)), (S("WB", 5120 + c0, 5632 + c0, 1, 0, 16), part(slot, 112, 128))], 256)
+                else:
+                    c0 = 512 * hf
+                    y = sub(VP, c0, 512)
+                    tt(y, PS(tb), y, ALU.max)
+                    dma("S", [(lambda c0=c0: T.y[:, c0:c0 + 512], lambda y=y: ap(y))], 256, [y], [])
+                    ts(s_, S("GAP", 1536 * hf, 1536 * hf + 1536), 128.0, ALU.min, None, None, sub(OGI, 32 * hf, 32))
+                    cp("A", s_, s_, None, -1.0, 0.0, AF.Exp)
+                    dma("A", [(lambda c0=c0: T.ye[:, c0:c0 + 512], lambda s_=s_: ap(s_))], 256, [s_], [])
+                    flip(a2, PS(ub))
+                    dma("S", [((lambda k=k, c0=c0: T.yf[8 * k:8 * k + 8, c0:c0 + 512]), (lambda row=row, a2=a2: T.WK[row:128:16, a2[1]:a2[2]]))
+                              for k, row in enumerate((12, 13, 14, 15, 0))], 80, [a2], [])
         if r < 2:
-            lf, lb = S("MF", 192 * r, 192 * r + 192), S("MB", 192 * r, 192 * r + 192)
-            sm = send([(lo, sub(ms_, 0, 192), lf, "aMF%d" % r), (hi, sub(ms_, 128, 192), lb, "aMB%d" % r)], 100)
-            am = [arrive("aMF%d" % r, half, lf, sm), arrive("aMB%d" % r, half, lb, sm)]
-        tt(st(JC, 64), st(JC, 64), won, ALU.mult)
-        tt(st(BASE, 64), st(BASE, 64), st(JC, 64), ALU.add)
-        cp("V", OVP, st(BASE, 64))
-        for j in range(4):
-            slot("A" if j % 2 else "V", 6 + j, sub(ms_, place[j], 64))
-        if r < 2:
-            tt(st(BASE, 64), st(BASE, 64), sub(ms_, 128, 64), ALU.add)
-            cp("V", OVN, st(BASE, 64))
-            win = S("VAL", 1024, 2056) if r == 0 else S("VAL", 0, 2056)
-            vp = S("VAL", 0, 1024) if r == 0 else S("VAL", 2056, 3080)
-            vn = S("WK", 2048, 3072)
-            cp("A", vp, win, OVP)
-            cp("V", vn, win, OVN)
-            s1 = send([(far, vp, D3("vs", 2 * r), "aVp%d" % r), (far, vn, D3("vs", 2 * r + 1), "aVn%d" % r)], 1024)
-            s2 = send([(lo, vp, S("WF", 0, 1024), "aVf%d" % r), (hi, vn, S("WB", 0, 1024), "aVb%d" % r)], 1500, am)
-            arrive("aVf%d" % r, half, S("WF", 0, 1024), s2)
-            arrive("aVb%d" % r, half, S("WB", 0, 1024), s2)
-            arrive("aVp%d" % r, half, D3("vs", 2 * r), s1)
-            arrive("aVn%d" % r, half, D3("vs", 2 * r + 1), s1)
-            sdma("S", [(S("WF", 5120, 6144, 1, 0, 112), D3("vs", 2 * r, 16, 128)), (S("WF", 5120, 6144, 1, 112, 128), D3("vs", 2 * r, 0, 16))], 512)
-            sdma("S", [(S("WB", 5120, 6144, 1, 16, 128), D3("vs", 2 * r + 1, 0, 112)), (S("WB", 5120, 6144, 1, 0, 16), D3("vs", 2 * r + 1, 112, 128))], 512)
-            for row, k in ((1, 0), (2, 1), (0, 2)):
-                slot("V", row, sub(lf, 64 * k, 64))
-            for row, k in ((4, 1), (5, 2), (3, 0)):
-                slot("A", row, sub(lb, 64 * k, 64))
-            for w in range(2):
-                cp("A", st(FL + 128 * w, 128), sub(ms_, 192 * w, 128))
-            cp("A", st(MISS, 64), sub(ms_, 128, 64))
-            axb("A", st(THR, 64), st(MISS, 64), -100.0, 109.0)
-            cp("A", st(GI + 64 * r, 64), st(MISS, 64), None, None, 1024.0)
-            tt(st(GI, 64), st(GI, 64), st((JJ, GI + 64)[r], 64), ALU.add)
-            if r:
-                cp("V", OGI, st(GI, 64))
-    ts(S("WK", 2048, 3072), S("GAP", 0, 3072), 128.0, ALU.min, None, None, OGI)
-    cp("A", S("WK", 2048, 3072), S("WK", 2048, 3072), None, AF.Exp, -1.0)
-    dma("S", [(lambda: T.ye[:], lambda: T.WK[:, 2048:3072])], 512, [S("WK", 2048, 3072)], [])
-    cp("A", S("VAL", 0, 1024), S("VAL", 1024, 3080), OVP)
-    dma("A", [(lambda: T.y[:], lambda: T.VAL[:, 0:1024])], 512, [S("VAL", 0, 1024)], [])
-    axb("V", sub(QB, 0, 64), S("MSG", 128, 192), -1.0, 1.0)
-    slot("V", 0, sub(QB, 0, 64))
-    lanes_table()
-    cp("V", S("WK", 0, 1024), LT, OJS)
-    dma("S", [((lambda k=k: T.yf[8 * k:8 * k + 8, :]), (lambda row=row: T.WK[row:128:16, 0:1024])) for k, row in enumerate((6, 7, 8, 9, 0))],
-        160, [S("WK", 0, 1024)], [])
+            cp("A", VP, VN, None, 1.0, 0.0, AF.Abs)
+            s2 = send([(helper(0), VP, S("vp", 0, 1024, 1, 144 * r, 144 * r + 128), "hv%d" % r)], 512)
+            ops[s2]["soft"] += [s1] + ([free["F"]] if r else [])
+            arrive("aVf%d" % r, half, S("WF", 0, 1024), s2, 11.0)
+            arrive("aVp%d" % r, half, S("WF", 5120, 6144), s2, 11.0)
     return ops, q
 
 
@@ -663,75 +734,132 @@ def schedule(ops):
     if ORDER:
         return ORDER[0]
     n = len(ops)
-    succ = [[] for _ in range(n)]
-    pred = [sorted(set(o["deps"]) | set(o["soft"])) for o in ops]
-    for i in range(n):
-        for j in pred[i]:
-            succ[j].append(i)
-    prio = [0.0] * n
-    for i in range(n - 1, -1, -1):
-        prio[i] = ops[i]["dur"] + 0.1 + max([prio[j] for j in succ[i]] or [0.0])
-    best, seed = None, 1
+    link = lambda i, j: (0 if ops[i]["kind"] != "a" and ops[j]["kind"] != "a" and i not in ops[j]["deps"] else
+                         1 if ops[i]["kind"] == ops[j]["kind"] == "c" and not (ops[j]["deps"].get(i) or ops[i]["deps"].get(j)) else 2)
+    fwd, bwd = [[] for _ in range(n)], [[] for _ in range(n)]
+    for j in range(n):
+        for i in sorted(set(ops[j]["deps"]) | set(ops[j]["soft"])):
+            fwd[i].append((j, link(i, j)))
+            bwd[j].append((i, link(i, j)))
+    flex = [len(o["dur"]) > 1 for o in ops]
+    seed = [SEED]
+
+    def rnd():
+        seed[0] = (seed[0] * 1103515245 + 12345) % 2147483648
+        return seed[0] / 2147483648.0
+
+    def worth(got):
+        return max(got[2]) + 0.02 * sum(got[2]) / n
+
+    def again(got, slack):
+        rev = one_pass(ops, bwd, got[2], 0.25, got[3])
+        return one_pass(ops, fwd, rev[2], slack, got[3])
+
+    def chain(got):
+        i, out = max(range(n), key=lambda i: got[2][i]), []
+        while i is not None:
+            out.append(i)
+            i = got[4][i]
+        return out
+
+    best = None
     for it in range(ROUNDS):
-        got = one_pass(ops, succ, pred, prio, (0.25, 0.6, 1.0, 1.6)[it % 4])
-        if best is None or max(got[2]) < max(best[2]):
-            best = got
-        base = got if it % 8 < 6 else best
-        back = one_pass(ops, pred, succ, base[2], 0.25)
-        prio = []
-        for i in range(n):
-            seed = (seed * 1103515245 + 12345) % 2147483648
-            prio.append(back[2][i] + (seed / 2147483648.0) * (0.0, 0.5, 1.5)[it % 3])
+        eng = [o["eng"] if len(o["dur"]) == 1 else ("V" if it and rnd() < (0.1, 0.2, 0.3)[it % 3] else "A") for o in ops]
+        got = one_pass(ops, fwd, [-o["when"] for o in ops], (0.3, 0.6, 1.0, 1.5)[it % 4], eng)
+        for k in range(3):
+            if best is None or worth(got) < worth(best):
+                best = got
+            got = again(got, (0.25, 0.6, 1.0)[k % 3])
+    now, path = best, chain(best)
     for it in range(TRIES):
-        prio = [-t for t in best[1]]
-        seed = (seed * 1103515245 + 12345) % 2147483648
-        mid = (seed / 2147483648.0) * max(best[2])
-        for i in range(n):
-            if abs(best[1][i] - mid) < 12.0:
-                seed = (seed * 1103515245 + 12345) % 2147483648
-                if seed % 1000 < (60, 150, 300)[it % 3]:
-                    prio[i] += (seed / 1073741824.0 - 1.0) * (1.0, 3.0, 8.0)[(it // 3) % 3]
-        got = one_pass(ops, succ, pred, prio, (0.3, 1.0, 1.7)[(it // 9) % 3])
-        if max(got[2]) <= max(best[2]):
-            best = got
+        prio = [-t for t in now[1]]
+        eng = list(now[3])
+        for k in range(1 + (it % 4 == 3)):
+            at = int(rnd() * (len(path) - 1))
+            i, j = path[at], path[at + 1]
+            if flex[i] and rnd() < 0.6:
+                eng[i] = "A" if eng[i] == "V" else "V"
+            elif eng[i] == eng[j] and j not in ops[i]["deps"]:
+                if rnd() < 0.5:
+                    prio[i] = prio[j] + 0.01 + 2.0 * rnd() ** 2
+                else:
+                    prio[j] = prio[i] - 0.01 - 6.0 * rnd() ** 2
+            else:
+                for x in range(n):
+                    if abs(now[1][x] - now[1][i]) < 3.0 and rnd() < 0.1:
+                        prio[x] += (2.0 * rnd() - 1.0) * 3.0
+                        if flex[x] and rnd() < 0.3:
+                            eng[x] = "A" if eng[x] == "V" else "V"
+        got = one_pass(ops, fwd, prio, (0.3, 1.0, 2.0)[it % 3], eng)
+        if it % 8 == 0:
+            more = again(got, 0.5)
+            got = more if worth(more) < worth(got) else got
+        if worth(got) <= worth(now) + HEAT * (1.0 - it / TRIES) * rnd():
+            now, path = got, chain(got)
+            if worth(now) < worth(best):
+                best = now
     ORDER.append(best)
     return best
 
 
-ROUNDS, TRIES = 60, 1800
+ROUNDS, TRIES, HEAT, SEED = 20, 6000, 0.5, 1
 
 
-def one_pass(ops, succ, pred, prio, slack):
+def one_pass(ops, succ, prio, slack, eng):
     n = len(ops)
-    left = [len(p) for p in pred]
-    free = {}
-    done = [0.0] * n
-    start = [0.0] * n
-    can = [0.0] * n
-    ready = [i for i in range(n) if left[i] == 0]
+    left = [0] * n
+    for lst in succ:
+        for j, _ in lst:
+            left[j] += 1
+    free = {None: 0.0, "D": 0.0, "P": 0.0, "V": 0.0, "A": 0.0, "S": 0.0, "G": 0.0}
+    done, start, can, why = [0.0] * n, [0.0] * n, [0.0] * n, [None] * n
+    ready, soon, last = {e: [] for e in free}, {e: 1e9 for e in free}, {}
+    for i in range(n):
+        if left[i] == 0:
+            ready[eng[i]].append(i)
+            soon[eng[i]] = 0.0
     order = []
-    while ready:
-        est = [(max(can[i], free.get(ops[i]["eng"], 0.0)) if ops[i]["eng"] else can[i]) for i in ready]
-        first = min(est)
-        e0 = ops[ready[est.index(first)]]["eng"]
-        k = max((k for k in range(len(ready)) if ops[ready[k]]["eng"] == e0 and est[k] <= first + slack), key=lambda k: prio[ready[k]])
-        i = ready.pop(k)
+    for _ in range(n):
+        first, e = 1e9, None
+        for x, t in soon.items():
+            if t < 1e9:
+                if free[x] > t:
+                    t = free[x]
+                if t < first:
+                    first, e = t, x
+        lst = ready[e]
+        i, top, bar = None, -1e18, first + slack
+        for x in lst:
+            if can[x] <= bar and prio[x] > top:
+                i, top = x, prio[x]
+        lst.remove(i)
+        soon[e] = min([can[x] for x in lst]) if lst else 1e9
         o = ops[i]
-        start[i] = est[k]
-        done[i] = est[k] + o["dur"]
+        est = can[i]
+        if e and free[e] > est:
+            est, why[i] = free[e], last[e]
+        start[i] = est
+        end = est + o["dur"][e]
         if o["kind"] == "d":
-            done[i] = free["D"] = max(done[i], free.get("D", 0.0) + o["dur"] - 2.0)
-        if o["eng"]:
-            free[o["eng"]] = est[k] + o["hold"]
+            t = free["D"] + o["dur"][e] - 1.8 - (o["hold"] if e == "G" else 0.0)
+            if t > end:
+                end, why[i] = t, last["D"]
+            free["D"], last["D"] = end, i
+        done[i] = end
+        if e:
+            free[e], last[e] = est + (o["dur"][e] if o["hold"] is None else o["hold"]), i
         order.append(i)
-        for j in succ[i]:
-            same = ops[j]["eng"] == o["eng"] and o["kind"] == "c" and not (ops[j]["deps"].get(i) or o["deps"].get(j))
-            same = same or (ops[j]["eng"] == o["eng"] and (i in ops[j]["soft"] or j in o["soft"]))
-            can[j] = max(can[j], start[i] if same else done[i] + 0.1)
+        for j, how in succ[i]:
+            t = est if how == 0 else end if how == 1 and eng[j] == e else end + WAKE
+            if t > can[j]:
+                can[j], why[j] = t, i
             left[j] -= 1
             if left[j] == 0:
-                ready.append(j)
-    return order, start, done
+                x = eng[j]
+                ready[x].append(j)
+                if can[j] < soon[x]:
+                    soon[x] = can[j]
+    return order, start, done, eng, why
 
 
 def rank_program(g, core, T, topo):
@@ -742,14 +870,14 @@ def rank_program(g, core, T, topo):
                 helper_program(g, core, T, topo, r)
         return
     ops, q = build(g, core, T, topo, rank)
-    order, _, _ = schedule(ops)
+    order, _, _, eng, _ = schedule(ops)
     count = {}
     mark = {}
     for i in order:
         o = ops[i]
         if o["kind"] == "c":
-            count[o["eng"]] = count.get(o["eng"], 0) + 1
-            mark[i] = ("c" + o["eng"], count[o["eng"]])
+            count[eng[i]] = count.get(eng[i], 0) + 1
+            mark[i] = ("c" + eng[i], count[eng[i]])
         else:
             mark[i] = (o["sem"], o["cnt"])
     seen = {}
@@ -759,17 +887,17 @@ def rank_program(g, core, T, topo):
             continue
         want = {}
         for j, raw in o["deps"].items():
-            if ops[j]["kind"] == "c" and o["kind"] == "c" and ops[j]["eng"] == o["eng"] and not raw:
+            if ops[j]["kind"] == "c" and o["kind"] == "c" and eng[j] == eng[i] and not raw:
                 continue
             sem, v = mark[j]
             want[sem] = max(want.get(sem, 0), v)
         for sem, v in sorted(want.items()):
-            if seen.get((o["eng"], sem), 0) < v:
-                q[o["eng"]].wait_ge(T.sem[sem], v)
-                seen[(o["eng"], sem)] = v
-        r = o["emit"]()
+            if seen.get((eng[i], sem), 0) < v:
+                q[eng[i]].wait_ge(T.sem[sem], v)
+                seen[(eng[i], sem)] = v
+        r = o["emit"](eng[i])
         if o["kind"] == "c":
-            r.then_inc(T.sem["c" + o["eng"]], 1)
+            r.then_inc(T.sem["c" + eng[i]], 1)
     total = {}
     for sem, v in mark.values():
         total[sem] = max(total.get(sem, 0), v)

@@ -7,19 +7,19 @@ SCRATCH = {
     "XF": ("sbuf", [128, 8224], BF), "XB": ("sbuf", [128, 8224], BF),
     "PTf": ("sbuf", [128, 4096], BF), "PTb": ("sbuf", [128, 4096], BF), "PT2": ("sbuf", [128, 4096], BF),
     "AR": ("sbuf", [128, 4096], BF), "INV": ("sbuf", [128, 4096], BF), "GB": ("sbuf", [128, 8224], BF),
-    "IB": ("sbuf", [128, 1024], I32), "IS": ("sbuf", [128, 512], I32),
-    "CU": ("sbuf", [128, 1024], U16), "OF": ("sbuf", [128, 768], U16),
+    "IB": ("sbuf", [128, 1024], I32), "IS": ("sbuf", [128, 448], I32),
+    "CU": ("sbuf", [128, 1024], U16), "OF": ("sbuf", [128, 640], U16),
     "WK": ("sbuf", [128, 3072], F32), "GAP": ("sbuf", [128, 3072], F32), "VAL": ("sbuf", [128, 3072], F32),
     "LL": ("sbuf", [128, 2048], BF), "BA": ("sbuf", [128, 720], BF), "BC": ("sbuf", [128, 144], BF),
-    "RM": ("sbuf", [128, 240], BF), "PM": ("sbuf", [128, 1920], BF), "ID": ("sbuf", [128, 384], F32),
+    "RM": ("sbuf", [128, 304], BF), "PM": ("sbuf", [128, 2048], BF), "ID": ("sbuf", [128, 512], F32),
     "Q": ("sbuf", [128, 1024], F32), "COL": ("sbuf", [128, 48], F32), "EPS": ("sbuf", [128, 4], F32),
     "ST": ("sbuf", [128, 576], F32), "SB": ("sbuf", [128, 3712], BF),
     "xd": ("dram", [128, 4096], BF), "xe": ("dram", [160, 4096], BF),
-    "vn": ("dram", [4, 128, 512], F32), "vp": ("dram", [288, 1024], F32),
+    "vp": ("dram", [288, 1024], F32),
 }
 for _b in range(8):
     SCRATCH["PS%d" % _b] = ("psum", [128, 512], F32)
-ARRIVALS = (["aXh", "aXF0", "aXF1", "aXB0", "aXB1", "sB", "sL"]
+ARRIVALS = (["aXh", "aXF0", "aXF1", "aXB0", "aXB1", "sB", "sL", "sC"]
             + ["aPT%s%d" % (t, h) for t in "fb" for h in range(4)] + ["aPT2"]
             + ["a%s%d%d" % (t, r, h) for t in ("Lf", "Lb", "Vb", "Vn") for r in range(2) for h in range(2)]
             + ["aV%s%d" % (t, r) for t in "fp" for r in range(2)])
@@ -102,10 +102,10 @@ def helper_program(g, core, T, topo, rank):
 
 WAKE = 0.22
 CY, PE, GATHER, SCATTER = 0.00086, 0.00045, 1.45, 3.5
-HALVED = [(r, h) for r in range(3) for h in range(2)]
-ADDED = [(r, w, h) for r in range(3) for w in range(2) for h in range(2)]
-BY_DMA = {"B": (4, 4), "F": (4, 2)}
-RATE = (280.0, 210.0)
+BY_TENSOR = [(0, 1, 1), (0, 0, 0), (0, 0, 1)]
+SPLIT = True
+BY_DMA = {"B": (4, 4), "F": (4, 0)}
+RATE = (310.0, 225.0)
 START = (32.0, 68.0, 106.0)
 
 
@@ -273,18 +273,18 @@ def build(g, core, T, topo, rank):
     sb = lambda a, w: S("SB", a, a + w)
     st = lambda a, w: S("ST", a, a + w)
     gb = lambda a, w=1024: S("GB", a, a + w)
-    H, P1, P2, QB, RR, UV = sb(0, 128), [sb(128, 256), sb(384, 256)], sb(640, 256), sb(896, 640), sb(1536, 768), sb(2304, 256)
+    H, P1, P2, QB, RR, UV = sb(0, 128), [sb(128, 256), sb(384, 256)], sb(640, 256), sb(896, 640) , sb(1536, 768), sb(2304, 256)
     FL, FLO, MSG, MISS = sb(2560, 256), sb(2816, 256), sb(3072, 256), [sb(3328, 64), sb(3392, 64)]
     OK, WON, PEN, ONE = sb(3456, 64), sb(3520, 64), sb(3584, 64), sb(3648, 64)
     T1A, JJ = st(0, 512), st(512, 64)
     AA, JC, DN, TM = S("IB", 0, 256), S("IB", 256, 384), S("IB", 384, 512), S("IB", 512, 576)
     OFS, OFT = S("CU", 0, 512), S("CU", 512, 1024)
     OC1, OC2, OSP, ONB, OMS, ONS, OGI = [S("OF", a, b) for a, b in (
-        (0, 128), (128, 256), (256, 384), (384, 576), (576, 640), (640, 704), (704, 768))]
-    LTB, LTF, GC, LTO, GNB, LE = 0, 1040, 2080, 4128, 5152, 7200
+        (0, 128), (128, 256), (256, 384), (384, 576), (576, 640), (384, 448), (576, 640))]
+    LTF, LTB, GC, LTO, GNB, LE = 0, 1040, 2080, 4128, 5152, 7200
     MSI = S("IS", 0, 64)
     FB = S("SB", 1536, 2560)
-    ID, HALF, LESS = S("ID", 0, 128), S("ID", 128, 256), S("ID", 256, 384)
+    ID, HALF, LESS = S("ID", 0, 128), S("ID", 256, 384), S("ID", 384, 512)
     pm = lambda k: S("PM", 128 * k, 128 * k + 128)
     moved = lambda k, var: S("PM", 256 * k + (112, 0, 16)[var], 256 * k + (112, 0, 16)[var] + 128)
     UP, EYE, DOWN = [moved(0, var) for var in range(3)]
@@ -297,7 +297,7 @@ def build(g, core, T, topo, rank):
     early = [cp("V", S("CU", 512 * i, 512 * i + 512), S("IB", 512 * i, 512 * i + 512)) for i in range(2)]
     dma("S", [(lambda: T.IB[:], lambda: T.fl[:])], 512, [], [S("IB", 0, 1024)])
     at(9)
-    cp("V", FB, S("IB", 0, 1024))
+    cf = cp("V", FB, S("IB", 0, 1024))
     at(0)
     dma("S", [(lambda: T.EPS[:, 0:1], lambda: T.eps[:])], 1, [], [S("EPS", 0, 1)])
     sx = send([(helper(0), S("xd", 0, 4096), S("xe", 0, 4096, 1, 16, 144), "aXh")], 1024, hold=5.0)
@@ -306,7 +306,7 @@ def build(g, core, T, topo, rank):
 
     pc = S("IS", 64, 65)
     iota(pc, [[0, 1]], 0, 1)
-    iota(S("IS", 256, 512), [[1, 16], [0, 16]], 0, 0)
+    iota(S("IS", 192, 448), [[1, 16], [0, 16]], 0, 0)
     iota(S("IS", 128, 192), [[0, 4], [1, 16]], 0, 0)
     iota(S("IS", 80, 97), [[16, 17]], -64, 0)
     ts(S("IS", 66, 67), pc, 15, ALU.bitwise_and)
@@ -320,17 +320,18 @@ def build(g, core, T, topo, rank):
     ts(S("INV", 256, 320), S("IS", 128, 192), col(3), ALU.mult)
     for j in range(2):
         cp("V", S("INV", 256 + (64 << j), 256 + (128 << j)), S("INV", 256, 256 + (64 << j)))
-    ts(PS(0, 0, 256), S("IS", 256, 512), col(0), ALU.mult)
+    ts(PS(0, 0, 256), S("IS", 192, 448), col(0), ALU.mult)
     tt(S("INV", 0, 256), PS(0, 0, 256), S("INV", 256, 512), ALU.add)
     LC = gb(LE)
     cp("V", S("INV", 256, 512), S("INV", 0, 256), None, 1.0, step(16))
     cp("V", S("INV", 512, 1024), S("INV", 0, 512), None, 1.0, step(32))
     for j in range(1, 4):
-        cp("VA", S("INV", 1024 * j, 1024 * j + 1024), S("INV", 0, 1024), None, 1.0, step(64 * j))
+        cp("AV", S("INV", 1024 * j, 1024 * j + 1024), S("INV", 0, 1024), None, 1.0, step(64 * j))
     cp("VA", LC, S("INV", 0, 1024), None, 1.0, col(2))
     cp("V", OMS, MSI)
     sc = add("V", {"V": cost(SCATTER, 1024)}, lambda e: g.vector.tensor_copy(ind(S("INV", 0, 4096), OMS), ap(LC)), [LC, OMS], [S("INV", 0, 4096)])
     ops[sc]["soft"] += early
+    ops[cf]["soft"].append(sc)
     ones = lambda w: S("BA", 0, w)
     mset(ones(720), 1.0)
     keep = lambda i: sb(2560 + 128 * i, 128)
@@ -369,8 +370,8 @@ def build(g, core, T, topo, rank):
     arrive("aPT2", whole, S("PT2", 0, 4096), s2)
 
     at(20)
-    mset(ID, 1.0)
-    asel(ID, [[-1, 128]], 0, 1)
+    mset(S("ID", 0, 256), 1.0)
+    asel(S("ID", 0, 256), [[0, 2], [-1, 128]], 0, 1)
     cp("VA", HALF, ID, None, 0.5)
     cp("VA", LESS, ID, None, -0.5)
     EM, RT = sb(896, 128), [S("RM", 32 * v, 32 * v + 32) for v in range(3)]
@@ -392,8 +393,8 @@ def build(g, core, T, topo, rank):
     tt(TWO, sub(EYE, 0, 64), sub(EYE, 64, 64), ALU.add)
     cp("VA", S("PM", 256, 512), S("PM", 0, 256), None, 64.0)
     scaled = {64.0: pm(2), 1.0: EYE}
-    for k, v in enumerate((-1.0, -16.0, 0.5, -0.5, 0.25, 0.1875, 512.0)):
-        scaled[v] = pm(4 + k)
+    for k, v in enumerate((-1.0, -16.0, 0.5, -0.5, 0.25, 0.1875, 512.0, 4.0)):
+        scaled[v] = pm(4 + k + 4 * (k // 7))
         cp("VA", scaled[v], EYE, None, v)
     ts(S("IS", 68, 69), pc, 16, ALU.bitwise_and)
     ts(S("IS", 74, 75), pc, 4, ALU.arith_shift_right)
@@ -406,12 +407,15 @@ def build(g, core, T, topo, rank):
     ki = S("IS", 192, 256)
     iota(ki, [[1, 64]], 0, 0)
     ts(JJ, ki, 16.0, ALU.mult, col(8), ALU.add)
-    ts(sub(JC, 0, 64), JJ, GC - LTF - 8192.0, ALU.add)
-    ts(sub(JC, 64, 64), JJ, GC + 1024 - LTB - 8192.0, ALU.add)
+    ts(sub(JC, 0, 64), JJ, GC + 1024 - LTF - 8192.0, ALU.add)
+    ts(sub(JC, 64, 64), JJ, GC - LTB - 8192.0, ALU.add)
     mset(S("BC", 0, 144), 0.0)
     ts(S("BC", 16, 144, 16), sub(ki, 0, 8), col(11), ALU.is_equal)
     for j in range(4):
         asel(S("LL", 512 * j, 512 * j + 512), [[-1, 4], [-16, 8], [0, 16]], -4 * j, 1, ones(512))
+    mset(ones(720), 0.25)
+    ROUND = S("RM", 240, 304)
+    mset(ROUND, -0.375)
     asel(S("BA", 0, 144), [[-16, 9], [1000, 16]], 16, 1)
     asel(S("BA", 144, 720), [[-1, 4], [-16, 9], [1000, 16]], 4, 1)
     mset(ONE, 1024.0)
@@ -461,59 +465,64 @@ def build(g, core, T, topo, rank):
     def opened(bank):
         mm([(PS(bank), S("LL", 0, 128), S("LL", 0, 512))], True, False)
 
-    def place_of(pos, qb, var, bank, out):
-        cp("VA", qb, pos, None, 0.25, 191.625)
+    def place_of(qb, var, bank, out):
         mm([(sub(bank, 64 * w, 64), moved(k, var), sub(qb, 128 * w + 64 * k, 64)) for w in range(width(out) // 64) for k in range(2)])
         ts(out, bank, -12480.0, ALU.add)
 
     def visit1(r, flows):
         p1 = P1[r % 2]
-        mm([(PS(X2, 128 * w, 128 * w + 128), EYE, H) for w in range(2)] + [(PS(X2, 64 * j, 64 * j + 64), EYE, sub(flows, j, 64, 4)) for j in range(4)])
-        ts(p1, PS(X2, 0, 256), 0.0, ALU.max, 255.0, ALU.min)
-        place_of(p1, sub(QB, 0, 256), 1, PS(X2, 256, 384), OC1)
+        mm([(PS(VB, 128 * w, 128 * w + 128), EYE, H) for w in range(2)] + [(PS(VB, 64 * j, 64 * j + 64),) + flows[j] for j in range(4)])
+        ts(p1, PS(VB, 0, 256), 0.0, ALU.max, 255.0, ALU.min)
+        cp("VA", sub(QB, 0, 256), p1, None, 0.25, 191.625)
+        place_of(sub(QB, 0, 256), 1, PS(VB, 256, 384), OC1)
         for w in (1, 0):
-            cp("A" if r else "AV"[w], gb(GC + 1024 * w), S(("PTf", "PTb")[w], 0, 4096), sub(OC1, 64 * w, 64))
+            cp("VA" if r or not w else "AV", gb(GC + 1024 - 1024 * w), S(("PTf", "PTb")[w], 0, 4096), sub(OC1, 64 * w, 64))
         both = gb(GC, 2048)
         if r:
             turn(X0, both, RT[1], 0, 1024.0)
             turn(X1, both, RC, 512, 1024.0)
-            mm([back(PS(X1, 128 + 64 * w, 192 + 64 * w), 512, 0, w) for w in range(2)])
+            mm([back(PS(X1, 128 + 64 * w, 192 + 64 * w), 512, 0, 1 - w) for w in range(2)])
             tt(PS(X1, 128, 256), PS(X1, 128, 256), JC, ALU.min)
             ts(OSP, PS(X1, 128, 256), 8192.0, ALU.add)
         else:
+            at(START[0] + 1.5)
             turn(X0, both, RT[1], 0, 16.0, AF.Relu)
             turn(X1, both, RH, 512, 0.0, AF.Relu)
-        mm([back(PS(X0, 256 * w + 64 * i, 256 * w + 64 * i + 64), 0, i, w) for w in range(2) for i in range(4)])
+        mm([back(PS(X0, 256 * w + 64 * i, 256 * w + 64 * i + 64), 0, i, 1 - w) for w in range(2) for i in range(4)])
         cp("VA", T1A, PS(X0), None, 1.0, 0.0 if r else -4112.0)
         if r:
             ts(OFS, PS(X0), 1024.0, ALU.min)
 
     def visit2(r, w, t0):
         bp, ba, bt, cnt, br, by = ((PS(X0, 0, 192), X1, PS(X0, 256, 512), PS(X2, 0, 64), PS(X1, 0, 384), PS(X2, 128, 384)),
-                                   (PS(U0, 0, 192), U1, PS(T0, 0, 256), PS(T1, 0, 64), PS(U0, 0, 384), PS(T0, 256, 512)))[w]
+                                   (PS(U0, 0, 192), U1, PS(T0, 0, 256), PS(T1, 0, 64), PS(U0, 0, 384), PS(T1, 128, 384)))[w]
+        bc = (PS(X1, 0, 64), PS(U1, 0, 64))[w]
         p1, p2, rr = sub(P1[r % 2], 128 * w, 128), sub(P2, 128 * w, 128), sub(RR, 384 * w, 384)
         lt = (LTF, LTB)[w]
-        o = gb(GC + 1024 * w)
+        o = gb(GC + 1024 - 1024 * w)
         reads = []
         if r:
             o = S("INV", 1024 * w, 1024 * w + 1024)
             at(t0 + 1.5 * (1 - w))
-            reads.append(cp("V", o, S("GB", lt, GC + 1024 * w + 1024), sub(OSP, 64 * w, 64)))
+            reads.append(cp("AV", o, S("GB", lt, GC + 2048 - 1024 * w), sub(OSP, 64 * w, 64)))
         at(t0 + (8, 1)[w])
+        start = [(sub(bp, 0, 128), scaled[0.25], p1)] + [(sub(bp, 64 * j, 64), m, x) for j in range(2) for m, x in ((scaled[0.1875], ONE), (EYE, ROUND))]
         if w or not r:
-            mm([(sub(bp, 0, 128), EYE, p1)] + pick(sub(bp, 0, 64), 1 + 2 * w, o) + pick(sub(bp, 64, 64), 2 + 2 * w, o))
+            mm(start, True, False)
+            mm(pick(sub(bp, 0, 64), 1 + 2 * w, o) + pick(sub(bp, 64, 64), 2 + 2 * w, o), False, True)
         else:
             small(X0, o, sub(RO, 0, 16))
-            mm([(sub(bp, 0, 128), EYE, p1)] + [(sub(bp, 64 * j, 64), part(sub(QS, 128 * j, 128), 0, 64), part(sub(EYE, 0, 64), 0, 64)) for j in range(2)])
-        ts(p2, sub(bp, 0, 128), 0.0, ALU.max, 255.0, ALU.min)
-        place_of(p2, sub(QB, 256 + 128 * w, 128), 2 * w, sub(bp, 128, 64), sub(OC2, 64 * w, 64))
+            mm(start + [(sub(bp, 64 * j, 64), part(sub(QS, 128 * j, 128), 0, 64), part(sub(scaled[0.25], 0, 64), 0, 64)) for j in range(2)])
+        ts(sub(QB, 256 + 128 * w, 128), sub(bp, 0, 128), 191.625, ALU.max, 255.375, ALU.min)
+        ts(p2, sub(bp, 0, 128), 255.375, ALU.min, -191.625, ALU.add)
+        place_of(sub(QB, 256 + 128 * w, 128), 2 * w, bc, sub(OC2, 64 * w, 64))
         g2 = S("XB", 1024 * w, 1024 * w + 1024) if r else gb((LE, LTO)[w])
-        cp("AV"[w], g2, S("PT2", 0, 4096), sub(OC2, 64 * w, 64))
+        cp(("VA", "AV")[w], g2, S("PT2", 0, 4096), sub(OC2, 64 * w, 64))
         if r:
             for i in range(4):
                 o = S("XF", 4096 * w + 1024 * i, 4096 * w + 1024 * i + 1024)
                 at(t0 + ((5, 9, 11, 13), (0, 1.5, 3, 4.5))[w][i])
-                reads.append(cp("A" if w or i else "V", o, gb(lt, 1040), sub(OFS, 256 * w + 64 * i, 64)))
+                reads.append(cp("VA" if (w, i) != (1, 1) else "AV", o, gb(lt, 1040), sub(OFS, 256 * w + 64 * i, 64)))
                 if w:
                     mm(pick(cnt, 0, o), i == 0, i == 3)
                 elif i % 2:
@@ -524,13 +533,14 @@ def build(g, core, T, topo, rank):
             at(t0 + (12, 4)[w])
             turn(ba, g2, RT[2 - 2 * w], 512, 6144.0)
         else:
-            mm([back(cnt, 512, i, w) for i in range(4)])
+            mm([back(cnt, 512, i, 1 - w) for i in range(4)])
             turn(ba, g2, RT[2 - 2 * w], (512, 0)[w], 16.0, AF.Relu)
-        cp("A", OK, cnt, None, -1024.0, 1024.0, AF.Relu)
+        cp("A", OK, cnt, None, -4096.0, 1024.0, AF.Relu)
         mm([it for i in range(4) for it in (back(sub(bt, 64 * i, 64), 512 if r or not w else 0, i, 0, 64), (sub(bt, 64 * i, 64), scaled[-16.0], OK))])
         tt(bt, bt, sub(T1A, 256 * w, 256), ALU.max)
         ts(sub(OFT, 256 * w, 256), bt, 0.0 if r else 4112.0, ALU.add)
-        mm([(sub(br, 128 * j, 128), EYE, x) for j, x in enumerate((p1, p2, H))]
+        at(t0 + (12, 3.5)[w])
+        mm([(sub(br, 128 * j, 128), scaled[4.0 if j == 1 else 1.0], x) for j, x in enumerate((p1, p2, H))]
            + [(sub(br, 64 * j, 64), scaled[-1.0 if j // 2 == 1 else 1.0], OK) for j in range(6)]
            + [(sub(br, 128 + 64 * j, 64), EYE, ONE) for j in range(2)])
         cp("VA", rr, br, None, 1.0, -1024.0, AF.Relu)
@@ -540,9 +550,8 @@ def build(g, core, T, topo, rank):
         mm([(sub(by, 128, 128), scaled[0.25], sub(rr, 128 * j, 128)) for j in range(2)] + [(sub(by, 128, 128), scaled[-1.0], qe)]
            + [(sub(by, 128 + 64 * j, 64), scaled[0.1875], ONE) for j in range(2)])
         cp("VA", sub(UV, 128 * w, 128), sub(by, 128, 128), None, 1.0, TINY)
-        if w == 0 and (r, 0) in HALVED:
-            v = sub(UV, 64, 64 if (r, 1) in HALVED else 32)
-            cp("VA", v, v, None, 0.5)
+        if w == 0:
+            cp("VA", sub(UV, 64, 32), sub(UV, 64, 32), None, 0.5)
         return reads
 
     def lanes_table(bank, hf, flag):
@@ -552,15 +561,19 @@ def build(g, core, T, topo, rank):
                 items.append((PS(bank, row + 16 * (k // 2), 512, 32), SWAP[k], sub(x, (k % 2) * x[3], 16, 2 * x[3])))
         mm(items)
 
-    own = S("INV", 2048, 4096)
+    def next_flows(o):
+        small(VB, o, RO)
+        mm([(PS(VB, j, 256, 4), part(sub(QS, 128 * j, 128), 0, 64), part(sub(EYE, 0, 64), 0, 64)) for j in range(4)])
+        cp("VA", FLO, PS(VB, 0, 256))
+
     at(23)
-    cp("V", sub(own, 0, 1024), S("AR", 0, 4096), OMS)
-    cp("A", sub(own, 1024, 1024), S("AR", 0, 4096), sub(ONB, 0, 64))
-    turn(X1, own, RO, 0)
-    mm([back(PS(X1, 256 * w + j, 256 * w + 256, 4), 0, j, w) for w in range(2) for j in range(4)])
-    cp("VA", sb(2560, 512), PS(X1))
-    visit1(0, FL)
-    nch, casts = 0, []
+    cp("AV", S("INV", 2048, 3072), S("AR", 0, 4096), OMS)
+    small(X1, S("INV", 2048, 3072), RO)
+    visit1(0, [(part(sub(QS, 128 * j, 128), 0, 64), part(sub(EYE, 0, 64), 0, 64)) for j in range(4)])
+    at(40)
+    cp("VA", gb(GNB), S("AR", 0, 4096), sub(ONB, 0, 64))
+    next_flows(gb(GNB))
+    casts = []
     VN, VP = S("VAL", 1024, 2048), S("VAL", 2048, 3072)
     for r in range(3):
         t0 = START[r]
@@ -582,90 +595,97 @@ def build(g, core, T, topo, rank):
             tt(TM, TM, JJ, ALU.add)
             cp("V", ONS, TM)
             o = S("INV", 2048, 3072)
-            cp("A", o, gb(LTO, 3072), ONS)
-            small(X1, o, RO)
-            mm([(PS(X1, j, 256, 4), part(sub(QS, 128 * j, 128), 0, 64), part(sub(EYE, 0, 64), 0, 64)) for j in range(4)])
-            cp("VA", FLO, PS(X1, 0, 256))
+            cp("VA", o, gb(LTO, 3072), ONS)
+            next_flows(o)
         flags = visit2(r, 0, t0 - (0 if r else 5))
         at(t0 + 20)
         mm([(PS(X1, j, 256, 4), scaled[v], sub(RR, 384 * (j // 2) + 128 * k + 64 * (j % 2), 64)) for j in range(4) for k, v in enumerate((1.0, 0.5, -0.5))]
            + [(PS(X1, j, 256, 4), scaled[-0.5], sub(H, 64 * (j % 2), 64)) for j in range(4)] + [(PS(X1, 0, 256), scaled[-1.0], FLO)])
         ts(AA, PS(X1, 0, 256), -0.25, ALU.add)
-        at(t0 + (21 if r else 14))
-        if r < 2:
-            visit1(r + 1, FLO)
         if r == 0:
+            at(t0 + 14)
             for k in range(2):
-                cp("A", gb(GNB + 1024 * k), S("AR", 0, 4096), sub(ONB, 64 + 64 * k, 64))
+                cp("VA", gb(GNB + 1024 * k), S("AR", 0, 4096), sub(ONB, 64 + 64 * k, 64))
             turn(X1, gb(GNB, 2048), RC, 512, 1024.0)
             mm([it for k in range(2) for it in (back(PS(X1, 128 + 64 * k, 192 + 64 * k), 512, 0, k), (PS(X1, 128 + 64 * k, 192 + 64 * k), LESS, JJ),
                                                  (PS(X1, 128 + 64 * k, 192 + 64 * k), LESS, JJ))])
             for k in range(2):
                 ts(sub(DN, 64 * k, 64), PS(X1, 128 + 64 * k, 192 + 64 * k), 1024.0 * k - 7168.0, ALU.min, 8192.0, ALU.add)
+        at(t0 + (19 if r else 16))
+        if r < 2:
+            visit1(r + 1, [(EYE, sub(FLO, j, 64, 4)) for j in range(4)])
         if r == 2:
             mm([(PS(X1, 0, 64), ID, JJ)] + [(PS(X1, 0, 64), scaled[512.0], MISS[k]) for k in range(2)])
             for hf in range(2):
                 ts(sub(OGI, 32 * hf, 32), PS(X1, 32 * hf, 32 * hf + 32), -512.0 * hf, ALU.add)
             cp("VA", VP, VN, None, 1.0, 0.0, AF.Relu)
-        taps = {}
+        taps, turns, rear = {}, [], [None] * 4
         for w in (1, 0):
             for hf in range(2):
                 win = S(("XF", "XB")[w], 0, 8224) if r == 0 else S(("WF", "WB")[w], 0, 10240)
                 off = lambda i: sub(OFT, 256 * w + 64 * i + 32 * hf, 32)
                 ub, tb = (U0, U1)[hf], (T0, T1)[hf]
                 a0, a2 = [S("WK", 1024 * hf + 512 * j, 1024 * hf + 512 * j + 512) for j in range(2)]
-                s_, e_ = a0, a2
+                s_, e_ = a0, S("GAP", 1536 * hf + 1024, 1536 * hf + 1536)
                 if r == 0:
                     a0, a2 = [S("INV", 1024 * hf + 512 * j, 1024 * hf + 512 * j + 512) for j in range(2)]
-                d1, d2 = [S("WK", 2048 + 512 * ((nch + j) % 2), 2560 + 512 * ((nch + j) % 2)) for j in range(2)]
-                nch += 1
+                d1, d2 = S("WK", 2048, 2560), S("WK", 2560, 3072)
+                vb = VB if (w, hf) == (0, 1) else ub
                 at(t0 + (7 if r else 5) + 5 * (2 * (1 - w) + hf))
                 mm(spread(ub, sub(UV, 128 * w + 32 * hf, 32)))
-                if (r, w, hf) in ADDED:
-                    opened(tb)
+                opened(tb)
                 cp("A", a2, win, off(2))
                 cp("A", a0, win, off(0))
-                taps[w, hf] = [tt(d2, win, a2, ALU.subtract, off(3)), tt(d1, win, a0, ALU.subtract, off(1))]
+                taps[w, hf] = [tt(d2, win, a2, ALU.subtract, off(3))]
+                if (r, w, hf) in BY_TENSOR:
+                    a1, d1 = [S("INV", 2048 + 1024 * j + 512 * hf, 2560 + 1024 * j + 512 * hf) for j in range(2)]
+                    cp("A", d1, PS(ub), None, 2.0)
+                    cp("A", a1, win, off(1))
+                else:
+                    taps[w, hf].append(tt(d1, win, a0, ALU.subtract, off(1)))
                 if (r, w, hf) == (0, 0, 0):
                     for j in casts:
                         ops[j]["soft"].append(taps[w, hf][0])
                 if r == 1 and hf == 1:
                     if w:
-                        sg = send([(lo, None, None, "sB"), (hi, None, None, "sL")], 0, taps[1, 0] + taps[1, 1] + flags)
-                        free = {t: arrive("s" + t, 1, None, sg) for t in "BL"}
+                        sg = send([(lo, None, None, "sB"), (hi, None, None, "sL"), (far, None, None, "sC")], 0, taps[1, 0] + taps[1, 1] + flags)
+                        free = {t: arrive("s" + t, 1, None, sg) for t in "BLC"}
                     else:
                         free["F"] = send([(helper(1), None, None, "hF"), (helper(2), None, None, "hF")], 0, taps[0, 0] + taps[0, 1])
-                tt(PS(tb), PS(ub), d2, ALU.mult)
-                if (r, w, hf) in ADDED:
-                    mm([(PS(tb), ID if r else EYE, a2)], False, True)
-                else:
-                    tt(PS(tb), PS(tb), a2, ALU.add)
-                tt(PS(ub), PS(ub), d1, ALU.mult)
-                tt(s_, PS(ub), a0, ALU.add)
-                mm(spread(ub, sub(UV, 128 * w + 64 + 32 * hf, 32)))
-                tt(e_, PS(tb), s_, ALU.subtract)
+                front = (taps[w, hf] + [None])[:2] + [tt(PS(tb), PS(ub), d2, ALU.mult)]
+                mm([(PS(tb), ID if r else EYE, a2)], False, True)
+                if (r, w, hf) in BY_TENSOR:
+                    mm([(PS(ub), scaled[0.5], a1), (PS(ub), scaled[-0.5], a0)])
+                front.append(tt(PS(ub), PS(ub), d1, ALU.mult))
+                turns += [j for pair in zip(front, rear) for j in pair if j is not None]
+                rear = [tt(s_, PS(ub), a0, ALU.add)]
+                mm(spread(vb, sub(UV, 128 * w + 64 + 32 * hf, 32)))
+                rear.append(tt(e_, PS(tb), s_, ALU.subtract))
                 zb = S("VAL", 512 * hf, 512 * hf + 512)
                 if w:
-                    tt(PS(ub), PS(ub), e_, ALU.mult)
-                    tt(zb, PS(ub), s_, ALU.add)
+                    rear.append(tt(PS(ub), PS(ub), e_, ALU.mult))
+                    rear.append(tt(zb, PS(ub), s_, ALU.add))
                     continue
                 gp = S("GAP", 1536 * hf + 512 * r, 1536 * hf + 512 * r + 512)
                 le = gb(LE + 512 * hf, 512)
-                if (r, hf) not in HALVED:
-                    tt(PS(ub), PS(ub), e_, ALU.mult)
-                    tt(PS(ub), PS(ub), s_, ALU.add)
-                    tt(PS(ub), PS(ub), zb, ALU.subtract)
-                    opened(tb)
-                    cp("A", gp, PS(ub), None, 1.0, 0.0, AF.Abs)
-                    cp("A", PS(tb), PS(ub), None, 0.5)
-                    mm([(PS(tb), ID, zb)], False, False)
+                opened(tb)
+                if hf == 0:
+                    rear += [tt(PS(tb), PS(ub), e_, ALU.mult), None]
+                    mm([(PS(tb), HALF, s_), (PS(tb), LESS, zb)], False, True)
+                    opened(ub)
+                    cp("A", gp, PS(tb), None, 2.0, 0.0, AF.Abs)
+                    tt(PS(ub), PS(tb), zb, ALU.add)
+                    ub, tb = tb, ub
                 else:
-                    opened(VB)
-                    tt(PS(VB), PS(ub), e_, ALU.mult)
-                    mm([(PS(VB), HALF, s_), (PS(VB), LESS, zb)], False, True)
-                    opened(tb)
-                    cp("A", gp, PS(VB), None, 2.0, 0.0, AF.Abs)
-                    tt(PS(tb), PS(VB), zb, ALU.add)
+                    turns[-2:] = turns[:-3:-1]
+                    for i, j in zip(turns, turns[1:] + rear[:1]):
+                        ops[j]["soft"].append(i)
+                    tt(PS(vb), PS(vb), e_, ALU.mult)
+                    tt(PS(vb), PS(vb), s_, ALU.add)
+                    tt(PS(vb), PS(vb), zb, ALU.subtract)
+                    cp("A", gp, PS(vb), None, 1.0, 0.0, AF.Abs)
+                    cp("A", PS(tb), PS(vb), None, 0.5)
+                    mm([(PS(tb), ID, zb)], False, False)
                 at(t0 + (7 if r else 5) + 5 * (2 + hf) + 4)
                 ts(le, gp, S("EPS", 0, 1), ALU.is_le)
                 won, pen = sub(WON, 32 * hf, 32), sub(PEN, 32 * hf, 32)
@@ -692,38 +712,48 @@ def build(g, core, T, topo, rank):
                     cp("VA", le, PS(ub))
                     flip(gb(LTO + 512 * hf, 512), le)
                     src = gb(LTO + 512 * hf, 512)
-                    s0 = send([(hi, src, gb(LTB + 512 * hf, 512), "aLb%d%d" % (r, hf)), (lo, src, gb(LTF + 512 * hf, 512), "aLf%d%d" % (r, hf))],
-                              256, [free["B"], free["L"]] if r else [])
-                    arrive("aLb%d%d" % (r, hf), half, gb(LTB + 512 * hf, 512), s0)
-                    arrive("aLf%d%d" % (r, hf), half, gb(LTF + 512 * hf, 512), s0)
+                    both = [(hi, src, gb(LTB + 512 * hf, 512), "aLb%d%d" % (r, hf)), (lo, src, gb(LTF + 512 * hf, 512), "aLf%d%d" % (r, hf))]
+                    s0 = None
+                    for items in ([both[:1], both[1:]] if hf and SPLIT else [both]):
+                        s = send(items, 128 * len(items), [free["B"], free["L"]] if r else [])
+                        ops[s]["soft"] += [s0] if s0 else []
+                        s0 = s
+                        for it in items:
+                            arrive(it[3], half if len(items) == 2 else whole, it[2], s0)
                     at(t0 + 30 + hf)
                     if r:
                         tt(vn, PS(tb), vn, ALU.max)
                     else:
                         cp("VA", vn, PS(tb))
-                    c0, slot = 512 * hf, D3("vn", 2 * r + hf)
-                    s1 = send([(far, vn, slot, "aVn%d%d" % (r, hf)), (hi, vn, S("WB", c0, c0 + 512), "aVb%d%d" % (r, hf))], 512, [free["B"]] if r else [])
-                    ops[s1]["soft"].append(s0)
+                    c0, up = 512 * hf, S("WK", 1024 * hf + 512, 1024 * hf + 1024)
+                    mm([(PS(tb), S("ID", 112, 240), vn)])
+                    cp("VA", up, PS(tb))
+                    s1 = send([(hi, vn, S("WB", c0, c0 + 512), "aVb%d%d" % (r, hf)), (far, up, S("WB", 5120 + c0, 5632 + c0), "aVn%d%d" % (r, hf))],
+                              512, [free["B"], free["C"]] if r else [])
+                    for j in ([first, s1] if hf else []):
+                        ops[j]["soft"].append(s0)
+                    first = s1
                     arrive("aVb%d%d" % (r, hf), half, S("WB", c0, c0 + 512), s1)
-                    arrive("aVn%d%d" % (r, hf), half, slot, s1)
-                    s1 = sdma("S", [(S("WB", 5120 + c0, 5632 + c0, 1, 16, 128), part(slot, 0, 112)), (S("WB", 5120 + c0, 5632 + c0, 1, 0, 16), part(slot, 112, 128))], 256)
+                    arrive("aVn%d%d" % (r, hf), half, S("WB", 5120 + c0, 5632 + c0), s1)
                 else:
                     c0 = 512 * hf
                     y = sub(VP, c0, 512)
                     tt(y, PS(tb), y, ALU.max)
                     dma("S", [(lambda c0=c0: T.y[:, c0:c0 + 512], lambda y=y: ap(y))], 256, [y], [])
-                    ts(s_, S("GAP", 1536 * hf, 1536 * hf + 1536), 128.0, ALU.min, None, None, sub(OGI, 32 * hf, 32))
-                    cp("A", s_, s_, None, -1.0, 0.0, AF.Exp)
-                    dma("A", [(lambda c0=c0: T.ye[:, c0:c0 + 512], lambda s_=s_: ap(s_))], 256, [s_], [])
+                    cp("A", s_, S("GAP", 1536 * hf, 1536 * hf + 1536), sub(OGI, 32 * hf, 32), -1.0, 100.0, AF.Relu)
+                    ops[cp("A", s_, s_, None, 1.0, -100.0, AF.Exp)]["dur"]["A"] += 0.0 if hf else 1.3
+                    dma("S", [(lambda c0=c0: T.ye[:, c0:c0 + 512], lambda s_=s_: ap(s_))], 256, [s_], [])
                     flip(a2, PS(ub))
-                    dma("S", [((lambda k=k, c0=c0: T.yf[8 * k:8 * k + 8, c0:c0 + 512]), (lambda row=row, a2=a2: T.WK[row:128:16, a2[1]:a2[2]]))
-                              for k, row in enumerate((12, 13, 14, 15, 0))], 80, [a2], [])
+                    rows = [((lambda k=k, c0=c0: T.yf[8 * k:8 * k + 8, c0:c0 + 512]), (lambda row=row, a2=a2: T.WK[row:128:16, a2[1]:a2[2]]))
+                            for k, row in enumerate((12, 13, 14, 15, 0))]
+                    dma("S", rows[:3], 48, [a2], [])
+                    dma("A", rows[3:], 32, [a2], [])
         if r < 2:
             cp("A", VP, VN, None, 1.0, 0.0, AF.Abs)
             s2 = send([(helper(0), VP, S("vp", 0, 1024, 1, 144 * r, 144 * r + 128), "hv%d" % r)], 512)
             ops[s2]["soft"] += [s1] + ([free["F"]] if r else [])
-            arrive("aVf%d" % r, half, S("WF", 0, 1024), s2, 11.0)
-            arrive("aVp%d" % r, half, S("WF", 5120, 6144), s2, 11.0)
+            arrive("aVf%d" % r, half, S("WF", 0, 1024), s2, 8.0)
+            arrive("aVp%d" % r, half, S("WF", 5120, 6144), s2, 8.0)
     return ops, q
 
 
@@ -741,6 +771,7 @@ def schedule(ops):
         for i in sorted(set(ops[j]["deps"]) | set(ops[j]["soft"])):
             fwd[i].append((j, link(i, j)))
             bwd[j].append((i, link(i, j)))
+    fwd, bwd = fwd + [[len(x) for x in bwd]], bwd + [[len(x) for x in fwd]]
     flex = [len(o["dur"]) > 1 for o in ops]
     seed = [SEED]
 
@@ -764,7 +795,7 @@ def schedule(ops):
 
     best = None
     for it in range(ROUNDS):
-        eng = [o["eng"] if len(o["dur"]) == 1 else ("V" if it and rnd() < (0.1, 0.2, 0.3)[it % 3] else "A") for o in ops]
+        eng = [o["eng"] if len(o["dur"]) == 1 else o["eng"][0 if it and rnd() < (0.1, 0.2, 0.3)[it % 3] else 1] for o in ops]
         got = one_pass(ops, fwd, [-o["when"] for o in ops], (0.3, 0.6, 1.0, 1.5)[it % 4], eng)
         for k in range(3):
             if best is None or worth(got) < worth(best):
@@ -802,62 +833,68 @@ def schedule(ops):
     return best
 
 
-ROUNDS, TRIES, HEAT, SEED = 20, 6000, 0.5, 1
+ROUNDS, TRIES, HEAT, SEED = 12, 12000, 0.12, 1
 
 
 def one_pass(ops, succ, prio, slack, eng):
     n = len(ops)
-    left = [0] * n
-    for lst in succ:
-        for j, _ in lst:
-            left[j] += 1
-    free = {None: 0.0, "D": 0.0, "P": 0.0, "V": 0.0, "A": 0.0, "S": 0.0, "G": 0.0}
+    left = list(succ[n])
+    free = {None: 0.0, "P": 0.0, "V": 0.0, "A": 0.0, "S": 0.0, "G": 0.0}
     done, start, can, why = [0.0] * n, [0.0] * n, [0.0] * n, [None] * n
-    ready, soon, last = {e: [] for e in free}, {e: 1e9 for e in free}, {}
+    ready, soon, last = {e: [] for e in free}, {}, {}
+    moved, mover = 0.0, None
     for i in range(n):
         if left[i] == 0:
             ready[eng[i]].append(i)
             soon[eng[i]] = 0.0
     order = []
     for _ in range(n):
-        first, e = 1e9, None
+        first = 1e9
         for x, t in soon.items():
-            if t < 1e9:
-                if free[x] > t:
-                    t = free[x]
-                if t < first:
-                    first, e = t, x
+            if free[x] > t:
+                t = free[x]
+            if t < first:
+                first, e = t, x
         lst = ready[e]
-        i, top, bar = None, -1e18, first + slack
-        for x in lst:
-            if can[x] <= bar and prio[x] > top:
-                i, top = x, prio[x]
-        lst.remove(i)
-        soon[e] = min([can[x] for x in lst]) if lst else 1e9
+        if len(lst) == 1:
+            i = lst.pop()
+            del soon[e]
+        else:
+            top, bar, low, next_ = -1e18, first + slack, 1e9, 1e9
+            for x in lst:
+                t = can[x]
+                if t <= bar and prio[x] > top:
+                    i, top = x, prio[x]
+                if t < next_:
+                    low, next_ = (t, low) if t < low else (low, t)
+            lst.remove(i)
+            soon[e] = next_ if can[i] == low else low
         o = ops[i]
         est = can[i]
-        if e and free[e] > est:
+        if free[e] > est:
             est, why[i] = free[e], last[e]
         start[i] = est
         end = est + o["dur"][e]
-        if o["kind"] == "d":
-            t = free["D"] + o["dur"][e] - 1.8 - (o["hold"] if e == "G" else 0.0)
+        hold = o["hold"]
+        if hold is not None:
+            t = moved + o["dur"][e] - 1.8 - (hold if e == "G" else 0.0)
             if t > end:
-                end, why[i] = t, last["D"]
-            free["D"], last["D"] = end, i
+                end, why[i] = t, mover
+            moved, mover = end, i
+            free[e], last[e] = est + hold, i
+        elif e:
+            free[e], last[e] = end, i
         done[i] = end
-        if e:
-            free[e], last[e] = est + (o["dur"][e] if o["hold"] is None else o["hold"]), i
         order.append(i)
         for j, how in succ[i]:
-            t = est if how == 0 else end if how == 1 and eng[j] == e else end + WAKE
+            x = eng[j]
+            t = end + WAKE if how == 2 else est if how == 0 else end if x == e else end + WAKE
             if t > can[j]:
                 can[j], why[j] = t, i
             left[j] -= 1
-            if left[j] == 0:
-                x = eng[j]
+            if not left[j]:
                 ready[x].append(j)
-                if can[j] < soon[x]:
+                if can[j] < soon.get(x, 1e9):
                     soon[x] = can[j]
     return order, start, done, eng, why
 

from concourse.bass import DstId, RemoteDMATransfer
from concourse.mybir import AluOpType as ALU, ActivationFunctionType as AF

F32, BF, I32, U16 = "float32", "bfloat16", "int32", "uint16"
SCRATCH = {
    "WF": ("sbuf", [128, 10240], F32), "WB": ("sbuf", [128, 10240], F32),
    "XF": ("sbuf", [128, 8224], BF), "XB": ("sbuf", [128, 8224], BF),
    "PTf": ("sbuf", [128, 4096], BF), "PTb": ("sbuf", [128, 4096], BF), "PT2": ("sbuf", [128, 4096], BF),
    "AR": ("sbuf", [128, 4096], BF), "INV": ("sbuf", [128, 4096], BF), "GB": ("sbuf", [128, 8224], BF),
    "IB": ("sbuf", [128, 1024], I32), "IS": ("sbuf", [128, 448], I32),
    "CU": ("sbuf", [128, 1024], U16), "OF": ("sbuf", [128, 640], U16),
    "WK": ("sbuf", [128, 3072], F32), "GAP": ("sbuf", [128, 3072], F32), "VAL": ("sbuf", [128, 3072], F32),
    "LL": ("sbuf", [128, 2048], BF), "BA": ("sbuf", [128, 720], BF), "BC": ("sbuf", [128, 144], BF),
    "RM": ("sbuf", [128, 304], BF), "PM": ("sbuf", [128, 2048], BF), "ID": ("sbuf", [128, 512], F32),
    "Q": ("sbuf", [128, 1024], F32), "COL": ("sbuf", [128, 48], F32), "EPS": ("sbuf", [128, 4], F32),
    "ST": ("sbuf", [128, 576], F32), "SB": ("sbuf", [128, 3712], BF),
    "xd": ("dram", [128, 4096], BF), "xe": ("dram", [160, 4096], BF),
    "vp": ("dram", [288, 1024], F32),
}
for _b in range(8):
    SCRATCH["PS%d" % _b] = ("psum", [128, 512], F32)
ARRIVALS = (["aXh", "aXF0", "aXF1", "aXB0", "aXB1", "sB", "sL", "sC"]
            + ["aPT%s%d" % (t, h) for t in "fb" for h in range(4)] + ["aPT2"]
            + ["a%s%d%d" % (t, r, h) for t in ("Lf", "Lb", "Vb", "Vn") for r in range(2) for h in range(2)]
            + ["aV%s%d" % (t, r) for t in "fp" for r in range(2)])
HANDED = ["h0", "h1", "hF", "hv0", "hv1", "hw0", "hw1"]
SEMAPHORES = ["cP", "cV", "cA", "cG"] + ARRIVALS + HANDED + ["d%d" % i for i in range(60)]

TINY = 2.0 ** -48
ROOT = 2.0 ** 52


def S(name, lo, hi, step=1, p0=0, p1=128, ps=1):
    return (name, lo, hi, step, p0, p1, ps)


def D3(name, t, p0=0, p1=128, ps=1):
    return (name, t, t + 1, 0, p0, p1, ps)


def width(s):
    return (s[2] - s[1] + s[3] - 1) // s[3]


def sub(s, a, w, step=1):
    return (s[0], s[1] + a, s[1] + a + (w - 1) * step + 1, step) + s[4:]


def part(s, p0, p1):
    return s[:4] + (p0, p1, 1)


def helper_of(T, topo, rank):
    free = [c for c in topo.cores_of(T.cores[0]) if T.rank_of(c) is None]
    out = []
    for c in T.cores:
        far = [h for h in free if h not in out and topo.die(h) != topo.die(c)] or [h for h in free if h not in out]
        out.append(far[0])
    return out[rank]


def pair_masks(topo, src, a, b):
    ea, eb = topo.engines(src, a), topo.engines(src, b)
    return sum(1 << e for e in ea[0::2]), sum(1 << e for e in eb[1::2]), len(ea[0::2]), len(eb[1::2])


def dst_id(topo, c):
    rid, pid, _ = topo.addr(c)
    return DstId(rid=rid, pnc=pid)


def helper_program(g, core, T, topo, rank):
    n = len(T.cores)
    lo, hi, far = T.cores[(rank - 1) % n], T.cores[(rank + 1) % n], T.cores[(rank + 2) % n]
    full = len(topo.engines(T.cores[rank], core))
    x = T.xe
    g.sync.wait_ge(T.sem.aXh, full)
    g.sync.dma_start(x[0:16, :], x[128:144, :]).then_inc(T.sem.h0, 16)
    g.sync.dma_start(x[144:160, :], x[16:32, :]).then_inc(T.sem.h0, 16)
    g.wait_ge(T.sem.aXh, full)
    sent = 0
    for k, (c, w, v, row) in enumerate(((hi, "B", 0, 16), (far, "B", 1, 0), (lo, "F", 0, 16), (far, "F", 1, 32))):
        if k == 1:
            g.wait_ge(T.sem.h0, 32)
        rid, pid, _ = topo.addr(c)
        g.remote_dma(T["X" + w][:, 16 + 4112 * v:4112 + 4112 * v], x[row:row + 128, :], T.sem["aX%s%d" % (w, v)], T.sem.h1, pid, rid, topo.mask(core, c))
        sent += len(topo.engines(core, c))
    for r in range(2):
        x, top = T.vp, 144 * r
        g.sync.wait_ge(T.sem["hv%d" % r], full)
        g.sync.dma_start(x[top + 128:top + 144, :], x[top:top + 16, :]).then_inc(T.sem["hw%d" % r], 16)
        g.wait_ge(T.sem["hw%d" % r], 16)
        if r:
            g.wait_ge(T.sem.hF, 2)
        ma, mb, na, nb = pair_masks(topo, core, lo, far)
        g.remote_dma_fused([RemoteDMATransfer(dst_ids=[dst_id(topo, c)], dma_engine_mask=m, remote_sem=T.sem[s % r], src=x[top + row:top + row + 128, :],
                                              dst=T.WF[:, o:o + 1024])
                            for c, m, s, row, o in ((lo, ma, "aVf%d", 0, 0), (far, mb, "aVp%d", 16, 5120))], local_sem=T.sem.h1)
        sent += na + nb
    g.wait_ge(T.sem.h1, sent)


WAKE = 0.22
CY, PE, GATHER, SCATTER = 0.00086, 0.00045, 1.45, 3.5
BY_TENSOR = [(0, 1, 1), (0, 0, 0), (0, 0, 1)]
SPLIT = True
BY_DMA = {"B": (4, 4), "F": (4, 0)}
RATE = (310.0, 225.0)
START = (32.0, 68.0, 106.0)


def build(g, core, T, topo, rank):
    n = len(T.cores)
    lo, hi, far = T.cores[(rank - 1) % n], T.cores[(rank + 1) % n], T.cores[(rank + 2) % n]
    ops = []
    acc = {}
    nsem, now = [0], [0.0]
    q = {"P": g.tensor, "V": g.vector, "A": g.scalar, "S": g.sync, "G": g}

    def ap(s):
        if s[3] == 0:
            return T[s[0]][s[1], s[4]:s[5]:s[6], :] if (s[4], s[5], s[6]) != (0, 128, 1) else T[s[0]][s[1]]
        return T[s[0]][s[4]:s[5]:s[6], s[1]:s[2]:s[3]]

    def ind(win, off):
        return ap(win).indirect(ap(off))

    def add(eng, dur, emit, reads, writes, kind="c", sem=None, cnt=0, after=(), hold=None):
        i = len(ops)
        deps = {}
        for s, mode in [(s, "r") for s in reads] + [(s, "w") for s in writes]:
            for (l, h, m, j, k) in acc.get(s[0], []):
                if l < s[2] and s[1] < h and (m == "w" or mode == "w") and j != i and not (k == s[3] > 1 and (l - s[1]) % k):
                    deps[j] = True
        for s in list(reads) + list(writes):
            if s[0].startswith("PS"):
                j = acc.get("lock" + s[0])
                if j is not None and j != i:
                    deps[j] = deps.get(j, False)
                acc["lock" + s[0]] = i
        for s in writes:
            full = s[3] <= 1 and (s[4], s[5], s[6]) == (0, 128, 1)
            if full:
                acc[s[0]] = [e for e in acc.get(s[0], []) if not (s[1] <= e[0] and e[1] <= s[2])]
            acc.setdefault(s[0], []).append((s[1], s[2], "w", i, s[3]))
        for s in reads:
            acc.setdefault(s[0], []).append((s[1], s[2], "r", i, s[3]))
        for j in after:
            deps[j] = True
        ops.append({"eng": eng, "dur": dur, "emit": emit, "deps": deps, "kind": kind, "sem": sem, "cnt": cnt,
                    "hold": hold, "soft": [], "when": now[0]})
        now[0] += 0.001
        return i

    def at(t):
        now[0] = t

    def new_sem():
        nsem[0] += 1
        return "d%d" % (nsem[0] - 1)

    def is2(s):
        return SCRATCH[s[0]][2] in (BF, U16)

    def cost(c, k, e="V"):
        return (0.055 if e == "V" else 0.07) + max(64, c * k) * CY

    def cols(x):
        return [x] if isinstance(x, tuple) else []

    def val(x):
        return ap(x) if isinstance(x, tuple) else x

    def ts(out, in0, s1, op0, s2=None, op1=None, off=None):
        def emit(e):
            a = ind(in0, off) if off else ap(in0)
            if op1 is None:
                return g.vector.tensor_scalar(ap(out), a, val(s1), None, op0)
            return g.vector.tensor_scalar(ap(out), a, val(s1), val(s2), op0, op1)
        c = GATHER if off else (0.5 if is2(out) and is2(in0) else 1)
        return add("V", {"V": cost(c, width(out))}, emit, [in0] + cols(s1) + cols(s2) + cols(off), [out])

    def tt(out, in0, in1, op, off=None):
        def emit(e):
            return g.vector.tensor_tensor(ap(out), ind(in0, off) if off else ap(in0), ap(in1), op)
        c = 2 if not (in0[0].startswith("PS") or in1[0].startswith("PS")) else 1
        return add("V", {"V": cost(GATHER if off else c, width(out))}, emit, [in0, in1] + cols(off), [out])

    def cp(eng, out, in_, off=None, a=1.0, b=0.0, func=None, after=()):
        def emit(e):
            x = ind(in_, off) if off else ap(in_)
            if e == "V":
                if func == AF.Relu:
                    return g.vector.tensor_scalar(ap(out), x, val(b), 0.0, ALU.add, ALU.max)
                if a == 1.0 and b == 0.0:
                    return g.vector.tensor_copy(ap(out), x)
                return g.vector.tensor_scalar(ap(out), x, val(a), val(b), ALU.mult, ALU.add)
            if b != 0.0:
                return g.scalar.activation(ap(out), x, func or AF.Identity, bias=val(b), scale=val(a))
            if a != 1.0:
                return g.scalar.activation(ap(out), x, func or AF.Copy, scale=val(a))
            return g.scalar.activation(ap(out), x, func or AF.Copy)
        dur = {e: cost(GATHER if off else (0.5 if e == "V" and is2(out) and is2(in_) else 1), width(out), e) for e in eng}
        return add(eng, dur, emit, [in_] + cols(off) + cols(a) + cols(b), [out], after=after)

    def mset(out, v):
        return add("V", {"V": cost(0.5 if is2(out) else 1, width(out))}, lambda e: g.vector.memset(ap(out), v), [], [out])

    def iota(out, pat, base, cm):
        return add("G", {"G": 0.15 + width(out) * 2 * CY}, lambda e: g.iota(ap(out), pat, base, cm), [], [out])

    def asel(out, pat, base, cm, in_=None):
        return add("G", {"G": 0.2 + width(out) * 2 * CY},
                   lambda e: g.affine_select(ap(out), ap(in_ or out), pat, ALU.is_equal, 0.0, base, cm), [in_ or out], [out])

    def mm(items, first=True, last=True):
        def emit(e):
            r = None
            for k, (o, l, x) in enumerate(items):
                r = g.tensor.matmul(ap(o), ap(l), ap(x), first and k == 0, last and k == len(items) - 1)
            return r
        rd = sorted({s for it in items for s in it[1:3]})
        wr = sorted({it[0] for it in items})
        i = add("P", {"P": 0.03 + sum(max(64, width(x)) * (1 if is2(x) else 4) * PE for (_, _, x) in items)}, emit, rd, wr)
        for j in ops[i]["deps"]:
            ops[i]["deps"][j] = ops[i]["deps"][j] and (first or ops[j]["eng"] != "P")
        return i

    def flip(out, in_):
        return add("V", {"V": cost(0.5 if is2(out) else 1, width(out))}, lambda e: g.vector.transpose(ap(out), ap(in_)), [in_], [out])

    def dma(eng, items, kb, reads, writes, after=()):
        sem = new_sem()

        def emit(e):
            for (o, x) in items:
                q[eng].dma_start(o(), x()).then_inc(T.sem[sem], 16)
        return add(eng, {eng: 1.8 + kb / RATE[0]}, emit, reads, writes, "d", sem, 16 * len(items), after,
                   hold=(1.0 if eng == "G" else 0.07) * len(items))

    def sdma(eng, pairs, kb, after=()):
        return dma(eng, [((lambda o=o: ap(o)), (lambda x=x: ap(x))) for (o, x) in pairs], kb,
                   [x for (_, x) in pairs], [o for (o, _) in pairs], after)

    def send(items, kb, after=(), hold=0.35):
        sem = new_sem()
        if items[0][1] is None:
            masks, cnt = [1 << topo.engines(core, it[0])[k] for k, it in enumerate(items)], len(items)
        elif len(items) == 2:
            ma, mb, na, nb = pair_masks(topo, core, items[0][0], items[1][0])
            masks, cnt = [ma, mb], na + nb
        else:
            masks, cnt = [topo.mask(core, items[0][0])], len(topo.engines(core, items[0][0]))

        def emit(e):
            g.remote_dma_fused([RemoteDMATransfer(dst_ids=[dst_id(topo, c)], dma_engine_mask=m, remote_sem=T.sem[rs], src=ap(s), dst=ap(d))
                                if s else RemoteDMATransfer(dst_ids=[dst_id(topo, c)], dma_engine_mask=m, remote_sem=T.sem[rs])
                                for (c, s, d, rs), m in zip(items, masks)], local_sem=T.sem[sem])
        return add("G", {"G": 1.8 + hold + kb / RATE[1]}, emit, [it[1] for it in items if it[1]], [], "d", sem, cnt, after, hold=hold)

    helper = lambda d: helper_of(T, topo, (rank + d) % n)
    half = len(topo.engines(core, lo)[0::2])
    whole = len(topo.engines(core, far))

    def arrive(sem, cnt, piece, like, lag=0.3):
        i = add(None, {None: lag}, None, [], [piece] if piece else [], "a", sem, cnt)
        ops[i]["soft"].append(like)
        return i

    PS = lambda b, l=0, h=512, step=1: S("PS%d" % b, l, h, step)
    X0, X1, X2, U0, U1, T0, T1, VB = range(8)
    col = lambda j: S("COL", j, j + 1)
    sb = lambda a, w: S("SB", a, a + w)
    st = lambda a, w: S("ST", a, a + w)
    gb = lambda a, w=1024: S("GB", a, a + w)
    H, P1, P2, QB, RR, UV = sb(0, 128), [sb(128, 256), sb(384, 256)], sb(640, 256), sb(896, 640) , sb(1536, 768), sb(2304, 256)
    FL, FLO, MSG, MISS = sb(2560, 256), sb(2816, 256), sb(3072, 256), [sb(3328, 64), sb(3392, 64)]
    OK, WON, PEN, ONE = sb(3456, 64), sb(3520, 64), sb(3584, 64), sb(3648, 64)
    T1A, JJ = st(0, 512), st(512, 64)
    AA, JC, DN, TM = S("IB", 0, 256), S("IB", 256, 384), S("IB", 384, 512), S("IB", 512, 576)
    OFS, OFT = S("CU", 0, 512), S("CU", 512, 1024)
    OC1, OC2, OSP, ONB, OMS, ONS, OGI = [S("OF", a, b) for a, b in (
        (0, 128), (128, 256), (256, 384), (384, 576), (576, 640), (384, 448), (576, 640))]
    LTF, LTB, GC, LTO, GNB, LE = 0, 1040, 2080, 4128, 5152, 7200
    MSI = S("IS", 0, 64)
    FB = S("SB", 1536, 2560)
    ID, HALF, LESS = S("ID", 0, 128), S("ID", 256, 384), S("ID", 384, 512)
    pm = lambda k: S("PM", 128 * k, 128 * k + 128)
    moved = lambda k, var: S("PM", 256 * k + (112, 0, 16)[var], 256 * k + (112, 0, 16)[var] + 128)
    UP, EYE, DOWN = [moved(0, var) for var in range(3)]

    l0 = dma("S", [(lambda: ap(MSI), lambda: T.ms[:])], 32, [], [MSI])
    lc = dma("S", [(lambda: T.IB[:], lambda: T.cor[:])], 512, [], [S("IB", 0, 1024)])
    lx = dma("S", [(lambda: T.xd[:], lambda: T.x[:])], 1024, [], [S("xd", 0, 4096)])
    ops[lc]["soft"].append(l0)
    ops[lx]["soft"].append(lc)
    early = [cp("V", S("CU", 512 * i, 512 * i + 512), S("IB", 512 * i, 512 * i + 512)) for i in range(2)]
    dma("S", [(lambda: T.IB[:], lambda: T.fl[:])], 512, [], [S("IB", 0, 1024)])
    at(9)
    cf = cp("V", FB, S("IB", 0, 1024))
    at(0)
    dma("S", [(lambda: T.EPS[:, 0:1], lambda: T.eps[:])], 1, [], [S("EPS", 0, 1)])
    sx = send([(helper(0), S("xd", 0, 4096), S("xe", 0, 4096, 1, 16, 144), "aXh")], 1024, hold=5.0)
    for k, (t, v) in enumerate((("B", 0), ("B", 1), ("F", 0), ("F", 1))):
        arrive("aX%s%d" % (t, v), whole, S("X" + t, 16 + 4112 * v, 4112 + 4112 * v), sx, 11 + 4.5 * k)

    pc = S("IS", 64, 65)
    iota(pc, [[0, 1]], 0, 1)
    iota(S("IS", 192, 448), [[1, 16], [0, 16]], 0, 0)
    iota(S("IS", 128, 192), [[0, 4], [1, 16]], 0, 0)
    iota(S("IS", 80, 97), [[16, 17]], -64, 0)
    ts(S("IS", 66, 67), pc, 15, ALU.bitwise_and)
    cp("V", col(8), S("IS", 66, 67))
    ts(col(0), col(8), 5.0, ALU.is_lt)
    ts(col(1), col(8), 5.0, ALU.is_ge)
    ts(S("COL", 24, 41), S("IS", 80, 97), col(0), ALU.mult)
    step = lambda v: col(24 + (v + 64) // 16)
    ts(col(3), col(8), 6.0, ALU.not_equal, col(1), ALU.mult)
    ts(col(2), col(8), 6.0, ALU.is_equal, step(-64), ALU.add)
    ts(S("INV", 256, 320), S("IS", 128, 192), col(3), ALU.mult)
    for j in range(2):
        cp("V", S("INV", 256 + (64 << j), 256 + (128 << j)), S("INV", 256, 256 + (64 << j)))
    ts(PS(0, 0, 256), S("IS", 192, 448), col(0), ALU.mult)
    tt(S("INV", 0, 256), PS(0, 0, 256), S("INV", 256, 512), ALU.add)
    LC = gb(LE)
    cp("V", S("INV", 256, 512), S("INV", 0, 256), None, 1.0, step(16))
    cp("V", S("INV", 512, 1024), S("INV", 0, 512), None, 1.0, step(32))
    for j in range(1, 4):
        cp("AV", S("INV", 1024 * j, 1024 * j + 1024), S("INV", 0, 1024), None, 1.0, step(64 * j))
    cp("VA", LC, S("INV", 0, 1024), None, 1.0, col(2))
    cp("V", OMS, MSI)
    sc = add("V", {"V": cost(SCATTER, 1024)}, lambda e: g.vector.tensor_copy(ind(S("INV", 0, 4096), OMS), ap(LC)), [LC, OMS], [S("INV", 0, 4096)])
    ops[sc]["soft"] += early
    ops[cf]["soft"].append(sc)
    ones = lambda w: S("BA", 0, w)
    mset(ones(720), 1.0)
    keep = lambda i: sb(2560 + 128 * i, 128)
    asel(S("PM", 0, 256), [[0, 2], [-1, 128]], 0, 1, ones(256))
    asel(sb(2560, 512), [[-1000, 4], [-8, 16], [999, 8]], 0, 1, ones(512))
    asel(sb(3200, 512), [[-1, 4], [-4, 8], [-32, 16]], 384, 1, ones(512))
    ts(col(4), col(8), 4.0, ALU.is_ge)
    ts(col(4), col(8), 7.0, ALU.is_lt, col(4), ALU.mult)
    cp("VA", keep(4), EYE, None, col(4))
    stage = (LTB, LTF, GC, GC + 1024, LTO, GNB, GNB + 1024, LE)
    last, laid = [], []
    for k in range(4):
        a, b = 1024 * k, 1024 * k + 1024
        made = []
        at(7 + k)
        for h in range(2):
            mm([(PS(2 * k + h), keep(4), S("INV", a + 512 * h, a + 512 * h + 512))], True, False)
        at(8 + 3 * k)
        for i in range(4):
            c = stage[(4 * k + i) % 8]
            made.append(cp("VA"[i % 2], gb(c), S("INV", 0, 4096), S("CU", 256 * i + 64 * k, 256 * i + 64 * k + 64)))
            ops[made[i]]["soft"] += last + (laid[-2:][i % 2:i % 2 + 1] if i > 1 else [])
            for h in range(2):
                if i == 2:
                    mm([(PS(2 * k + h), keep(5 + k), sub(FB, 512 * h, 512))], False, False)
                mm([(PS(2 * k + h), keep(i), gb(c + 512 * h, 512))], False, i == 3)
        for h in range(2):
            laid.append(cp("VA"[h], S("AR", a + 512 * h, a + 512 * h + 512), PS(2 * k + h)))
        last = made[2:]
        land = lambda t: S(t, a, b)
        s1 = send([(hi, land("AR"), land("PTb"), "aPTb%d" % k), (lo, land("AR"), land("PTf"), "aPTf%d" % k)], 512)
        arrive("aPTf%d" % k, half, land("PTf"), s1)
        arrive("aPTb%d" % k, half, land("PTb"), s1)
    s2 = send([(far, S("AR", 0, 4096), S("PT2", 0, 4096), "aPT2")], 1024)
    ops[s2]["soft"].append(s1)
    arrive("aPT2", whole, S("PT2", 0, 4096), s2)

    at(20)
    mset(S("ID", 0, 256), 1.0)
    asel(S("ID", 0, 256), [[0, 2], [-1, 128]], 0, 1)
    cp("VA", HALF, ID, None, 0.5)
    cp("VA", LESS, ID, None, -0.5)
    EM, RT = sb(896, 128), [S("RM", 32 * v, 32 * v + 32) for v in range(3)]
    RH, RO, RC = S("RM", 96, 128), S("RM", 128, 160), S("RM", 160, 168)
    asel(EM, [[-1, 16], [-16, 8]], 0, 1, ones(128))
    cp("VA", RT[1], sub(EM, 0, 32), None, 16.0)
    tt(RT[1], RT[1], sub(EM, 64, 32), ALU.add)
    mm([(PS(X2, 0, 32), DOWN, RT[1]), (PS(X2, 64, 96), UP, RT[1])])
    for v in (0, 2):
        cp("VA", RT[v], PS(X2, 32 * v, 32 * v + 32))
    ts(RC, sub(EM, 48, 8), -512.0, ALU.mult)
    tt(RC, RC, sub(EM, 32, 8), ALU.add)
    ts(RC, RC, 16.0, ALU.mult)
    tt(RC, RC, sub(EM, 40, 8), ALU.add)
    cp("VA", RH, sub(EM, 0, 32), None, -1.0)
    cp("VA", RO, sub(EM, 96, 32))
    RF, TWO = S("RM", 168, 176), S("RM", 176, 240)
    cp("VA", RF, sub(EM, 0, 8))
    tt(TWO, sub(EYE, 0, 64), sub(EYE, 64, 64), ALU.add)
    cp("VA", S("PM", 256, 512), S("PM", 0, 256), None, 64.0)
    scaled = {64.0: pm(2), 1.0: EYE}
    for k, v in enumerate((-1.0, -16.0, 0.5, -0.5, 0.25, 0.1875, 512.0, 4.0)):
        scaled[v] = pm(4 + k + 4 * (k // 7))
        cp("VA", scaled[v], EYE, None, v)
    ts(S("IS", 68, 69), pc, 16, ALU.bitwise_and)
    ts(S("IS", 74, 75), pc, 4, ALU.arith_shift_right)
    ts(col(9), S("IS", 68, 69), 0, ALU.is_equal)
    ts(col(10), S("IS", 68, 69), 16, ALU.is_equal)
    cp("V", col(11), S("IS", 74, 75))
    SWAP = [pm(11 + k) for k in range(4)]
    for k, (m, c) in enumerate(((EYE, 9), (UP, 9), (DOWN, 10), (EYE, 10))):
        cp("VA", SWAP[k], m, None, col(c))
    ki = S("IS", 192, 256)
    iota(ki, [[1, 64]], 0, 0)
    ts(JJ, ki, 16.0, ALU.mult, col(8), ALU.add)
    ts(sub(JC, 0, 64), JJ, GC + 1024 - LTF - 8192.0, ALU.add)
    ts(sub(JC, 64, 64), JJ, GC - LTB - 8192.0, ALU.add)
    mset(S("BC", 0, 144), 0.0)
    ts(S("BC", 16, 144, 16), sub(ki, 0, 8), col(11), ALU.is_equal)
    for j in range(4):
        asel(S("LL", 512 * j, 512 * j + 512), [[-1, 4], [-16, 8], [0, 16]], -4 * j, 1, ones(512))
    mset(ones(720), 0.25)
    ROUND = S("RM", 240, 304)
    mset(ROUND, -0.375)
    asel(S("BA", 0, 144), [[-16, 9], [1000, 16]], 16, 1)
    asel(S("BA", 144, 720), [[-1, 4], [-16, 9], [1000, 16]], 4, 1)
    mset(ONE, 1024.0)
    mset(S("COL", 16, 24), ROOT)
    for j, v in enumerate((-8.0, -64.0, 16.0)):
        cp("VA", col(12 + j), col(16), None, v * ROOT)
    for a in (0, 8, 4112, 4120):
        cp("VA", S("XF", a, a + 8), S("COL", 16, 24), None, ROOT)
        cp("VA", S("XB", a, a + 8), S("COL", 16, 24), None, -ROOT)
    for a in (LTB, LTF):
        mset(gb(a + 1024, 16), 0.0)
    m1, m2, m3 = S("IS", 256, 320), S("IS", 320, 384), S("IS", 384, 448)
    ts(m1, MSI, 63, ALU.bitwise_and)
    ts(m2, MSI, 6, ALU.arith_shift_right)
    ts(sub(H, 0, 128), S("IS", 256, 384), 4.0, ALU.mult)
    ts(m2, MSI, 4032, ALU.bitwise_and)
    for r, d in ((0, 1.0), (2, 63.0)):
        ts(m3, m1, d, ALU.add)
        ts(m3, m3, 63, ALU.bitwise_and)
        tt(m3, m3, m2, ALU.add)
        cp("V", sub(ONB, 64 * r, 64), m3)
    ts(m3, MSI, 64.0, ALU.add)
    ts(m3, m3, 4095, ALU.bitwise_and)
    cp("V", sub(ONB, 64, 64), m3)

    def turn(bank, src, rhs, qoff, b=0.0, func=None):
        nq, m = width(rhs) // 8, width(src) // 16
        mm([(part(PS(bank, s, nq * 128, 16), 0, m), sub(src, s, m, 16), rhs) for s in range(16)])
        cp("VA", S("Q", qoff, qoff + nq * 128, 1, 0, m), part(PS(bank, 0, nq * 128), 0, m), None, 1.0, b, func)

    QS = S("INV", 3072, 3584)

    def small(bank, src, rhs):
        nq, m = width(rhs) // 8, width(src) // 16
        mm([(part(PS(bank, s, nq * 128, 16), 0, m), sub(src, s, m, 16), rhs) for s in range(16)])
        cp("VA", part(sub(QS, 0, nq * 128), 0, m), part(PS(bank, 0, nq * 128), 0, m))

    def back(out, qoff, j, w, m=128):
        return (out, S("Q", qoff + 128 * j, qoff + 128 * j + 128, 1, 0, m), part(sub(ID, 64 * w, 64), 0, m))

    def pick(out, k, src):
        return [(out, S("BA", k * 144 + 16 - s, k * 144 + 144 - s), sub(src, s, 64, 16)) for s in range(16)]

    def spread(bank, lst):
        return [(PS(bank, s, 512, 16), S("LL", 128 * s, 128 * s + 128), lst) for s in range(16)]

    def opened(bank):
        mm([(PS(bank), S("LL", 0, 128), S("LL", 0, 512))], True, False)

    def place_of(qb, var, bank, out):
        mm([(sub(bank, 64 * w, 64), moved(k, var), sub(qb, 128 * w + 64 * k, 64)) for w in range(width(out) // 64) for k in range(2)])
        ts(out, bank, -12480.0, ALU.add)

    def visit1(r, flows):
        p1 = P1[r % 2]
        mm([(PS(VB, 128 * w, 128 * w + 128), EYE, H) for w in range(2)] + [(PS(VB, 64 * j, 64 * j + 64),) + flows[j] for j in range(4)])
        ts(p1, PS(VB, 0, 256), 0.0, ALU.max, 255.0, ALU.min)
        cp("VA", sub(QB, 0, 256), p1, None, 0.25, 191.625)
        place_of(sub(QB, 0, 256), 1, PS(VB, 256, 384), OC1)
        for w in (1, 0):
            cp("VA" if r or not w else "AV", gb(GC + 1024 - 1024 * w), S(("PTf", "PTb")[w], 0, 4096), sub(OC1, 64 * w, 64))
        both = gb(GC, 2048)
        if r:
            turn(X0, both, RT[1], 0, 1024.0)
            turn(X1, both, RC, 512, 1024.0)
            mm([back(PS(X1, 128 + 64 * w, 192 + 64 * w), 512, 0, 1 - w) for w in range(2)])
            tt(PS(X1, 128, 256), PS(X1, 128, 256), JC, ALU.min)
            ts(OSP, PS(X1, 128, 256), 8192.0, ALU.add)
        else:
            at(START[0] + 1.5)
            turn(X0, both, RT[1], 0, 16.0, AF.Relu)
            turn(X1, both, RH, 512, 0.0, AF.Relu)
        mm([back(PS(X0, 256 * w + 64 * i, 256 * w + 64 * i + 64), 0, i, 1 - w) for w in range(2) for i in range(4)])
        cp("VA", T1A, PS(X0), None, 1.0, 0.0 if r else -4112.0)
        if r:
            ts(OFS, PS(X0), 1024.0, ALU.min)

    def visit2(r, w, t0):
        bp, ba, bt, cnt, br, by = ((PS(X0, 0, 192), X1, PS(X0, 256, 512), PS(X2, 0, 64), PS(X1, 0, 384), PS(X2, 128, 384)),
                                   (PS(U0, 0, 192), U1, PS(T0, 0, 256), PS(T1, 0, 64), PS(U0, 0, 384), PS(T1, 128, 384)))[w]
        bc = (PS(X1, 0, 64), PS(U1, 0, 64))[w]
        p1, p2, rr = sub(P1[r % 2], 128 * w, 128), sub(P2, 128 * w, 128), sub(RR, 384 * w, 384)
        lt = (LTF, LTB)[w]
        o = gb(GC + 1024 - 1024 * w)
        reads = []
        if r:
            o = S("INV", 1024 * w, 1024 * w + 1024)
            at(t0 + 1.5 * (1 - w))
            reads.append(cp("AV", o, S("GB", lt, GC + 2048 - 1024 * w), sub(OSP, 64 * w, 64)))
        at(t0 + (8, 1)[w])
        start = [(sub(bp, 0, 128), scaled[0.25], p1)] + [(sub(bp, 64 * j, 64), m, x) for j in range(2) for m, x in ((scaled[0.1875], ONE), (EYE, ROUND))]
        if w or not r:
            mm(start, True, False)
            mm(pick(sub(bp, 0, 64), 1 + 2 * w, o) + pick(sub(bp, 64, 64), 2 + 2 * w, o), False, True)
        else:
            small(X0, o, sub(RO, 0, 16))
            mm(start + [(sub(bp, 64 * j, 64), part(sub(QS, 128 * j, 128), 0, 64), part(sub(scaled[0.25], 0, 64), 0, 64)) for j in range(2)])
        ts(sub(QB, 256 + 128 * w, 128), sub(bp, 0, 128), 191.625, ALU.max, 255.375, ALU.min)
        ts(p2, sub(bp, 0, 128), 255.375, ALU.min, -191.625, ALU.add)
        place_of(sub(QB, 256 + 128 * w, 128), 2 * w, bc, sub(OC2, 64 * w, 64))
        g2 = S("XB", 1024 * w, 1024 * w + 1024) if r else gb((LE, LTO)[w])
        cp(("VA", "AV")[w], g2, S("PT2", 0, 4096), sub(OC2, 64 * w, 64))
        if r:
            for i in range(4):
                o = S("XF", 4096 * w + 1024 * i, 4096 * w + 1024 * i + 1024)
                at(t0 + ((5, 9, 11, 13), (0, 1.5, 3, 4.5))[w][i])
                reads.append(cp("VA" if (w, i) != (1, 1) else "AV", o, gb(lt, 1040), sub(OFS, 256 * w + 64 * i, 64)))
                if w:
                    mm(pick(cnt, 0, o), i == 0, i == 3)
                elif i % 2:
                    mm([(PS(X2, s, 128, 16), S("XF", 1024 * i - 1024 + s, 1024 * i + 1024, 16), RF) for s in range(16)], i == 1, i == 3)
            if w == 0:
                cp("VA", S("INV", 3584, 3712), PS(X2, 0, 128))
                mm([(cnt, S("INV", 3584, 3712), TWO)])
            at(t0 + (12, 4)[w])
            turn(ba, g2, RT[2 - 2 * w], 512, 6144.0)
        else:
            mm([back(cnt, 512, i, 1 - w) for i in range(4)])
            turn(ba, g2, RT[2 - 2 * w], (512, 0)[w], 16.0, AF.Relu)
        cp("A", OK, cnt, None, -4096.0, 1024.0, AF.Relu)
        mm([it for i in range(4) for it in (back(sub(bt, 64 * i, 64), 512 if r or not w else 0, i, 0, 64), (sub(bt, 64 * i, 64), scaled[-16.0], OK))])
        tt(bt, bt, sub(T1A, 256 * w, 256), ALU.max)
        ts(sub(OFT, 256 * w, 256), bt, 0.0 if r else 4112.0, ALU.add)
        at(t0 + (12, 3.5)[w])
        mm([(sub(br, 128 * j, 128), scaled[4.0 if j == 1 else 1.0], x) for j, x in enumerate((p1, p2, H))]
           + [(sub(br, 64 * j, 64), scaled[-1.0 if j // 2 == 1 else 1.0], OK) for j in range(6)]
           + [(sub(br, 128 + 64 * j, 64), EYE, ONE) for j in range(2)])
        cp("VA", rr, br, None, 1.0, -1024.0, AF.Relu)
        qe = sub(QB, 512, 128)
        mm([(sub(by, 0, 128), EYE, sub(rr, 128 * j, 128)) for j in range(2)])
        cp("VA", qe, sub(by, 0, 128), None, 0.25, 191.625)
        mm([(sub(by, 128, 128), scaled[0.25], sub(rr, 128 * j, 128)) for j in range(2)] + [(sub(by, 128, 128), scaled[-1.0], qe)]
           + [(sub(by, 128 + 64 * j, 64), scaled[0.1875], ONE) for j in range(2)])
        cp("VA", sub(UV, 128 * w, 128), sub(by, 128, 128), None, 1.0, TINY)
        if w == 0:
            cp("VA", sub(UV, 64, 32), sub(UV, 64, 32), None, 0.5)
        return reads

    def lanes_table(bank, hf, flag):
        items = []
        for row, x in [(0, sub(flag, 32 * hf, 32))] + [(12 + j, sub(MSG, 128 * hf + j, 32, 4)) for j in range(4)]:
            for k in range(4):
                items.append((PS(bank, row + 16 * (k // 2), 512, 32), SWAP[k], sub(x, (k % 2) * x[3], 16, 2 * x[3])))
        mm(items)

    def next_flows(o):
        small(VB, o, RO)
        mm([(PS(VB, j, 256, 4), part(sub(QS, 128 * j, 128), 0, 64), part(sub(EYE, 0, 64), 0, 64)) for j in range(4)])
        cp("VA", FLO, PS(VB, 0, 256))

    at(23)
    cp("AV", S("INV", 2048, 3072), S("AR", 0, 4096), OMS)
    small(X1, S("INV", 2048, 3072), RO)
    visit1(0, [(part(sub(QS, 128 * j, 128), 0, 64), part(sub(EYE, 0, 64), 0, 64)) for j in range(4)])
    at(40)
    cp("VA", gb(GNB), S("AR", 0, 4096), sub(ONB, 0, 64))
    next_flows(gb(GNB))
    casts = []
    VN, VP = S("VAL", 1024, 2048), S("VAL", 2048, 3072)
    for r in range(3):
        t0 = START[r]
        visit2(r, 1, t0)
        if r == 0:
            for t in "BF":
                for k in range(2):
                    wide = lambda a, b: (S("W" + t, 5120 * k + 1024 + 1024 * a, 5120 * k + 1024 + 1024 * b), S("X" + t, 4112 * k + 16 + 1024 * a, 4112 * k + 16 + 1024 * b))
                    if BY_DMA[t][k]:
                        sw = sdma("G", [wide(0, BY_DMA[t][k])], 512 * BY_DMA[t][k])
                        ops[sw]["soft"].append(s2)
                        s2 = sw
                    for j in range(BY_DMA[t][k], 4):
                        at(t0 + 26 + j + 4 * k)
                        casts.append(cp("VA", *wide(j, j + 1)))
        else:
            at(t0 - 2)
            tt(TM, sub(DN, 64 * (r - 1), 64), MISS[r - 1], ALU.mult)
            tt(TM, TM, JJ, ALU.add)
            cp("V", ONS, TM)
            o = S("INV", 2048, 3072)
            cp("VA", o, gb(LTO, 3072), ONS)
            next_flows(o)
        flags = visit2(r, 0, t0 - (0 if r else 5))
        at(t0 + 20)
        mm([(PS(X1, j, 256, 4), scaled[v], sub(RR, 384 * (j // 2) + 128 * k + 64 * (j % 2), 64)) for j in range(4) for k, v in enumerate((1.0, 0.5, -0.5))]
           + [(PS(X1, j, 256, 4), scaled[-0.5], sub(H, 64 * (j % 2), 64)) for j in range(4)] + [(PS(X1, 0, 256), scaled[-1.0], FLO)])
        ts(AA, PS(X1, 0, 256), -0.25, ALU.add)
        if r == 0:
            at(t0 + 14)
            for k in range(2):
                cp("VA", gb(GNB + 1024 * k), S("AR", 0, 4096), sub(ONB, 64 + 64 * k, 64))
            turn(X1, gb(GNB, 2048), RC, 512, 1024.0)
            mm([it for k in range(2) for it in (back(PS(X1, 128 + 64 * k, 192 + 64 * k), 512, 0, k), (PS(X1, 128 + 64 * k, 192 + 64 * k), LESS, JJ),
                                                 (PS(X1, 128 + 64 * k, 192 + 64 * k), LESS, JJ))])
            for k in range(2):
                ts(sub(DN, 64 * k, 64), PS(X1, 128 + 64 * k, 192 + 64 * k), 1024.0 * k - 7168.0, ALU.min, 8192.0, ALU.add)
        at(t0 + (19 if r else 16))
        if r < 2:
            visit1(r + 1, [(EYE, sub(FLO, j, 64, 4)) for j in range(4)])
        if r == 2:
            mm([(PS(X1, 0, 64), ID, JJ)] + [(PS(X1, 0, 64), scaled[512.0], MISS[k]) for k in range(2)])
            for hf in range(2):
                ts(sub(OGI, 32 * hf, 32), PS(X1, 32 * hf, 32 * hf + 32), -512.0 * hf, ALU.add)
            cp("VA", VP, VN, None, 1.0, 0.0, AF.Relu)
        taps, turns, rear = {}, [], [None] * 4
        for w in (1, 0):
            for hf in range(2):
                win = S(("XF", "XB")[w], 0, 8224) if r == 0 else S(("WF", "WB")[w], 0, 10240)
                off = lambda i: sub(OFT, 256 * w + 64 * i + 32 * hf, 32)
                ub, tb = (U0, U1)[hf], (T0, T1)[hf]
                a0, a2 = [S("WK", 1024 * hf + 512 * j, 1024 * hf + 512 * j + 512) for j in range(2)]
                s_, e_ = a0, S("GAP", 1536 * hf + 1024, 1536 * hf + 1536)
                if r == 0:
                    a0, a2 = [S("INV", 1024 * hf + 512 * j, 1024 * hf + 512 * j + 512) for j in range(2)]
                d1, d2 = S("WK", 2048, 2560), S("WK", 2560, 3072)
                vb = VB if (w, hf) == (0, 1) else ub
                at(t0 + (7 if r else 5) + 5 * (2 * (1 - w) + hf))
                mm(spread(ub, sub(UV, 128 * w + 32 * hf, 32)))
                opened(tb)
                cp("A", a2, win, off(2))
                cp("A", a0, win, off(0))
                taps[w, hf] = [tt(d2, win, a2, ALU.subtract, off(3))]
                if (r, w, hf) in BY_TENSOR:
                    a1, d1 = [S("INV", 2048 + 1024 * j + 512 * hf, 2560 + 1024 * j + 512 * hf) for j in range(2)]
                    cp("A", d1, PS(ub), None, 2.0)
                    cp("A", a1, win, off(1))
                else:
                    taps[w, hf].append(tt(d1, win, a0, ALU.subtract, off(1)))
                if (r, w, hf) == (0, 0, 0):
                    for j in casts:
                        ops[j]["soft"].append(taps[w, hf][0])
                if r == 1 and hf == 1:
                    if w:
                        sg = send([(lo, None, None, "sB"), (hi, None, None, "sL"), (far, None, None, "sC")], 0, taps[1, 0] + taps[1, 1] + flags)
                        free = {t: arrive("s" + t, 1, None, sg) for t in "BLC"}
                    else:
                        free["F"] = send([(helper(1), None, None, "hF"), (helper(2), None, None, "hF")], 0, taps[0, 0] + taps[0, 1])
                front = (taps[w, hf] + [None])[:2] + [tt(PS(tb), PS(ub), d2, ALU.mult)]
                mm([(PS(tb), ID if r else EYE, a2)], False, True)
                if (r, w, hf) in BY_TENSOR:
                    mm([(PS(ub), scaled[0.5], a1), (PS(ub), scaled[-0.5], a0)])
                front.append(tt(PS(ub), PS(ub), d1, ALU.mult))
                turns += [j for pair in zip(front, rear) for j in pair if j is not None]
                rear = [tt(s_, PS(ub), a0, ALU.add)]
                mm(spread(vb, sub(UV, 128 * w + 64 + 32 * hf, 32)))
                rear.append(tt(e_, PS(tb), s_, ALU.subtract))
                zb = S("VAL", 512 * hf, 512 * hf + 512)
                if w:
                    rear.append(tt(PS(ub), PS(ub), e_, ALU.mult))
                    rear.append(tt(zb, PS(ub), s_, ALU.add))
                    continue
                gp = S("GAP", 1536 * hf + 512 * r, 1536 * hf + 512 * r + 512)
                le = gb(LE + 512 * hf, 512)
                opened(tb)
                if hf == 0:
                    rear += [tt(PS(tb), PS(ub), e_, ALU.mult), None]
                    mm([(PS(tb), HALF, s_), (PS(tb), LESS, zb)], False, True)
                    opened(ub)
                    cp("A", gp, PS(tb), None, 2.0, 0.0, AF.Abs)
                    tt(PS(ub), PS(tb), zb, ALU.add)
                    ub, tb = tb, ub
                else:
                    turns[-2:] = turns[:-3:-1]
                    for i, j in zip(turns, turns[1:] + rear[:1]):
                        ops[j]["soft"].append(i)
                    tt(PS(vb), PS(vb), e_, ALU.mult)
                    tt(PS(vb), PS(vb), s_, ALU.add)
                    tt(PS(vb), PS(vb), zb, ALU.subtract)
                    cp("A", gp, PS(vb), None, 1.0, 0.0, AF.Abs)
                    cp("A", PS(tb), PS(vb), None, 0.5)
                    mm([(PS(tb), ID, zb)], False, False)
                at(t0 + (7 if r else 5) + 5 * (2 + hf) + 4)
                ts(le, gp, S("EPS", 0, 1), ALU.is_le)
                won, pen = sub(WON, 32 * hf, 32), sub(PEN, 32 * hf, 32)
                thr = 73.0 if r else 9.0
                mm([(PS(ub, 0, 32), S("BC", 16 - s, 144 - s), sub(le, s, 32, 16)) for s in range(16)]
                   + ([(PS(ub, 0, 32), scaled[64.0], sub(MISS[r - 1], 32 * hf, 32))] if r else []))
                ts(won, PS(ub, 0, 32), thr, ALU.is_ge)
                ts(pen, PS(ub, 0, 32), thr, ALU.is_lt, col(13 if r else 12), ALU.mult)
                mm([(PS(ub, 128 + j, 256, 4), EYE, won) for j in range(4)])
                mm(spread(tb, pen), False, True)
                tt(PS(ub, 128, 256), PS(ub, 128, 256), sub(AA, 128 * hf, 128), ALU.mult)
                tt(sub(MSG, 128 * hf, 128), PS(ub, 128, 256), sub(FLO, 128 * hf, 128), ALU.add)
                flag = MISS[r] if r < 2 else PEN
                if r == 0:
                    cp("VA", sub(flag, 32 * hf, 32), won, None, -1.0, 1.0)
                elif r == 1:
                    tt(sub(flag, 32 * hf, 32), sub(MISS[0], 32 * hf, 32), won, ALU.subtract)
                else:
                    tt(won, won, sub(MISS[1], 32 * hf, 32), ALU.subtract)
                    cp("VA", sub(flag, 32 * hf, 32), won, None, 1.0, 1.0)
                lanes_table(ub, hf, flag)
                vn = sub(VN, 512 * hf, 512)
                if r < 2:
                    cp("VA", le, PS(ub))
                    flip(gb(LTO + 512 * hf, 512), le)
                    src = gb(LTO + 512 * hf, 512)
                    both = [(hi, src, gb(LTB + 512 * hf, 512), "aLb%d%d" % (r, hf)), (lo, src, gb(LTF + 512 * hf, 512), "aLf%d%d" % (r, hf))]
                    s0 = None
                    for items in ([both[:1], both[1:]] if hf and SPLIT else [both]):
                        s = send(items, 128 * len(items), [free["B"], free["L"]] if r else [])
                        ops[s]["soft"] += [s0] if s0 else []
                        s0 = s
                        for it in items:
                            arrive(it[3], half if len(items) == 2 else whole, it[2], s0)
                    at(t0 + 30 + hf)
                    if r:
                        tt(vn, PS(tb), vn, ALU.max)
                    else:
                        cp("VA", vn, PS(tb))
                    c0, up = 512 * hf, S("WK", 1024 * hf + 512, 1024 * hf + 1024)
                    mm([(PS(tb), S("ID", 112, 240), vn)])
                    cp("VA", up, PS(tb))
                    s1 = send([(hi, vn, S("WB", c0, c0 + 512), "aVb%d%d" % (r, hf)), (far, up, S("WB", 5120 + c0, 5632 + c0), "aVn%d%d" % (r, hf))],
                              512, [free["B"], free["C"]] if r else [])
                    for j in ([first, s1] if hf else []):
                        ops[j]["soft"].append(s0)
                    first = s1
                    arrive("aVb%d%d" % (r, hf), half, S("WB", c0, c0 + 512), s1)
                    arrive("aVn%d%d" % (r, hf), half, S("WB", 5120 + c0, 5632 + c0), s1)
                else:
                    c0 = 512 * hf
                    y = sub(VP, c0, 512)
                    tt(y, PS(tb), y, ALU.max)
                    dma("S", [(lambda c0=c0: T.y[:, c0:c0 + 512], lambda y=y: ap(y))], 256, [y], [])
                    cp("A", s_, S("GAP", 1536 * hf, 1536 * hf + 1536), sub(OGI, 32 * hf, 32), -1.0, 100.0, AF.Relu)
                    ops[cp("A", s_, s_, None, 1.0, -100.0, AF.Exp)]["dur"]["A"] += 0.0 if hf else 1.3
                    dma("S", [(lambda c0=c0: T.ye[:, c0:c0 + 512], lambda s_=s_: ap(s_))], 256, [s_], [])
                    flip(a2, PS(ub))
                    rows = [((lambda k=k, c0=c0: T.yf[8 * k:8 * k + 8, c0:c0 + 512]), (lambda row=row, a2=a2: T.WK[row:128:16, a2[1]:a2[2]]))
                            for k, row in enumerate((12, 13, 14, 15, 0))]
                    dma("S", rows[:3], 48, [a2], [])
                    dma("A", rows[3:], 32, [a2], [])
        if r < 2:
            cp("A", VP, VN, None, 1.0, 0.0, AF.Abs)
            s2 = send([(helper(0), VP, S("vp", 0, 1024, 1, 144 * r, 144 * r + 128), "hv%d" % r)], 512)
            ops[s2]["soft"] += [s1] + ([free["F"]] if r else [])
            arrive("aVf%d" % r, half, S("WF", 0, 1024), s2, 8.0)
            arrive("aVp%d" % r, half, S("WF", 5120, 6144), s2, 8.0)
    return ops, q


ORDER = []


def schedule(ops):
    if ORDER:
        return ORDER[0]
    n = len(ops)
    link = lambda i, j: (0 if ops[i]["kind"] != "a" and ops[j]["kind"] != "a" and i not in ops[j]["deps"] else
                         1 if ops[i]["kind"] == ops[j]["kind"] == "c" and not (ops[j]["deps"].get(i) or ops[i]["deps"].get(j)) else 2)
    fwd, bwd = [[] for _ in range(n)], [[] for _ in range(n)]
    for j in range(n):
        for i in sorted(set(ops[j]["deps"]) | set(ops[j]["soft"])):
            fwd[i].append((j, link(i, j)))
            bwd[j].append((i, link(i, j)))
    fwd, bwd = fwd + [[len(x) for x in bwd]], bwd + [[len(x) for x in fwd]]
    flex = [len(o["dur"]) > 1 for o in ops]
    seed = [SEED]

    def rnd():
        seed[0] = (seed[0] * 1103515245 + 12345) % 2147483648
        return seed[0] / 2147483648.0

    def worth(got):
        return max(got[2]) + 0.02 * sum(got[2]) / n

    def again(got, slack):
        rev = one_pass(ops, bwd, got[2], 0.25, got[3])
        return one_pass(ops, fwd, rev[2], slack, got[3])

    def chain(got):
        i, out = max(range(n), key=lambda i: got[2][i]), []
        while i is not None:
            out.append(i)
            i = got[4][i]
        return out

    best = None
    for it in range(ROUNDS):
        eng = [o["eng"] if len(o["dur"]) == 1 else o["eng"][0 if it and rnd() < (0.1, 0.2, 0.3)[it % 3] else 1] for o in ops]
        got = one_pass(ops, fwd, [-o["when"] for o in ops], (0.3, 0.6, 1.0, 1.5)[it % 4], eng)
        for k in range(3):
            if best is None or worth(got) < worth(best):
                best = got
            got = again(got, (0.25, 0.6, 1.0)[k % 3])
    now, path = best, chain(best)
    for it in range(TRIES):
        prio = [-t for t in now[1]]
        eng = list(now[3])
        for k in range(1 + (it % 4 == 3)):
            at = int(rnd() * (len(path) - 1))
            i, j = path[at], path[at + 1]
            if flex[i] and rnd() < 0.6:
                eng[i] = "A" if eng[i] == "V" else "V"
            elif eng[i] == eng[j] and j not in ops[i]["deps"]:
                if rnd() < 0.5:
                    prio[i] = prio[j] + 0.01 + 2.0 * rnd() ** 2
                else:
                    prio[j] = prio[i] - 0.01 - 6.0 * rnd() ** 2
            else:
                for x in range(n):
                    if abs(now[1][x] - now[1][i]) < 3.0 and rnd() < 0.1:
                        prio[x] += (2.0 * rnd() - 1.0) * 3.0
                        if flex[x] and rnd() < 0.3:
                            eng[x] = "A" if eng[x] == "V" else "V"
        got = one_pass(ops, fwd, prio, (0.3, 1.0, 2.0)[it % 3], eng)
        if it % 8 == 0:
            more = again(got, 0.5)
            got = more if worth(more) < worth(got) else got
        if worth(got) <= worth(now) + HEAT * (1.0 - it / TRIES) * rnd():
            now, path = got, chain(got)
            if worth(now) < worth(best):
                best = now
    ORDER.append(best)
    return best


ROUNDS, TRIES, HEAT, SEED = 12, 12000, 0.12, 1


def one_pass(ops, succ, prio, slack, eng):
    n = len(ops)
    left = list(succ[n])
    free = {None: 0.0, "P": 0.0, "V": 0.0, "A": 0.0, "S": 0.0, "G": 0.0}
    done, start, can, why = [0.0] * n, [0.0] * n, [0.0] * n, [None] * n
    ready, soon, last = {e: [] for e in free}, {}, {}
    moved, mover = 0.0, None
    for i in range(n):
        if left[i] == 0:
            ready[eng[i]].append(i)
            soon[eng[i]] = 0.0
    order = []
    for _ in range(n):
        first = 1e9
        for x, t in soon.items():
            if free[x] > t:
                t = free[x]
            if t < first:
                first, e = t, x
        lst = ready[e]
        if len(lst) == 1:
            i = lst.pop()
            del soon[e]
        else:
            top, bar, low, next_ = -1e18, first + slack, 1e9, 1e9
            for x in lst:
                t = can[x]
                if t <= bar and prio[x] > top:
                    i, top = x, prio[x]
                if t < next_:
                    low, next_ = (t, low) if t < low else (low, t)
            lst.remove(i)
            soon[e] = next_ if can[i] == low else low
        o = ops[i]
        est = can[i]
        if free[e] > est:
            est, why[i] = free[e], last[e]
        start[i] = est
        end = est + o["dur"][e]
        hold = o["hold"]
        if hold is not None:
            t = moved + o["dur"][e] - 1.8 - (hold if e == "G" else 0.0)
            if t > end:
                end, why[i] = t, mover
            moved, mover = end, i
            free[e], last[e] = est + hold, i
        elif e:
            free[e], last[e] = end, i
        done[i] = end
        order.append(i)
        for j, how in succ[i]:
            x = eng[j]
            t = end + WAKE if how == 2 else est if how == 0 else end if x == e else end + WAKE
            if t > can[j]:
                can[j], why[j] = t, i
            left[j] -= 1
            if not left[j]:
                ready[x].append(j)
                if can[j] < soon.get(x, 1e9):
                    soon[x] = can[j]
    return order, start, done, eng, why


def rank_program(g, core, T, topo):
    rank = T.rank_of(core)
    if rank is None:
        for r in range(len(T.cores)):
            if helper_of(T, topo, r) == core:
                helper_program(g, core, T, topo, r)
        return
    ops, q = build(g, core, T, topo, rank)
    order, _, _, eng, _ = schedule(ops)
    count = {}
    mark = {}
    for i in order:
        o = ops[i]
        if o["kind"] == "c":
            count[eng[i]] = count.get(eng[i], 0) + 1
            mark[i] = ("c" + eng[i], count[eng[i]])
        else:
            mark[i] = (o["sem"], o["cnt"])
    seen = {}
    for i in order:
        o = ops[i]
        if o["kind"] == "a":
            continue
        want = {}
        for j, raw in o["deps"].items():
            if ops[j]["kind"] == "c" and o["kind"] == "c" and eng[j] == eng[i] and not raw:
                continue
            sem, v = mark[j]
            want[sem] = max(want.get(sem, 0), v)
        for sem, v in sorted(want.items()):
            if seen.get((eng[i], sem), 0) < v:
                q[eng[i]].wait_ge(T.sem[sem], v)
                seen[(eng[i], sem)] = v
        r = o["emit"](eng[i])
        if o["kind"] == "c":
            r.then_inc(T.sem["c" + eng[i]], 1)
    total = {}
    for sem, v in mark.values():
        total[sem] = max(total.get(sem, 0), v)
    for sem, v in sorted(total.items()):
        if seen.get(("G", sem), 0) < v:
            g.wait_ge(T.sem[sem], v)
